import numpy as np, ml_dtypes
CORES = [2,3,42,43,82,83,122,123]
N = 8
BF = ml_dtypes.bfloat16
W, NS, TS = 4096, 128, 6
B = W // NS
def parts(rng):
    size = rng.choice(np.array([256, 256, 256, 64, 16]), (N, 8, 1, W))
    x = (rng.random((N, 8, 16, W)) * size).astype(np.int64)
    v = rng.integers(0, W, (N, 8, 16, W)); s = rng.integers(0, W, (N, 8, 16, NS)); z = rng.integers(0, 256, (N, 8, 16, NS)); w = rng.integers(0, 256, (N, 8, 16))
    h = np.where(rng.random((N, 8, 16)) < 0.75, rng.integers(0, 600, (N, 8, 16)), rng.integers(600, 1600, (N, 8, 16)))
    return x, v, s, z, w, h, rng.integers(0, 2, (N, 8, NS))
def pack(x, v, s, z, w, h, a):
    return {"reg": np.ascontiguousarray(x.reshape(N, 128, W)).astype(np.float32).astype(BF), "vw": np.ascontiguousarray((v[..., :W // 2] + W * v[..., W // 2:]).reshape(N, 128, W // 2)).astype(np.int32),
            "scan": np.ascontiguousarray(s.reshape(N, 128, NS)).astype(np.int32), "z0": np.ascontiguousarray(z.reshape(N, 128, NS)).astype(np.float32).astype(BF),
            "wt": np.ascontiguousarray(w.reshape(N, 128, 1)).astype(np.int32), "th": np.ascontiguousarray(h.reshape(N, 128, 1)).astype(np.int32), "warm": np.ascontiguousarray(a).astype(np.int32)}
def setup_inputs(rng):
    return pack(*parts(rng))
def setup_inputs_corners(rng):
    x, v, s, z, w, h, a = parts(rng); i = np.arange(NS)[None, :]; k = np.arange(16)[:, None]; d = np.arange(W)[None, :]
    for q in range(N):
        for g in range(8):
            c = (g + 3 * q) % 8
            x[q, g][:, ::7] = 0; x[q, g][:, 3::7] = 255; x[q, g][:, W - 1] = 255
            if (q + g) % 3 == 0: a[q, g] = 0
            if (q + g) % 3 == 1: a[q, g] = 1
            if c == 0: s[q, g] = 0; w[q, g] = 255
            if c == 1: s[q, g] = W - 1; h[q, g] = 4079
            if c == 2: s[q, g] = B * i + k % B; h[q, g] = 0
            if c == 3: s[q, g] = B * rng.integers(0, NS, (16, NS)); w[q, g] = 0; h[q, g] = 0; a[q, g] = rng.integers(0, 2, NS)
            if c == 4: s[q, g] = (16 * i + k + 1) % W; v[q, g] = np.where(k >= 0, (d + 1) % W, 0)
            if c == 5: v[q, g] = np.where(k >= 0, d, 0); w[q, g] = 255 * rng.integers(0, 2, 16)
            if c == 6: v[q, g] = (W - 1) * rng.integers(0, 2, (1, W)); h[q, g] = 4079 * rng.integers(0, 2, 16)
            if c == 7: s[q, g] = B * rng.integers(0, NS, (16, NS)) + B - 1; a[q, g] = rng.integers(0, 2, NS); h[q, g] = 0
            if c % 3 == 0: z[q, g] = 0
            if c % 3 == 1: z[q, g] = 255
    return pack(x, v, s, z, w, h, a)
def setup_inputs_crowd(rng):
    x, v, s, z, w, h, a = parts(rng); h = rng.integers(0, 1000, (N, 8, 16))
    for q in range(N):
        for g in range(8):
            pl = rng.permutation(W)[:4]; x[q, g][:, pl[:3]] = rng.integers(200, 256, (16, 3)); x[q, g][:, pl[3]] = 0
            s[q, g] = rng.choice(pl[:1 + 2 * (g % 2)], (16, NS)); a[q, g] = 1
            if g % 4 == 1: w[q, g] = 0
            if g % 4 == 2: w[q, g] = 255
            o = int(rng.integers(0, NS)) if g < 7 else NS - 1
            if q % 4 == 3:
                a[q, g] = 0
                if g == 7: a[q, g, o] = 1
            elif (q % 4 == 1 and g == 7) or (q % 4 == 2 and g % 2 == 1):
                way = (g // 2 + q) % 3
                if way == 0: a[q, g, o] = 0
                else: s[q, g, :, o] = pl[3]
                if way == 2: s[q, g, int(rng.integers(0, 16)), o] = pl[0]
    return pack(x, v, s, z, w, h, a)
def setup_inputs_ends(rng):
    x = np.where(rng.random((N, 8, 1, W)) < 0.5, 255 * rng.integers(0, 2, (N, 8, 1, W)), 255 * rng.integers(0, 2, (N, 8, 16, W)))
    x[..., 0] = 0; x[..., W - 1] = 255; x[:, 1, :, 0] = 255; x[:, 1, :, W - 1] = 0
    e = (W - 1) * rng.integers(0, 2, (N, 8, 16, W // 2)); c = rng.random(e.shape) < 0.7
    v = np.concatenate([np.where(c, e, rng.integers(0, W, e.shape)), np.where(c, e, rng.integers(0, W, e.shape))], axis=3)
    s = np.where(rng.random((N, 8, 16, NS)) < 0.72, (W - 1) * rng.integers(0, 2, (N, 8, 16, NS)), rng.integers(0, W, (N, 8, 16, NS)))
    z = np.where(rng.random((N, 8, 1, NS)) < 0.5, 255 * rng.integers(0, 2, (N, 8, 1, NS)), 255 * rng.integers(0, 2, (N, 8, 16, NS)))
    w = 255 * rng.integers(0, 2, (N, 8, 16)); w[:, 2] = 255; w[:, 6] = 255
    w[:, 3] = 0; w[:, 3, 15] = 255; w[:, 3, 0] = 2; w[:, 7] = w[:, 3]; w[0, 7] = 255
    h = 4079 * rng.integers(0, 2, (N, 8, 16)); h[..., 0] = 4079; h[..., 8] = 0; h[..., 15] = 0
    a = (rng.random((N, 8, NS)) < 0.6).astype(np.int64); i = np.arange(NS); last = i[i % 8 == 7]; one = i[i % 8 == 6]; two = i[i % 8 == 1]; three = i[i % 8 == 5]; late = 5 * B - 1
    for q in range(N):
        b = (N - 1 - q) % 2 == 0
        v[q, :, :, W - 1] = W - 1 if b else 0; v[q, :, :, W // 2 - 1] = W - 1 if b else 0
        s[q][:, :, last] = W - 1; z[q][:, :, last] = 0 if b else 255; a[q][:, last] = 1
        if b:
            both = np.concatenate([one, two]); s[q][:, :, both] = 0; z[q][:, :, both] = 255; a[q][:, both] = 1
            s[q][:, 15, one] = W - 1; s[q][:, 8, two] = W - 1
            for g in (3, 7):
                x[q, g][:, late] = 0; s[q, g][:, 4] = W - 1; z[q, g][:, 4] = 0; a[q, g, 4] = 1
                s[q, g][:, three] = 0; s[q, g][15, three] = W - 1; s[q, g][8, three] = late; z[q, g][:, three] = 0; a[q, g, three] = 1
    s[0, :, 3] = W - 1; s[0, :, 15] = W - 1; s[0, 1, 3] = 0; s[0, 1, 15] = 0; a[0] = 1; a[0, 0, 0] = 0
    return pack(x, v, s, z, w, h, a)
def setup_inputs_spread(rng):
    x, v, s, z, w, h, a = parts(rng)
    x = (np.exp2(8 * rng.random((N, 8, 1, W))) * rng.random((N, 8, 16, W))).astype(np.int64)
    z = (np.exp2(8 * rng.random((N, 8, 1, NS))) * rng.random((N, 8, 16, NS))).astype(np.int64)
    w = np.minimum(np.exp2(8 * rng.random((N, 8, 16))).astype(np.int64), 255); h = np.minimum(np.exp2(12 * rng.random((N, 8, 16))).astype(np.int64) - 1, 4079)
    p = rng.choice(np.array([0.5, 1.0, 2.0, 3.0]), (N, 8, 1, 1))
    s = np.minimum((W * rng.random((N, 8, 16, NS)) ** p).astype(np.int64), W - 1); v = np.minimum((W * rng.random((N, 8, 16, W)) ** p).astype(np.int64), W - 1)
    a = (rng.random((N, 8, NS)) < rng.choice(np.array([0.1, 0.5, 0.9]), (N, 8, 1))).astype(np.int64)
    return pack(x, v, s, z, w, h, a)
def setup_inputs_ties(rng):
    x, v, s, z, w, h, a = parts(rng); lane = np.arange(16)[:, None]
    for q in range(N):
        for g in range(8):
            if g % 2 == 0:
                c = (0, 16, 1000, 4079)[(g // 2 + q) % 4]
                m = np.minimum(np.maximum(c + rng.integers(-1, 2, W), 0), 4080)
                x[q, g] = m // 16 + ((lane + rng.integers(0, 16, W)) % 16 < m % 16); h[q, g] = c
                z[q, g] = z[q, g] * rng.integers(0, 2, (1, NS)); a[q, g] = rng.random(NS) < 0.8
            else:
                x[q, g] = rng.integers(0, 16, (16, W)); x[q, g][:, W // 2:] = x[q, g][:, :W // 2]
                s[q, g, 1::2] = (s[q, g, 0::2] + W // 2) % W; h[q, g] = rng.integers(10, 70, 16); z[q, g] = rng.integers(0, 16, (16, NS))
                x[q, g][:, 5] = 255; x[q, g, (g + q) % 16, 5] = 254; x[q, g][:, W - 1] = 255
                s[q, g][:, NS - 2:] = 5; s[q, g, 15, NS - 2:] = W - 1; z[q, g][:, NS - 2:] = 0; a[q, g, NS - 2:] = 1
                if g % 4 == 3:
                    x[q, g][:, W - 3] = 0; x[q, g][:, W // 2 - 3] = 0; w[q, g, 0] = 1; w[q, g, 1] = 16
                    s[q, g][:, 4:6] = W - 3; z[q, g][:, 4:6] = 0; z[q, g, 0, 4:6] = 11; z[q, g, 1, 4:6] = W // 16 - 2; a[q, g, 4:6] = 1
    return pack(x, v, s, z, w, h, a)
def check_inputs(d):
    bad = []
    for k, lo, hi in (("reg", 0, 255), ("vw", 0, W * W - 1), ("scan", 0, W - 1), ("z0", 0, 255), ("wt", 0, 255), ("th", 0, 4079), ("warm", 0, 1)):
        a = np.asarray(d[k]).astype(np.float64)
        if not (np.min(a) >= lo and np.max(a) <= hi): bad.append("range of " + k)
        elif np.any(a != np.floor(a)): bad.append("whole numbers in " + k)
    return bad
def pick(x, ix):
    return np.take_along_axis(x, ix.reshape(N, 8, 1, 16 * NS), 3).reshape(N, 8, 16, 16, NS)
def reference(reg, vw, scan, z0, wt, th, warm):
    X = reg.astype(np.float32).astype(np.int32).reshape(N, 8, 16, W); pk = vw.astype(np.int64).reshape(N, 8, 16, W // 2)
    V = np.concatenate([pk % W, pk // W], axis=3)
    S = scan.astype(np.int64).reshape(N, 8, 16, NS); z = z0.astype(np.float32).astype(np.int32).reshape(N, 8, 16, NS)
    wl = wt.astype(np.int64).reshape(N, 8, 16, 1); theta = th.astype(np.int64).reshape(N, 8, 16, 1); new = warm == 0
    last = np.zeros((N, 8, 16, 16, NS), np.int32); m = np.zeros((N, 8, 16, NS), np.int64); A = np.zeros((N, 1, 1, 1), np.int64)
    row37 = 37 * np.arange(16).reshape(1, 1, 16, 1); sc = np.arange(NS)
    for t in range(TS):
        C = pick(X, S)
        moved = (np.add.reduce(np.abs(C - last), axis=2) > theta + A % 32) & ~new[:, :, None, :]
        m = m + moved; some = np.any(moved, axis=2)
        clean = ~new & ~some; borrow = some & (np.add.reduce(m, axis=2) >= 2); has = clean | borrow
        key = 4096 * m + np.add.reduce(np.abs(C - z[:, :, :, None, :]), axis=2)
        donor = np.argmax(key, axis=2)
        dr = np.take_along_axis(S, donor[:, :, None, :], 2)
        F = np.where(borrow[:, :, None, :], np.take_along_axis(V, dr, 3), S)
        D = pick(X, F); y = (np.max(D, axis=3) + np.min(D, axis=3)) >> 1
        z = np.where(has[:, :, None, :], np.abs(y - z), z)
        u = np.add.reduce(wl * z, axis=2, keepdims=True) % W
        place = B * sc + u[:, :, 0, :] % B
        X = X.copy(); V = V.copy()
        for r in range(N):
            for odd in range(2):
                q = (r + odd * (1 + t % 3)) % N
                gi, si = np.nonzero(has[r] & (sc % 2 == odd)); pl = place[r][gi, si]
                X[q][gi, :, pl] = y[r][gi, :, si]
                if t < TS - 1: V[q][gi, :, pl] = F[r][gi, :, si]
        S = np.where(has[:, :, None, :], (((F * u) >> 5) + F + row37 + A) % W, S)
        m = np.where(has[:, :, None, :], 0, m); new = has; last = C
        A = np.add.reduce(borrow.astype(np.int64).reshape(N, 8 * NS), axis=1).reshape(N, 1, 1, 1)
    return {"yx": X.reshape(N, 128, W).astype(np.float32).astype(BF), "ys": S.reshape(N, 128, NS).astype(np.float32), "yz": z.reshape(N, 128, NS).astype(np.float32).astype(BF)}

@@ -1,0 +1,599 @@
+from concourse.mybir import AluOpType as A, ActivationFunctionType as AF, AxisListType as AX
+
+BF, F32, I32, U16 = "bfloat16", "float32", "int32", "uint16"
+NSTEP = 6
+ZC = 4096
+SB = 4104
+VW = 4232
+TR = 8192
+WIN = 12288
+SC = 2.0 ** -17
+CY = 0.83e-3 * 1.25
+WAKE = 0.1
+ENG = 8
+
+SCRATCH = {
+    "X": ("sbuf", [128, WIN], BF), "Q": ("sbuf", [128, WIN], BF), "V": ("sbuf", [128, WIN], I32),
+    "vwb": ("sbuf", [128, 2048], I32), "zx": ("sbuf", [128, 2048], BF), "cols": ("sbuf", [128, 32], F32), "GI": ("sbuf", [128, 128], BF), "wmf": ("sbuf", [128, 128], BF),
+    "msg": ("sbuf", [128, NSTEP * 72], BF), "rxy": ("sbuf", [128, NSTEP * 72], BF), "rxf": ("sbuf", [128, NSTEP * 64], U16),
+    "fs": ("sbuf", [128, 48], F32), "fi": ("sbuf", [128, 16], I32), "Te": ("sbuf", [128, 160], F32), "To": ("sbuf", [128, 160], F32),
+}
+for _w, _d, _names in (
+        (1, I32, "wb thb"), (8, I32, "J8 JJ"), (8, F32, "BASE JS JN JZ TB XS HAS HX"), (8, BF, "BO"), (8, U16, "ov oz L0 L1"),
+        (64, I32, "KC1"), (64, F32, "THB THC"), (64, BF, "yE0 yE1"),
+        (128, I32, "scb wmb si sj Ri vi ym yi"), (128, BF, "dz zb Z0 Z1 WB ONE WpR WpH WpY WpM WpX qm qx Qn QR zo"), (128, U16, "zl S16 F0 F1 F2 F3 F4 F5"),
+        (128, F32, "ky dd GG DR um us OF blk ID UP DN E0 E1 Sa Sb MQ Kc RS1 MV NS WX so"), (144, I32, "PI NI N15 PQ PG NQ NG ti tj"), (144, F32, "tf tg Sf0 Sf1"),
+        (144, BF, "W1 WT2 WTm WQ WQ0"), (1024, BF, "T0 T1 C0 C1 D0 D1 mx mn RSM RSN")):
+    for _n in _names.split():
+        SCRATCH[_n] = ("sbuf", [128, _w], _d)
+PSUM = ("Ro", "Re", "Sx", "Uo", "Ue", "PQs", "P7", "VB")
+for _n in PSUM:
+    SCRATCH[_n] = ("psum", [128, 512], F32)
+LOADS = ["scb", "zb", "wb", "thb", "wmb", "vwb", "X0", "X1", "X2", "X3"]
+SEMAPHORES = ["sv", "ss", "sp", "sg", "ls", "dyx", "dys", "dyz"] + ["d" + n for n in LOADS] + ["ry%d" % t for t in range(NSTEP)] + ["rf%d" % t for t in range(NSTEP - 1)]
+
+
+def rank_program(g, core, T, topo):
+    rank = T.rank_of(core)
+    if rank is None:
+        return
+    queues = {"v": g.vector, "s": g.scalar, "p": g.tensor, "g": g, "y": g.sync}
+    own = {"v": "sv", "s": "ss", "p": "sp", "g": "sg"}
+    total = {}
+    know = {q: {} for q in queues}
+    ops = []
+    hist = {}
+
+    def h(name, lo=0, hi=None, step=1, rows=None):
+        return (name, lo, T[name].shape[1] if hi is None else hi, step, rows)
+
+    def ind(win, off):
+        return ("ind", win, off)
+
+    def ap(x):
+        if x[0] == "ind":
+            return ap(x[1]).indirect(ap(x[2]))
+        t = T[x[0]]
+        if x[4]:
+            return t[0:x[4], x[1]:x[2]]
+        return t[:, x[1]:x[2]] if x[3] == 1 else t[:, x[1]:x[2]:x[3]]
+
+    def regions(x):
+        return [x[1], x[2]] if x[0] == "ind" else [x]
+
+    def wait(q, tok, clock):
+        if know[q].get(tok[0], 0) >= tok[1]:
+            return
+        queues[q].wait_ge(T.sem[tok[0]], tok[1])
+        for s, v in clock.items():
+            if know[q].get(s, 0) < v:
+                know[q][s] = v
+
+    def need(q, reads, writes):
+        todo = []
+        for wr, group in ((False, reads), (True, writes)):
+            for x in group:
+                for e in hist.get(x[0], []):
+                    if e[3] == q and q == "p":
+                        continue
+                    ps = x[0] in PSUM and e[3] != q
+                    if not ps and (e[0] >= x[2] or e[1] <= x[1]):
+                        continue
+                    if (e[2] or wr or ps) and (e[4], e[5]) not in todo:
+                        todo.append((e[4], e[5]))
+        todo.sort(key=lambda c: -len(c[1]))
+        for tok, clock in todo:
+            wait(q, tok, clock)
+
+    def note(q, tok, reads, writes, tag=None):
+        clock = dict(know[q])
+        clock[tok[0]] = tok[1]
+        tag = tag or q
+        for wr, group in ((True, writes), (False, reads)):
+            for x in group:
+                lo, hi = x[1], x[2]
+                lst = hist.setdefault(x[0], [])
+                if wr:
+                    lst[:] = [e for e in lst if not (e[0] >= lo and e[1] <= hi)]
+                else:
+                    lst[:] = [e for e in lst if not (not e[2] and e[3] == tag and e[0] >= lo and e[1] <= hi and tag in own)]
+                lst.append((lo, hi, wr, tag, tok, clock))
+
+    def bump(sem, n):
+        total[sem] = total.get(sem, 0) + n
+        return (sem, total[sem])
+
+    def schedule():
+        n = len(ops)
+        pred, seen = [[] for _ in ops], {}
+        for i, (q, _e, reads, writes, us, lat, tag) in enumerate(ops):
+            for wr, group in ((False, reads), (True, writes)):
+                for x in group:
+                    for e in seen.get(x[0], []):
+                        ps = x[0] in PSUM and e[3] != tag
+                        if not ps and (e[0] >= x[2] or e[1] <= x[1]):
+                            continue
+                        if e[2] or wr or ps:
+                            pred[i].append(e[4])
+            for wr, group in ((True, writes), (False, reads)):
+                for x in group:
+                    lst = seen.setdefault(x[0], [])
+                    if wr:
+                        lst[:] = [e for e in lst if not (e[0] >= x[1] and e[1] <= x[2])]
+                    lst.append((x[1], x[2], wr, tag, i))
+        succ, left = [[] for _ in ops], [0] * n
+        for i in range(n):
+            pred[i] = sorted(set(pred[i]))
+            left[i] = len(pred[i])
+            for j in pred[i]:
+                succ[j].append(i)
+        rest = [0.0] * n
+        for i in range(n - 1, -1, -1):
+            rest[i] = ops[i][4] + ops[i][5] + max([rest[j] + WAKE for j in succ[i]] + [0.0])
+        ready, free = [0.0] * n, {}
+        cand = [i for i in range(n) if not left[i]]
+        while cand:
+            st, _r, i = min([(max(ready[i], free.get(ops[i][0], 0.0)), -rest[i], i) for i in cand])
+            cand.remove(i)
+            free[ops[i][0]] = st + ops[i][4]
+            for j in succ[i]:
+                w = 0.0 if ops[i][0] == ops[j][0] == "p" else WAKE
+                ready[j] = max(ready[j], st + ops[i][4] + ops[i][5] + w)
+                left[j] -= 1
+                if not left[j]:
+                    cand.append(j)
+            ops[i][1]()
+
+    def elems(x):
+        return 16 * (x[2][2] - x[2][1]) if x[0] == "ind" else -(-(x[2] - x[1]) // x[3])
+
+    def vtime(o, ins, cyc):
+        n = elems(o)
+        if o[0] == "ind":
+            return 0.05 + 3.8 * n * CY
+        if [x for x in ins if x[0] == "ind"]:
+            return 0.05 + 1.56 * n * CY
+        return max(64.0, cyc * n) * CY
+
+    def rate(*xs):
+        return 1.0 if [x for x in xs if SCRATCH[x[1][0] if x[0] == "ind" else x[0]][2] in (F32, I32)] else 0.5
+
+    def run(q, call, out, ins, us):
+        reads = [r for x in ins for r in regions(x)] + regions(out)[1:]
+        writes = regions(out)[:1]
+
+        def emit():
+            need(q, reads, writes)
+            call().then_inc(T.sem[own[q]], 1)
+            note(q, bump(own[q], 1), reads, writes)
+        ops.append((q, emit, reads, writes, us, 0.0, q))
+
+    V, S = g.vector, g.scalar
+
+    def tt(o, x, y, op):
+        run("v", lambda: V.tensor_tensor(ap(o), ap(x), ap(y), op), o, [x, y], vtime(o, [x, y], 1.0 if x[0] in PSUM or y[0] in PSUM else 2.0))
+
+    def ts(o, x, s1, op0, s2=None, op1=None):
+        ins = [x] + [s for s in (s1, s2) if isinstance(s, tuple)]
+        c1 = ap(s1) if isinstance(s1, tuple) else s1
+        if op1 is None:
+            run("v", lambda: V.tensor_scalar(ap(o), ap(x), c1, None, op0), o, ins, vtime(o, [x], rate(o, x)))
+        else:
+            run("v", lambda: V.tensor_scalar(ap(o), ap(x), c1, s2, op0, op1), o, ins, vtime(o, [x], rate(o, x)))
+
+    def cp(o, x):
+        run("v", lambda: V.tensor_copy(ap(o), ap(x)), o, [x], vtime(o, [x], rate(o, x)))
+
+    def fill(o, c):
+        run("v", lambda: V.memset(ap(o), c), o, [], vtime(o, [], 1.0))
+
+    def scan(o, d0, d1, init, op0, op1):
+        run("v", lambda: V.tensor_tensor_scan(ap(o), ap(d0), ap(d1), init, op0, op1), o, [d0, d1], vtime(o, [], rate(o, d0, d1)))
+
+    def turn(o, x):
+        run("v", lambda: V.transpose(ap(o), ap(x)), o, [x], vtime(o, [], 1.0))
+
+    def act(o, x, f, bias=0.0):
+        us = 0.065 + 1.56 * elems(o) * CY if x[0] == "ind" else max(64, elems(o)) * CY
+        if f == AF.Copy:
+            run("s", lambda: S.activation(ap(o), ap(x), f), o, [x], us)
+        else:
+            run("s", lambda: S.activation(ap(o), ap(x), f, bias=bias), o, [x], us)
+
+    def times(o, x, s):
+        c = ap(s) if isinstance(s, tuple) else s
+        run("s", lambda: S.activation(ap(o), ap(x), AF.Identity, scale=c), o, [x] + ([s] if isinstance(s, tuple) else []), max(64, elems(o)) * CY)
+
+    def iota(o, pattern, base, cm, small=False):
+        run("g", lambda: g.iota(ap(o), pattern, base, cm, allow_small_or_imprecise_dtypes=small), o, [], 0.13 + 2 * elems(o) * CY)
+
+    def diag(o, base):
+        run("g", lambda: g.affine_select(ap(o), ap(h("OF")), [[1, 128]], A.is_equal, 0.0, base, -1), o, [h("OF")], 0.17 + 2 * elems(o) * CY)
+
+    def mms(out, pairs, start=True, stop=True):
+        reads = [x for p in pairs for x in p]
+        us = len(pairs) * max(64, elems(out)) * CY * (4 if SCRATCH[pairs[0][0][0]][2] == F32 else 1)
+
+        def emit():
+            need("p", reads, [out])
+            for n, (l, r) in enumerate(pairs):
+                i = g.tensor.matmul(ap(out), ap(l), ap(r), start and n == 0, stop and n == len(pairs) - 1)
+            i.then_inc(T.sem["sp"], 1)
+            note("p", bump("sp", 1), reads, [out])
+        ops.append(("p", emit, reads, [out], us, 0.0, "p"))
+
+    def dma(q, sem, out, in_, ohandle=None, ihandle=None):
+        reads, writes = ([ihandle] if ihandle else []), ([ohandle] if ohandle else [])
+
+        def emit():
+            need(q, reads, writes)
+            queues[q].dma_start(out, in_).then_inc(T.sem[sem], 16)
+            note(q, bump(sem, 16), reads, writes, q + "dma")
+        ops.append((q, emit, reads, writes, 0.06, 3.0, q + "dma"))
+
+    def send(out, in_, remote, dst):
+        rid, pid, _se = topo.addr(dst)
+        eng = topo.engines(core, dst)[:ENG]
+        m = 0
+        for e in eng:
+            m |= 1 << e
+
+        def emit():
+            need("g", [in_], [])
+            g.remote_dma(ap(out), ap(in_), T.sem[remote], T.sem["ls"], pid, rid, m)
+            bump("ls", len(eng))
+        ops.append(("g", emit, [in_], [("@" + remote, 0, 1, 1)], 0.8, 0.0, "g"))
+
+    def recv(out, sem, n):
+        def emit():
+            hist.setdefault(out[0], []).append((out[1], out[2], True, "remote", bump(sem, n), {sem: n}))
+        ops.append(("remote" + sem, emit, [("@" + sem, 0, 1, 1)], [out], 2.5, 0.0, "remote"))
+
+    for b, t in (("scb", T.scan), ("zb", T.z0), ("thb", T.th), ("wb", T.wt)):
+        dma("y", "d" + b, ap(h(b)), t[:, :], h(b))
+    for n in range(4):
+        dma("s", "dX%d" % n, ap(h("X", 1024 * n, 1024 * n + 1024)), T.reg[:, 1024 * n:1024 * n + 1024], h("X", 1024 * n, 1024 * n + 1024))
+    dma("y", "dwmb", T["wmb"][0:8, :], T.warm[:, :], h("wmb"))
+    dma("y", "dvwb", ap(h("vwb")), T.vw[:, :], h("vwb"))
+
+    m128 = lambda b: h(b, 0, 128)
+    col = lambda c: h("cols", c, c + 1)
+    QC, H0, H1, LQ, L0C, K37, AK0, AK1, CA, WC, THN, C64, A1, G0, G1, LQ1 = range(16)
+    half = lambda hh: (64 * hh, 64 * hh + 64)
+    four = lambda hh: (4 * hh, 4 * hh + 4)
+    fill(h("OF"), 1.0)
+    iota(h("PI"), [[0, 144]], 0, 1)
+    iota(h("NI"), [[1, 144]], 0, 0)
+    diag(h("ID"), 0)
+    diag(h("UP"), -16)
+    diag(h("DN"), 16)
+    iota(h("N15"), [[1, 144]], -15, 0)
+    iota(h("KC1"), [[16384, 4], [0, 16]], 0, 0)
+    iota(h("J8"), [[32, 2], [1024, 4]], 0, 0)
+    iota(h("JJ"), [[16, 8]], 0, 0)
+    iota(h("RSM"), [[0, 64], [256, 16]], 0, 0, True)
+    iota(h("RSN"), [[0, 64], [-255, 16]], 255, 0, True)
+    iota(h("X", ZC, ZC + 16), [[0, 16]], 0, 0, True)
+    iota(h("X", TR, WIN), [[0, WIN - TR]], 0, 0, True)
+    ts(h("PQ"), h("PI"), 15, A.bitwise_and)
+    ts(h("PG"), h("PI"), 112, A.bitwise_and)
+    ts(h("NG"), h("NI"), 112, A.bitwise_and)
+    ts(h("fi", 0, 1), h("PI", 0, 1), 4, A.logical_shift_right, 1, A.bitwise_and)
+    ts(col(H1), h("fi", 0, 1), SC, A.mult)
+    ts(col(H0), col(H1), -1.0, A.mult, SC, A.add)
+    ts(col(G1), h("fi", 0, 1), 1.0, A.mult)
+    ts(col(G0), col(G1), -1.0, A.mult, 1.0, A.add)
+    ts(h("ti"), h("PI"), 1, A.logical_shift_right, 7, A.bitwise_and)
+    tt(h("ti"), h("ti"), h("PG"), A.add)
+    tt(h("WpR"), m128("ti"), m128("NI"), A.is_equal)
+    tt(h("tj"), h("NG"), h("PQ"), A.add)
+    cp(h("zl"), m128("tj"))
+    fill(h("Te"), 0.0)
+    fill(h("To"), 0.0)
+    for nm, src, cc in (("E0", "ID", H0), ("E1", "ID", H1), ("Sa", "UP", H0), ("Sb", "DN", H1)):
+        times(h(nm), h(src), col(cc))
+    act(h("Z0", 64, 128), h("zb", 1, 128, 2), AF.Copy)
+    act(h("Z0", 0, 64), h("zb", 0, 128, 2), AF.Copy)
+    cp(h("V", SB, SB + 64), h("scb", 0, 128, 2))
+    cp(h("V", SB + 64, SB + 128), h("scb", 1, 128, 2))
+
+    def relocate_vector():
+        ts(m128("Sf0"), h("V", SB, SB + 128), col(G0), A.mult)
+        ts(m128("Sf1"), h("V", SB, SB + 128), col(G1), A.mult)
+        turn(h("Te", 16, 144), m128("Sf0"))
+        turn(h("To", 16, 144), m128("Sf1"))
+
+    def relocate_tensor():
+        mms(h("Sx", 0, 128), [(h("E0"), h("Te", 16, 144)), (h("Sa"), h("To", 32, 160)), (h("E1"), h("To", 16, 144)), (h("Sb"), h("Te", 0, 128))])
+
+    def relocate_list():
+        ts(h("S16"), h("Sx", 0, 128), 1.0 / SC, A.mult)
+
+    def refresh_zx(z, hh):
+        act(h("zx", 1024 * hh, 1024 * hh + 1024), ind(h(z), h("zl", *half(hh))), AF.Copy)
+
+    banks = ["Uo", "Ue", "PQs", "P7"]
+
+    refresh_zx("Z0", 1)
+    relocate_vector()
+    relocate_tensor()
+    for n in range(8):
+        b = h(banks[n % 4], 0, 512)
+        mms(b, [(h("WpR"), h("X", 512 * n, 512 * n + 512))])
+        act(h("Q", 512 * n, 512 * n + 512), b, AF.Identity, -255.0)
+    tt(h("W1"), h("PG"), h("N15"), A.is_equal)
+    ts(col(LQ1), h("PQ", 0, 1), 8.0, A.is_lt)
+    ts(col(L0C), col(LQ1), 4096.0, A.mult)
+    ts(col(LQ), col(LQ1), -4097.0, A.mult, 4096.0, A.add)
+    relocate_list()
+    times(h("WTm"), h("W1"), -1.0)
+    times(h("WT2"), h("W1"), 2.0)
+    times(h("WQ"), h("W1"), col(LQ))
+    times(h("WQ0"), h("W1"), col(L0C))
+    ts(h("NQ"), h("NI"), 15, A.bitwise_and)
+    tt(h("blk"), m128("PG"), m128("NG"), A.is_equal)
+    tt(h("MQ"), m128("PQ"), m128("NQ"), A.is_equal)
+    ts(col(THN), h("thb"), 1.0, A.mult)
+    times(m128("tf"), h("MQ"), col(THN))
+    mms(h("Ro", 0, 64), [(h("blk"), h("tf", 0, 64))])
+    ts(h("THB"), h("Ro", 0, 64), -4096.0, A.mult, 4096.0 * 2039 - 2040, A.add)
+    ts(h("THC"), h("THB"), 4096.0 * 2040, A.add)
+    ts(h("tj", 0, 128, 1, 8), h("PI", 0, 128, 1, 8), 16.0, A.mult)
+    tt(h("GI", 0, 128, 1, 8), h("NG", 0, 128, 1, 8), h("tj", 0, 128, 1, 8), A.is_equal)
+    cp(h("wmf", 0, 128, 1, 8), h("wmb", 0, 128, 1, 8))
+    mms(h("VB", 0, 128), [(h("GI", 0, 128, 1, 8), h("wmf", 0, 128, 1, 8))])
+
+    def start_z(hh):
+        mms(h("Ro" if hh else "Re", 0, 64), [(h("WTm", 15 - q, 143 - q), h("zx", 1024 * hh + q, 1024 * hh + 1024, 16)) for q in range(16)], True, False)
+
+    def start_t(hh):
+        mms(h("Ro" if hh else "Re", 0, 64), [(h("ID"), h("THC"))], False, False)
+
+    def constants():
+        ts(h("RS1"), m128("NQ"), 1.0, A.min)
+        ts(m128("tg"), m128("NQ"), -0.0625, A.mult, 0.9375, A.add)
+        for hh in (0, 1):
+            tt(h("Kc", *half(hh)), h("tg", 0, 64), h("KC1"), A.add)
+        tt(h("tf", 0, 64), h("VB", 0, 128, 2), h("MQ", 0, 64), A.mult)
+        tt(h("tf", 64, 128), h("VB", 1, 128, 2), h("MQ", 0, 64), A.mult)
+        ts(col(QC), h("PQ", 0, 1), 1.0, A.mult)
+        ts(h("JS"), h("JJ"), col(QC), A.add, float(SB), A.add)
+        cp(h("VB", 384, 512), h("Kc"))
+        ts(h("JS"), h("JS"), SC, A.mult)
+        scan(h("WX"), h("RS1"), m128("tf"), 0.0, A.mult, A.add)
+        fill(h("V", ZC, ZC + 8), ZC)
+        ts(h("HX"), h("WX", 15, 128, 16), -1.0, A.mult, 1.0, A.add)
+        ts(h("TB"), h("HX"), 1.0e6, A.mult, 8192.0, A.add)
+        tt(h("JN"), h("JS"), h("HX"), A.subtract)
+        fill(h("WX"), 0.0)
+
+    def constants2():
+        ts(col(K37), col(QC), 37.0, A.mult)
+        ts(col(C64), col(QC), 64.0, A.mult)
+        ts(h("ti"), h("ti"), 8.0, A.add)
+        ts(col(WC), h("wb"), 1.0, A.mult)
+        cp(col(AK0), col(K37))
+        ts(h("BASE"), h("J8"), col(C64), A.add)
+        tt(h("WpH"), m128("ti"), m128("NI"), A.is_equal)
+        times(h("WB"), h("blk"), col(WC))
+        ts(h("JZ"), h("JJ"), col(QC), A.add, 64.0, A.mult)
+        tt(h("WpY"), h("WpR"), h("WpH"), A.subtract)
+        times(h("WpM"), h("WpH"), 2.0)
+        times(h("WpX"), h("WpH"), -1.0)
+        fill(h("ONE"), 1.0)
+
+    def gathers(hh):
+        lst = h("S16", *half(hh))
+        tt(h("T%d" % hh), ind(h("X", 0, 4096), lst), h("zx", 1024 * hh, 1024 * hh + 1024), A.max)
+        act(h("C%d" % hh), ind(h("Q", 0, 4096), lst), AF.Copy)
+
+    def sums(t, hh):
+        r = h("Ro" if hh else "Re", 0, 64)
+        part = lambda w, b: [(h(w, 15 - q, 143 - q), h("%s%d" % (b, hh), q, 1024, 16)) for q in range(16)]
+        mms(r, part("WT2", "T"), False, False)
+        mms(r, part("WQ", "C"), False, t > 0)
+        if t == 0:
+            mms(r, part("WQ0", "C"), False, True)
+
+    def keys(t, hh):
+        c, f = half(hh), four(hh)
+        r = h("Ro" if hh else "Re", 0, 64)
+        vb = lambda n: h("VB", 128 * n + c[0], 128 * n + c[1])
+        ns = h("NS", c[0] + 15, c[1], 16)
+        x = lambda n: h("fs", 4 * n + 16 * hh, 4 * n + 4 + 16 * hh)
+        ts(h("MV", *c), r, 0.0, A.is_ge, 4096.0, A.mult)
+        cp(h("Ri", *c), r)
+        tt(vb(0), h("MV", *c), vb(3), A.add)
+        ts(h("vi", *c), h("Ri", *c), 4095, A.bitwise_and)
+        scan(h("NS", *c), h("RS1", 0, 64), h("MV", *c), 0.0, A.mult, A.add)
+        tt(h("ky", *c), vb(0), h("vi", *c), A.add)
+        tt(x(0), h("TB", *f), ns, A.subtract)
+        scan(vb(1), h("ky", *c), h("ky", *c), -1.0, A.max, A.max)
+        tt(x(1), h("JN", *f), ns, A.subtract)
+        tt(h("dd", *c), vb(1), h("ky", *c), A.subtract)
+        ts(x(0), x(0), ZC * SC, A.min)
+        tt(h("GG", *c), h("Sx", *c), h("dd", *c), A.subtract)
+        tt(x(2), x(0), x(1), A.max)
+        scan(h("DR", *c), h("dd", *c), h("GG", *c), 0.0, A.min, A.max)
+        tt(h("XS", *f), h("DR", c[0] + 15, c[1], 16), x(2), A.max)
+        ts(h("ov", *f), h("XS", *f), 1.0 / SC, A.mult)
+        cp(h("F%d" % t, *c), ind(h("V", 0, VW), h("ov", *f)))
+
+    def dgather(t, hh, n):
+        a = 32 * n
+        act(h("D%d" % hh, 16 * a, 16 * a + 512), ind(h("X", 0, 4112), h("F%d" % t, 64 * hh + a, 64 * hh + a + 32)), AF.Copy)
+
+    def extremes(hh):
+        for a, b in ((0, 512), (512, 1024)):
+            scan(h("mx", a, b), h("RSM", a, b), h("D%d" % hh, a, b), 0.0, A.min, A.max)
+            scan(h("mn", a, b), h("RSN", a, b), h("D%d" % hh, a, b), 255.0, A.max, A.min)
+
+    def y_of(t, hh):
+        c = half(hh)
+        tt(h("ym", *c), h("mx", 15, 1024, 16), h("mn", 15, 1024, 16), A.add)
+        ts(h("yi", *c), h("ym", *c), 1, A.arith_shift_right)
+        tt(h("dz", *c), h("yi", *c), h("Z%d" % (t % 2), *c), A.subtract)
+        zn = h("Z%d" % ((t + 1) % 2), *c)
+        act(zn, h("dz", *c), AF.Abs)
+        cp(h("msg", 72 * t, 72 * t + 64) if hh else h("yE%d" % (t % 2)), h("yi", *c))
+        mms(h("Uo" if hh else "Ue", 0, 64), [(h("WB"), zn)])
+
+    def place(t, hh):
+        c, f = half(hh), four(hh)
+        fi = lambda n: h("fi", 4 * n, 4 * n + 4)
+        tt(h("um", *c), h("Uo" if hh else "Ue", 0, 64), h("MQ", 0, 64), A.mult)
+        scan(h("us", *c), h("RS1", 0, 64), h("um", *c), 0.0, A.mult, A.add)
+        cp(fi(2 * hh), h("us", c[0] + 15, c[1], 16))
+        ts(fi(2 * hh + 1), fi(2 * hh), 31, A.bitwise_and)
+        if hh:
+            tt(h("msg", 72 * t + 64, 72 * t + 68), fi(3), h("HX", *f), A.add)
+        else:
+            tt(h("fs", 36, 40), fi(1), h("fs", 32, 36), A.add)
+            cp(h("L%d" % (t % 2), *f), h("fs", 36, 40))
+
+    def write_half(t, hh, y):
+        c = half(hh)
+        lst = h("L%d" % (t % 2), *four(hh))
+        win = h("X", 0, WIN)
+        if t == NSTEP - 1:
+            cp(ind(win, lst), y)
+            return
+        act(h("qx", *c), ind(win, lst), AF.Copy)
+        tt(h("qm", *c), ind(win, lst), y, A.max)
+        pq = h("PQs", *c)
+        mms(pq, [(h("WpY"), y), (h("WpX"), h("qx", *c)), (h("WpM"), h("qm", *c))])
+        cp(ind(win, lst), y)
+        act(h("Qn", *c), pq, AF.Identity, -255.0)
+        cp(ind(h("Q", 0, WIN), lst), h("Qn", *c))
+
+    x8 = lambda n: h("tg", 8 * n, 8 * n + 8)
+
+    def books1(t):
+        ts(h("HX"), h("XS"), ZC * SC, A.is_equal, float(TR), A.mult)
+        if t < NSTEP - 1:
+            tt(h("BO"), h("NS", 15, 128, 16), h("TB"), A.is_ge)
+            ts(h("HAS"), h("XS"), ZC * SC, A.not_equal)
+            mms(h("P7", 0, 8), [(h("ONE"), h("BO"))])
+
+    def books2(t):
+        ak = AK1 if t % 2 == 0 else AK0
+        run("v", lambda: V.tensor_reduce(ap(col(A1)), ap(h("P7", 0, 8)), AX.X, A.add), col(A1), [h("P7", 0, 8)], 64 * CY)
+        ts(x8(0), h("TB"), 5.0e5, A.is_lt)
+        cp(h("fi", 0, 1), col(A1))
+        tt(x8(1), x8(0), h("HAS"), A.subtract)
+        ts(h("fi", 0, 1), h("fi", 0, 1), 31, A.bitwise_and)
+        cp(h("WX", 0, 128, 16), x8(1))
+        ts(col(CA), h("fi", 0, 1), -4096.0, A.mult)
+        ts(x8(2), x8(1), -4096.0, A.mult, 8192.0, A.add)
+        ts(h("THC"), h("THB"), col(CA), A.add, -4096.0 * 2041 - 2040, A.max)
+        scan(h("VB", 256, 384), h("RS1"), h("WX"), 0.0, A.mult, A.add)
+        ts(x8(3), h("HAS"), 1.0e6, A.mult)
+        tt(h("JN"), h("JS"), h("HAS"), A.subtract)
+        tt(h("VB", 0, 128), h("MV"), h("VB", 256, 384), A.mult)
+        tt(h("TB"), x8(2), x8(3), A.add)
+        tt(col(ak), col(A1), col(K37), A.add)
+        tt(h("VB", 384, 512), h("VB", 0, 128), h("Kc"), A.add)
+
+    def new_lists(t):
+        ff = h("VB", 256, 384)
+        cp(h("si", 0, 64), h("Ue", 0, 64))
+        cp(h("si", 64, 128), h("Uo", 0, 64))
+        tt(h("tf", 0, 8), h("HX"), h("JZ"), A.add)
+        cp(ff, h("F%d" % t))
+        ts(h("si"), h("si"), 4095, A.bitwise_and)
+        ts(h("oz"), h("tf", 0, 8), 1.0 / 64, A.mult)
+        tt(h("sj"), h("si"), ff, A.mult)
+        ts(h("sj"), h("sj"), 5, A.logical_shift_right)
+        tt(h("si"), h("sj"), ff, A.add)
+        ts(h("si"), h("si"), col(AK0 if t % 2 == 0 else AK1), A.add)
+        ts(h("sj"), h("si"), 4095, A.bitwise_and)
+        cp(ind(h("V", SB, SB + 256), h("oz")), h("sj"))
+
+    cores = T.cores
+    start_z(1)
+    start_t(1)
+    for t in range(NSTEP):
+        last = t == NSTEP - 1
+        fresh = 1 <= t < NSTEP - 1
+        gathers(1)
+        if t == 0:
+            ts(h("V", 0, 2048), h("vwb"), 4095, A.bitwise_and)
+            ts(h("V", 2048, 4096), h("vwb"), 12, A.logical_shift_right)
+            refresh_zx("Z0", 0)
+            start_z(0)
+            start_t(0)
+        gathers(0)
+        sums(t, 1)
+        sums(t, 0)
+        if fresh:
+            refresh_zx("Z%d" % (t % 2), 1)
+        p = (t - 1) % 2
+        if t == 0:
+            constants()
+        else:
+            cp(ind(h("V", 0, WIN), h("L%d" % p, 0, 4)), h("F%d" % (t - 1), 0, 64))
+            cp(ind(h("V", 0, WIN), h("L%d" % p, 4, 8)), h("rxf", 64 * t - 64, 64 * t))
+        keys(t, 1)
+        dst = cores[(rank + 1 + t % 3) % len(cores)]
+        if not last:
+            send(h("rxf", 64 * t, 64 * t + 64), h("F%d" % t, 64, 128), "rf%d" % t, dst)
+        dgather(t, 1, 0)
+        dgather(t, 1, 1)
+        keys(t, 0)
+        dgather(t, 0, 0)
+        if t == 0:
+            constants2()
+        extremes(1)
+        y_of(t, 1)
+        dgather(t, 0, 1)
+        books1(t)
+        if fresh:
+            refresh_zx("Z%d" % (t % 2), 0)
+        if not last:
+            start_z(1)
+        tt(h("fs", 32, 36), h("HX", 0, 4), h("BASE", 0, 4), A.add)
+        place(t, 1)
+        send(h("rxy", 72 * t, 72 * t + 68), h("msg", 72 * t, 72 * t + 68), "ry%d" % t, dst)
+        if fresh:
+            relocate_vector()
+            relocate_tensor()
+            cp(ind(h("Q", 0, WIN), h("L%d" % p)), h("QR"))
+        extremes(0)
+        y_of(t, 0)
+        if not last:
+            books2(t)
+        place(t, 0)
+        yE = h("yE%d" % (t % 2))
+        write_half(t, 0, yE)
+        if not last:
+            start_z(0)
+            start_t(1)
+            start_t(0)
+        new_lists(t)
+        if fresh:
+            relocate_list()
+        if last:
+            cp(h("so", 0, 128, 2), h("V", SB, SB + 64))
+            cp(h("so", 1, 128, 2), h("V", SB + 64, SB + 128))
+            dma("y", "dys", T.ys[:, :], ap(h("so")), None, h("so"))
+            zf = "Z%d" % (NSTEP % 2)
+            act(h("zo", 0, 128, 2), h(zf, 0, 64), AF.Copy)
+            act(h("zo", 1, 128, 2), h(zf, 64, 128), AF.Copy)
+            dma("y", "dyz", T.yz[:, :], ap(h("zo")), None, h("zo"))
+        src = cores[(rank - 1 - t % 3) % len(cores)]
+        landed = len(topo.engines(src, core)[:ENG])
+        if not last:
+            recv(h("rxf", 64 * t, 64 * t + 64), "rf%d" % t, landed)
+        recv(h("rxy", 72 * t, 72 * t + 68), "ry%d" % t, landed)
+        rx = h("rxy", 72 * t, 72 * t + 64)
+        tt(h("fs", 40, 44), h("rxy", 72 * t + 64, 72 * t + 68), h("BASE", 4, 8), A.add)
+        cp(h("L%d" % (t % 2), 4, 8), h("fs", 40, 44))
+        write_half(t, 1, rx)
+        if t < NSTEP - 2:
+            mms(h("P7", 128, 192), [(h("WpR"), yE)])
+            mms(h("P7", 192, 256), [(h("WpR"), rx)])
+            act(h("QR"), h("P7", 128, 256), AF.Identity, -255.0)
+    dma("y", "dyx", T.yx[:, :], ap(h("X", 0, 4096)), None, h("X", 0, 4096))
+    schedule()
+    for s in sorted(total):
+        wait("g", (s, total[s]), {s: total[s]})

@@ -1,35 +1,37 @@
-from concourse.mybir import AluOpType as A, ActivationFunctionType as AF, AxisListType as AX
+from concourse.mybir import AluOpType as A, ActivationFunctionType as AF
 
-BF, F32, I32, U16 = "bfloat16", "float32", "int32", "uint16"
+BF, F32, I32, U16, F16 = "bfloat16", "float32", "int32", "uint16", "float16"
 NSTEP = 6
 ZC = 4096
-SB = 4104
-VW = 4232
 TR = 8192
 WIN = 12288
+HW = 192
+VB = HW * NSTEP
+ZV = VB + 4096
+LA = ZV + 8
+MARK = 1 << 24
 SC = 2.0 ** -17
+RND = 1.5 * 2.0 ** 28
 CY = 0.83e-3 * 1.25
 WAKE = 0.1
+ROUNDS = 2
 ENG = 8
+PIECES = (0, 2, 6, 10, 14, 16)
+ZG = 15
 
-SCRATCH = {
-    "X": ("sbuf", [128, WIN], BF), "Q": ("sbuf", [128, WIN], BF), "V": ("sbuf", [128, WIN], I32),
-    "vwb": ("sbuf", [128, 2048], I32), "zx": ("sbuf", [128, 2048], BF), "cols": ("sbuf", [128, 32], F32), "GI": ("sbuf", [128, 128], BF), "wmf": ("sbuf", [128, 128], BF),
-    "msg": ("sbuf", [128, NSTEP * 72], BF), "rxy": ("sbuf", [128, NSTEP * 72], BF), "rxf": ("sbuf", [128, NSTEP * 64], U16),
-    "fs": ("sbuf", [128, 48], F32), "fi": ("sbuf", [128, 16], I32), "Te": ("sbuf", [128, 160], F32), "To": ("sbuf", [128, 160], F32),
-}
+SCRATCH = {"X": ("sbuf", [128, WIN], BF), "Q": ("sbuf", [128, WIN], F32), "V": ("sbuf", [128, LA + 128 + 256 * NSTEP], I32)}
 for _w, _d, _names in (
-        (1, I32, "wb thb"), (8, I32, "J8 JJ"), (8, F32, "BASE JS JN JZ TB XS HAS HX"), (8, BF, "BO"), (8, U16, "ov oz L0 L1"),
-        (64, I32, "KC1"), (64, F32, "THB THC"), (64, BF, "yE0 yE1"),
-        (128, I32, "scb wmb si sj Ri vi ym yi"), (128, BF, "dz zb Z0 Z1 WB ONE WpR WpH WpY WpM WpX qm qx Qn QR zo"), (128, U16, "zl S16 F0 F1 F2 F3 F4 F5"),
-        (128, F32, "ky dd GG DR um us OF blk ID UP DN E0 E1 Sa Sb MQ Kc RS1 MV NS WX so"), (144, I32, "PI NI N15 PQ PG NQ NG ti tj"), (144, F32, "tf tg Sf0 Sf1"),
-        (144, BF, "W1 WT2 WTm WQ WQ0"), (1024, BF, "T0 T1 C0 C1 D0 D1 mx mn RSM RSN")):
+        (1, I32, "wb thb"), (8, I32, "p8"), (8, U16, "ov og PL L0 L1"), (8, BF, "W2"), (16, F16, "WQa"), (8, F16, "WQb"), (16, F32, "CB QB f16"), (16, BF, "RH"), (16, I32, "fi i16"),
+        (32, F32, "cols"), (64, F32, "RSU"), (64, BF, "yE0 yE1 MQ20 JR"), (256, BF, "ZR"), (512, BF, "WZ d0 RSM RSN"),
+        (128, I32, "scb wmb si sj yi"), (128, BF, "zb Z0 Z1 WB2 WBn IDb ID2 IDn IDm blb blx MV P0 P1 N0 N1 ymx qm qx zo wmf wj GI L3 sg"), (128, U16, "S0 S1 F16"), (128, F16, "MQh THr"),
+        (128, F32, "OF blk ID MQ NQ us so Qn tf"), (256, F32, "RO"), (144, F32, "SP SPs VC RSK mk dd GG DR O144"), (144, BF, "RA1 RB1 RC1 KC"),
+        (NSTEP * 72, BF, "msg rxy"), (2048, BF, "T zx0 zx1"), (2048, F16, "C D"), (1024, F16, "mx mn")):
     for _n in _names.split():
         SCRATCH[_n] = ("sbuf", [128, _w], _d)
-PSUM = ("Ro", "Re", "Sx", "Uo", "Ue", "PQs", "P7", "VB")
+PSUM = ("RA", "RB", "KB", "PT", "Uo", "Ue", "M1", "M2")
 for _n in PSUM:
     SCRATCH[_n] = ("psum", [128, 512], F32)
-LOADS = ["scb", "zb", "wb", "thb", "wmb", "vwb", "X0", "X1", "X2", "X3"]
+LOADS = ["scb", "zb", "wb", "thb", "wmb", "vw", "X0", "X1", "X2", "X3"]
 SEMAPHORES = ["sv", "ss", "sp", "sg", "ls", "dyx", "dys", "dyz"] + ["d" + n for n in LOADS] + ["ry%d" % t for t in range(NSTEP)] + ["rf%d" % t for t in range(NSTEP - 1)]
 
 
@@ -42,6 +44,7 @@ def rank_program(g, core, T, topo):
     total = {}
     know = {q: {} for q in queues}
     ops = []
+    adds = set()
     hist = {}
 
     def h(name, lo=0, hi=None, step=1, rows=None):
@@ -55,11 +58,17 @@ def rank_program(g, core, T, topo):
             return ap(x[1]).indirect(ap(x[2]))
         t = T[x[0]]
         if x[4]:
-            return t[0:x[4], x[1]:x[2]]
+            return t[0:x[4], x[1]:x[2]] if x[3] == 1 else t[0:x[4], x[1]:x[2]:x[3]]
         return t[:, x[1]:x[2]] if x[3] == 1 else t[:, x[1]:x[2]:x[3]]
 
     def regions(x):
         return [x[1], x[2]] if x[0] == "ind" else [x]
+
+    def apart(a, b):
+        return a[1] >= b[2] or a[2] <= b[1] or (a[3] == b[3] > 1 and (a[1] - b[1]) % a[3] != 0)
+
+    def covers(a, b):
+        return a[1] <= b[1] and b[2] <= a[2] and (a[3] == 1 or (a[3] == b[3] and (a[1] - b[1]) % a[3] == 0))
 
     def wait(q, tok, clock):
         if know[q].get(tok[0], 0) >= tok[1]:
@@ -74,13 +83,13 @@ def rank_program(g, core, T, topo):
         for wr, group in ((False, reads), (True, writes)):
             for x in group:
                 for e in hist.get(x[0], []):
-                    if e[3] == q and q == "p":
+                    if e[2] == q and q == "p":
                         continue
-                    ps = x[0] in PSUM and e[3] != q
-                    if not ps and (e[0] >= x[2] or e[1] <= x[1]):
+                    ps = x[0] in PSUM and e[2] != q
+                    if not ps and apart(e[0], x):
                         continue
-                    if (e[2] or wr or ps) and (e[4], e[5]) not in todo:
-                        todo.append((e[4], e[5]))
+                    if (e[1] or wr or ps) and (e[3], e[4]) not in todo:
+                        todo.append((e[3], e[4]))
         todo.sort(key=lambda c: -len(c[1]))
         for tok, clock in todo:
             wait(q, tok, clock)
@@ -91,13 +100,12 @@ def rank_program(g, core, T, topo):
         tag = tag or q
         for wr, group in ((True, writes), (False, reads)):
             for x in group:
-                lo, hi = x[1], x[2]
                 lst = hist.setdefault(x[0], [])
                 if wr:
-                    lst[:] = [e for e in lst if not (e[0] >= lo and e[1] <= hi)]
+                    lst[:] = [e for e in lst if not covers(x, e[0])]
                 else:
-                    lst[:] = [e for e in lst if not (not e[2] and e[3] == tag and e[0] >= lo and e[1] <= hi and tag in own)]
-                lst.append((lo, hi, wr, tag, tok, clock))
+                    lst[:] = [e for e in lst if not (not e[1] and e[2] == tag and covers(x, e[0]) and tag in own)]
+                lst.append((x, wr, tag, tok, clock))
 
     def bump(sem, n):
         total[sem] = total.get(sem, 0) + n
@@ -110,38 +118,55 @@ def rank_program(g, core, T, topo):
             for wr, group in ((False, reads), (True, writes)):
                 for x in group:
                     for e in seen.get(x[0], []):
-                        ps = x[0] in PSUM and e[3] != tag
-                        if not ps and (e[0] >= x[2] or e[1] <= x[1]):
+                        if apart(e[0], x) or (x[0] in PSUM and i in adds and e[3] in adds):
                             continue
-                        if e[2] or wr or ps:
-                            pred[i].append(e[4])
+                        if e[1] or wr:
+                            pred[i].append(e[3])
             for wr, group in ((True, writes), (False, reads)):
                 for x in group:
                     lst = seen.setdefault(x[0], [])
-                    if wr:
-                        lst[:] = [e for e in lst if not (e[0] >= x[1] and e[1] <= x[2])]
-                    lst.append((x[1], x[2], wr, tag, i))
-        succ, left = [[] for _ in ops], [0] * n
+                    if wr and i not in adds:
+                        lst[:] = [e for e in lst if not covers(x, e[0])]
+                    lst.append((x, wr, tag, i))
+        succ = [[] for _ in ops]
         for i in range(n):
             pred[i] = sorted(set(pred[i]))
-            left[i] = len(pred[i])
             for j in pred[i]:
                 succ[j].append(i)
-        rest = [0.0] * n
-        for i in range(n - 1, -1, -1):
-            rest[i] = ops[i][4] + ops[i][5] + max([rest[j] + WAKE for j in succ[i]] + [0.0])
-        ready, free = [0.0] * n, {}
-        cand = [i for i in range(n) if not left[i]]
-        while cand:
-            st, _r, i = min([(max(ready[i], free.get(ops[i][0], 0.0)), -rest[i], i) for i in cand])
-            cand.remove(i)
-            free[ops[i][0]] = st + ops[i][4]
-            for j in succ[i]:
-                w = 0.0 if ops[i][0] == ops[j][0] == "p" else WAKE
-                ready[j] = max(ready[j], st + ops[i][4] + ops[i][5] + w)
-                left[j] -= 1
-                if not left[j]:
-                    cand.append(j)
+        holds = [[o[0]] + sorted(set([x[0] for x in o[2] + o[3] if x[0] in PSUM])) for o in ops]
+
+        def lag(i, j):
+            return ops[i][5] + (0.0 if ops[i][0] == ops[j][0] == "p" else WAKE)
+
+        def place(key, before, after, back):
+            end, used, left = [0.0] * n, {}, [len(b) for b in before]
+            cand = [i for i in range(n) if not left[i]]
+            while cand:
+                i = min(cand, key=lambda c: (key[c], c))
+                cand.remove(i)
+                st = max([end[j] + (lag(i, j) if back else lag(j, i)) for j in before[i]] + [0.0])
+                q, us, was = ops[i][0], ops[i][4], -1.0
+                while was < st:
+                    was = st
+                    for r in holds[i]:
+                        for a, b, who in used.setdefault(r, []):
+                            m = 0.0 if who == q else WAKE
+                            if a - m < st + us and st < b + m and (r == q or who != q):
+                                st = b + m
+                end[i] = st + us
+                for r in holds[i]:
+                    used[r].append((st, end[i], q))
+                for j in after[i]:
+                    left[j] -= 1
+                    if not left[j]:
+                        cand.append(j)
+            return end
+        best = end = place(list(range(n)), pred, succ, False)
+        for _ in range(ROUNDS):
+            end = place([-e for e in place([-e for e in end], succ, pred, True)], pred, succ, False)
+            if max(end) < max(best):
+                best = end
+        for i in sorted(range(n), key=lambda c: (best[c] - ops[c][4], c)):
             ops[i][1]()
 
     def elems(x):
@@ -158,9 +183,9 @@ def rank_program(g, core, T, topo):
     def rate(*xs):
         return 1.0 if [x for x in xs if SCRATCH[x[1][0] if x[0] == "ind" else x[0]][2] in (F32, I32)] else 0.5
 
-    def run(q, call, out, ins, us):
+    def run(q, call, out, ins, us, more=()):
         reads = [r for x in ins for r in regions(x)] + regions(out)[1:]
-        writes = regions(out)[:1]
+        writes = regions(out)[:1] + list(more)
 
         def emit():
             need(q, reads, writes)
@@ -170,68 +195,71 @@ def rank_program(g, core, T, topo):
 
     V, S = g.vector, g.scalar
 
+    def val(s):
+        return ap(s) if isinstance(s, tuple) else s
+
     def tt(o, x, y, op):
         run("v", lambda: V.tensor_tensor(ap(o), ap(x), ap(y), op), o, [x, y], vtime(o, [x, y], 1.0 if x[0] in PSUM or y[0] in PSUM else 2.0))
 
     def ts(o, x, s1, op0, s2=None, op1=None):
         ins = [x] + [s for s in (s1, s2) if isinstance(s, tuple)]
-        c1 = ap(s1) if isinstance(s1, tuple) else s1
         if op1 is None:
-            run("v", lambda: V.tensor_scalar(ap(o), ap(x), c1, None, op0), o, ins, vtime(o, [x], rate(o, x)))
+            run("v", lambda: V.tensor_scalar(ap(o), ap(x), val(s1), None, op0), o, ins, vtime(o, [x], rate(o, x)))
         else:
-            run("v", lambda: V.tensor_scalar(ap(o), ap(x), c1, s2, op0, op1), o, ins, vtime(o, [x], rate(o, x)))
+            run("v", lambda: V.tensor_scalar(ap(o), ap(x), val(s1), val(s2), op0, op1), o, ins, vtime(o, [x], rate(o, x)))
 
     def cp(o, x):
         run("v", lambda: V.tensor_copy(ap(o), ap(x)), o, [x], vtime(o, [x], rate(o, x)))
 
     def fill(o, c):
-        run("v", lambda: V.memset(ap(o), c), o, [], vtime(o, [], 1.0))
+        run("v", lambda: V.memset(ap(o), c), o, [], vtime(o, [], rate(o)))
 
     def scan(o, d0, d1, init, op0, op1):
         run("v", lambda: V.tensor_tensor_scan(ap(o), ap(d0), ap(d1), init, op0, op1), o, [d0, d1], vtime(o, [], rate(o, d0, d1)))
 
-    def turn(o, x):
-        run("v", lambda: V.transpose(ap(o), ap(x)), o, [x], vtime(o, [], 1.0))
-
-    def act(o, x, f, bias=0.0):
+    def act(o, x, f=AF.Identity, bias=0.0, scale=1.0, accum=None):
         us = 0.065 + 1.56 * elems(o) * CY if x[0] == "ind" else max(64, elems(o)) * CY
-        if f == AF.Copy:
-            run("s", lambda: S.activation(ap(o), ap(x), f), o, [x], us)
+        ins = [x] + [s for s in (bias, scale) if isinstance(s, tuple)]
+        if accum:
+            run("s", lambda: S.activation(ap(o), ap(x), f, bias=val(bias), scale=val(scale), accum_out=ap(accum)), o, ins, us + 0.02, [accum])
         else:
-            run("s", lambda: S.activation(ap(o), ap(x), f, bias=bias), o, [x], us)
+            run("s", lambda: S.activation(ap(o), ap(x), f, bias=val(bias), scale=val(scale)), o, ins, us)
 
-    def times(o, x, s):
-        c = ap(s) if isinstance(s, tuple) else s
-        run("s", lambda: S.activation(ap(o), ap(x), AF.Identity, scale=c), o, [x] + ([s] if isinstance(s, tuple) else []), max(64, elems(o)) * CY)
-
-    def iota(o, pattern, base, cm, small=False):
+    def iota(o, pattern, base, cm):
+        small = SCRATCH[o[0]][2] != I32
         run("g", lambda: g.iota(ap(o), pattern, base, cm, allow_small_or_imprecise_dtypes=small), o, [], 0.13 + 2 * elems(o) * CY)
 
-    def diag(o, base):
-        run("g", lambda: g.affine_select(ap(o), ap(h("OF")), [[1, 128]], A.is_equal, 0.0, base, -1), o, [h("OF")], 0.17 + 2 * elems(o) * CY)
+    def keep(o, x, pattern, op, base, cm):
+        run("g", lambda: g.affine_select(ap(o), ap(x), pattern, op, 0.0, base, cm), o, [x], 0.17 + 2 * elems(o) * CY)
 
-    def mms(out, pairs, start=True, stop=True):
-        reads = [x for p in pairs for x in p]
-        us = len(pairs) * max(64, elems(out)) * CY * (4 if SCRATCH[pairs[0][0][0]][2] == F32 else 1)
+    def mms(items, start=True, stop=True, after=(), mark=()):
+        reads = [x for p in items for x in p[1:]] + list(mark)
+        writes = [p[0] for p in items] + list(after)
+        us = sum([max(min(64, elems(l)), elems(o)) * CY * (4 if SCRATCH[l[0]][2] == F32 else 1) for o, l, r in items])
 
         def emit():
-            need("p", reads, [out])
-            for n, (l, r) in enumerate(pairs):
-                i = g.tensor.matmul(ap(out), ap(l), ap(r), start and n == 0, stop and n == len(pairs) - 1)
+            need("p", reads, writes)
+            for n, (o, l, r) in enumerate(items):
+                i = g.tensor.matmul(ap(o), ap(l), ap(r), start and n == 0, stop and n == len(items) - 1)
             i.then_inc(T.sem["sp"], 1)
-            note("p", bump("sp", 1), reads, [out])
-        ops.append(("p", emit, reads, [out], us, 0.0, "p"))
+            note("p", bump("sp", 1), reads, writes)
+        if not start and not stop:
+            adds.add(len(ops))
+        ops.append(("p", emit, reads, writes, us, 0.0, "p"))
 
-    def dma(q, sem, out, in_, ohandle=None, ihandle=None):
+    def mm(out, pairs, start=True, stop=True):
+        mms([(out, l, r) for l, r in pairs], start, stop)
+
+    def dma(q, sem, out, in_, ohandle=None, ihandle=None, lat=2.0):
         reads, writes = ([ihandle] if ihandle else []), ([ohandle] if ohandle else [])
 
         def emit():
             need(q, reads, writes)
             queues[q].dma_start(out, in_).then_inc(T.sem[sem], 16)
             note(q, bump(sem, 16), reads, writes, q + "dma")
-        ops.append((q, emit, reads, writes, 0.06, 3.0, q + "dma"))
+        ops.append((q, emit, reads, writes, 0.06, lat, q + "dma"))
 
-    def send(out, in_, remote, dst):
+    def send(out, in_, remote, dst, after=None):
         rid, pid, _se = topo.addr(dst)
         eng = topo.engines(core, dst)[:ENG]
         m = 0
@@ -242,214 +270,273 @@ def rank_program(g, core, T, topo):
             need("g", [in_], [])
             g.remote_dma(ap(out), ap(in_), T.sem[remote], T.sem["ls"], pid, rid, m)
             bump("ls", len(eng))
-        ops.append(("g", emit, [in_], [("@" + remote, 0, 1, 1)], 0.8, 0.0, "g"))
+        ops.append(("g", emit, [in_] + ([("@" + after, 0, 1, 1)] if after else []), [("@" + remote, 0, 1, 1)], 0.8, 0.0, "g"))
 
     def recv(out, sem, n):
         def emit():
-            hist.setdefault(out[0], []).append((out[1], out[2], True, "remote", bump(sem, n), {sem: n}))
+            hist.setdefault(out[0], []).append((out, True, "remote", bump(sem, n), {sem: n}))
         ops.append(("remote" + sem, emit, [("@" + sem, 0, 1, 1)], [out], 2.5, 0.0, "remote"))
 
-    for b, t in (("scb", T.scan), ("zb", T.z0), ("thb", T.th), ("wb", T.wt)):
+    def chain(name):
+        o = ops[-1]
+        ops[-1] = o[:3] + (o[3] + [(name, 0, 1, 1)],) + o[4:]
+
+    def load_x(n):
+        dma("y", "dX%d" % n, ap(h("X", 1024 * n, 1024 * n + 1024)), T.reg[:, 1024 * n:1024 * n + 1024], h("X", 1024 * n, 1024 * n + 1024), lat=0.0)
+        ops[-1] = ops[-1][:4] + (0.9, 1.6) + ops[-1][6:]
+    for b, t in (("zb", T.z0), ("scb", T.scan), ("thb", T.th), ("wb", T.wt)):
         dma("y", "d" + b, ap(h(b)), t[:, :], h(b))
+    dma("s", "dwmb", T["wmb"][0:8, :], T.warm[:, :], h("wmb"))
     for n in range(4):
-        dma("s", "dX%d" % n, ap(h("X", 1024 * n, 1024 * n + 1024)), T.reg[:, 1024 * n:1024 * n + 1024], h("X", 1024 * n, 1024 * n + 1024))
-    dma("y", "dwmb", T["wmb"][0:8, :], T.warm[:, :], h("wmb"))
-    dma("y", "dvwb", ap(h("vwb")), T.vw[:, :], h("vwb"))
+        load_x(n)
+    dma("y", "dvw", ap(h("V", VB, VB + 2048)), T.vw[:, :], h("V", VB, VB + 2048), lat=5.0)
+    for o in ops:
+        o[1]()
+    landing = {o[3][0][:3]: 2.0 for o in ops}
+    for n in range(4):
+        landing[("X", 1024 * n, 1024 * n + 1024)] = 2.8 + 0.9 * n
+    landing[("V", VB, VB + 2048)] = 9.0
+    ops[:] = [("load%d" % n, lambda: None, [], o[3], landing[o[3][0][:3]], 0.0, o[6]) for n, o in enumerate(ops)]
 
-    m128 = lambda b: h(b, 0, 128)
     col = lambda c: h("cols", c, c + 1)
-    QC, H0, H1, LQ, L0C, K37, AK0, AK1, CA, WC, THN, C64, A1, G0, G1, LQ1 = range(16)
-    half = lambda hh: (64 * hh, 64 * hh + 64)
-    four = lambda hh: (4 * hh, 4 * hh + 4)
+    QC, M0, M1, M2, M3, QBIAS, D0C, THN, WC, WN, K37, AK0, AK1, AT0, AT1, AP, T1, T2, ACC, C64 = range(20)
+    half = lambda hh: (0, 64) if hh else (64, 128)
+    four = lambda hh: (0, 4) if hh else (4, 8)
+    BK8 = h("blk", 0, 128, 16)
+    merged = lambda t: LA + 256 * (t + 1)
+    kept = lambda t: VB - HW * (t + 1)
+    iota(h("p8", 0, 1), [[0, 1]], 0, 1)
+    fill(h("O144"), 1.0)
     fill(h("OF"), 1.0)
-    iota(h("PI"), [[0, 144]], 0, 1)
-    iota(h("NI"), [[1, 144]], 0, 0)
-    diag(h("ID"), 0)
-    diag(h("UP"), -16)
-    diag(h("DN"), 16)
-    iota(h("N15"), [[1, 144]], -15, 0)
-    iota(h("KC1"), [[16384, 4], [0, 16]], 0, 0)
-    iota(h("J8"), [[32, 2], [1024, 4]], 0, 0)
-    iota(h("JJ"), [[16, 8]], 0, 0)
-    iota(h("RSM"), [[0, 64], [256, 16]], 0, 0, True)
-    iota(h("RSN"), [[0, 64], [-255, 16]], 255, 0, True)
-    iota(h("X", ZC, ZC + 16), [[0, 16]], 0, 0, True)
-    iota(h("X", TR, WIN), [[0, WIN - TR]], 0, 0, True)
-    ts(h("PQ"), h("PI"), 15, A.bitwise_and)
-    ts(h("PG"), h("PI"), 112, A.bitwise_and)
-    ts(h("NG"), h("NI"), 112, A.bitwise_and)
-    ts(h("fi", 0, 1), h("PI", 0, 1), 4, A.logical_shift_right, 1, A.bitwise_and)
-    ts(col(H1), h("fi", 0, 1), SC, A.mult)
-    ts(col(H0), col(H1), -1.0, A.mult, SC, A.add)
-    ts(col(G1), h("fi", 0, 1), 1.0, A.mult)
-    ts(col(G0), col(G1), -1.0, A.mult, 1.0, A.add)
-    ts(h("ti"), h("PI"), 1, A.logical_shift_right, 7, A.bitwise_and)
-    tt(h("ti"), h("ti"), h("PG"), A.add)
-    tt(h("WpR"), m128("ti"), m128("NI"), A.is_equal)
-    tt(h("tj"), h("NG"), h("PQ"), A.add)
-    cp(h("zl"), m128("tj"))
-    fill(h("Te"), 0.0)
-    fill(h("To"), 0.0)
-    for nm, src, cc in (("E0", "ID", H0), ("E1", "ID", H1), ("Sa", "UP", H0), ("Sb", "DN", H1)):
-        times(h(nm), h(src), col(cc))
-    act(h("Z0", 64, 128), h("zb", 1, 128, 2), AF.Copy)
-    act(h("Z0", 0, 64), h("zb", 0, 128, 2), AF.Copy)
-    cp(h("V", SB, SB + 64), h("scb", 0, 128, 2))
-    cp(h("V", SB + 64, SB + 128), h("scb", 1, 128, 2))
-
-    def relocate_vector():
-        ts(m128("Sf0"), h("V", SB, SB + 128), col(G0), A.mult)
-        ts(m128("Sf1"), h("V", SB, SB + 128), col(G1), A.mult)
-        turn(h("Te", 16, 144), m128("Sf0"))
-        turn(h("To", 16, 144), m128("Sf1"))
-
-    def relocate_tensor():
-        mms(h("Sx", 0, 128), [(h("E0"), h("Te", 16, 144)), (h("Sa"), h("To", 32, 160)), (h("E1"), h("To", 16, 144)), (h("Sb"), h("Te", 0, 128))])
-
-    def relocate_list():
-        ts(h("S16"), h("Sx", 0, 128), 1.0 / SC, A.mult)
-
-    def refresh_zx(z, hh):
-        act(h("zx", 1024 * hh, 1024 * hh + 1024), ind(h(z), h("zl", *half(hh))), AF.Copy)
-
-    banks = ["Uo", "Ue", "PQs", "P7"]
-
-    refresh_zx("Z0", 1)
-    relocate_vector()
-    relocate_tensor()
+    keep(h("tf"), h("OF"), [[-16, 8], [0, 16]], A.is_ge, 0, 1)
+    keep(h("blk"), h("tf"), [[16, 8], [0, 16]], A.is_ge, 15, -1)
+    ts(h("p8", 1, 2), h("p8", 0, 1), 15, A.bitwise_and)
+    cp(col(QC), h("p8", 1, 2))
+    ts(col(M0), col(QC), 0.0, A.is_equal)
+    ts(col(M1), col(QC), 1.0, A.is_equal)
+    ts(col(M2), col(QC), 2.0, A.is_equal)
+    ts(col(M3), col(QC), 3.0, A.is_equal)
+    ts(h("p8", 2, 3), h("p8", 0, 1), 7, A.bitwise_and)
+    ts(h("p8", 3, 4), h("p8", 0, 1), 3, A.logical_shift_right, 1, A.bitwise_and)
+    ts(col(T1), h("p8", 2, 3), 16.0, A.mult)
+    tt(col(T1), col(T1), h("p8", 3, 4), A.add)
+    iota(h("i16", 0, 8), [[2, 8]], 0, 0)
+    ts(h("PL"), h("i16", 0, 8), col(T1), A.add)
+    fill(h("WZ"), 0.0)
+    WS, WY, WX, WM = [h("WZ", 128 * n, 128 * n + 128) for n in range(4)]
+    for lo, s in ((0, 1.0), (1, 1.0), (128, 1.0), (129, -1.0), (257, -1.0), (385, 2.0)):
+        act(h("WZ", lo, lo + 113, 16), BK8, scale=s)
+    ts(col(D0C), col(M3), 30001.0, A.mult, -30000.0, A.add)
+    iota(h("RSM"), [[0, 32], [256, 16]], -1, 0)
+    act(h("d0"), h("WZ"), bias=col(D0C), scale=0.0)
+    banks = ["KB", "PT", "Uo", "Ue"]
     for n in range(8):
-        b = h(banks[n % 4], 0, 512)
-        mms(b, [(h("WpR"), h("X", 512 * n, 512 * n + 512))])
-        act(h("Q", 512 * n, 512 * n + 512), b, AF.Identity, -255.0)
-    tt(h("W1"), h("PG"), h("N15"), A.is_equal)
-    ts(col(LQ1), h("PQ", 0, 1), 8.0, A.is_lt)
-    ts(col(L0C), col(LQ1), 4096.0, A.mult)
-    ts(col(LQ), col(LQ1), -4097.0, A.mult, 4096.0, A.add)
-    relocate_list()
-    times(h("WTm"), h("W1"), -1.0)
-    times(h("WT2"), h("W1"), 2.0)
-    times(h("WQ"), h("W1"), col(LQ))
-    times(h("WQ0"), h("W1"), col(L0C))
-    ts(h("NQ"), h("NI"), 15, A.bitwise_and)
-    tt(h("blk"), m128("PG"), m128("NG"), A.is_equal)
-    tt(h("MQ"), m128("PQ"), m128("NQ"), A.is_equal)
-    ts(col(THN), h("thb"), 1.0, A.mult)
-    times(m128("tf"), h("MQ"), col(THN))
-    mms(h("Ro", 0, 64), [(h("blk"), h("tf", 0, 64))])
-    ts(h("THB"), h("Ro", 0, 64), -4096.0, A.mult, 4096.0 * 2039 - 2040, A.add)
-    ts(h("THC"), h("THB"), 4096.0 * 2040, A.add)
-    ts(h("tj", 0, 128, 1, 8), h("PI", 0, 128, 1, 8), 16.0, A.mult)
-    tt(h("GI", 0, 128, 1, 8), h("NG", 0, 128, 1, 8), h("tj", 0, 128, 1, 8), A.is_equal)
-    cp(h("wmf", 0, 128, 1, 8), h("wmb", 0, 128, 1, 8))
-    mms(h("VB", 0, 128), [(h("GI", 0, 128, 1, 8), h("wmf", 0, 128, 1, 8))])
+        b = h(banks[n % 4])
+        mm(b, [(WS, h("X", 512 * n, 512 * n + 512))])
+        scan(h("Q", 512 * n, 512 * n + 512), h("d0"), b, float(VB + 512 * n - 1), A.add, A.max)
+    act(h("Z0", 0, 64), h("zb", 1, 128, 2))
+    act(h("Z0", 64, 128), h("zb", 0, 128, 2))
+    cp(h("V", LA, LA + 64), h("scb", 1, 128, 2))
+    cp(h("V", LA + 64, LA + 128), h("scb", 0, 128, 2))
+    cp(h("S0"), ind(h("V", LA, LA + 128), h("PL")))
 
-    def start_z(hh):
-        mms(h("Ro" if hh else "Re", 0, 64), [(h("WTm", 15 - q, 143 - q), h("zx", 1024 * hh + q, 1024 * hh + 1024, 16)) for q in range(16)], True, False)
-
-    def start_t(hh):
-        mms(h("Ro" if hh else "Re", 0, 64), [(h("ID"), h("THC"))], False, False)
+    def spread(z, zx, ng):
+        act(h(zx, 0, 2048, 16), ind(h(z), h("PL")))
+        for k in range(1, 16):
+            if k <= ng:
+                keep(h(zx, k, 2048, 16), h(zx, 0, 2048, 16), [[0, 128]], A.is_ge, 0, 0)
+            else:
+                act(h(zx, k, 2048, 16), h(zx, 0, 2048, 16))
+    spread("Z0", "zx0", 0)
+    tt(col(T2), col(M0), col(M1), A.add)
+    ts(col(QBIAS), col(M3), -3200.0, A.mult)
+    ts(col(T2), col(T2), -2040.0, A.mult)
+    tt(col(QBIAS), col(QBIAS), col(T2), A.add)
+    act(h("W2"), BK8, scale=2.0)
+    ts(col(T2), col(M2), -256.0, A.mult, col(M3), A.add)
+    ts(h("WQa", 0, 8), BK8, col(M0), A.mult, -1.0, A.mult)
+    ts(h("WQa", 8, 16), BK8, col(T2), A.mult)
+    ts(col(T1), col(M2), 8192.0, A.mult, col(M1), A.add)
+    ts(h("WQb"), BK8, col(T1), A.mult)
+    iota(h("NQ"), [[0, 8], [1, 16]], 0, 0)
+    ts(h("MQ"), h("NQ"), col(QC), A.is_equal)
+    act(h("MQh"), h("MQ"))
+    ts(col(THN), h("thb"), -1.0, A.mult, 2040.0, A.add)
+    act(h("THr"), h("blk"), scale=col(THN))
+    keep(h("ID"), h("OF"), [[1, 128]], A.is_equal, 0, -1)
+    act(h("IDb"), h("ID"))
+    act(h("IDm"), h("ID"), scale=-16384.0)
+    act(h("blb"), h("blk"))
+    fill(h("ZR"), 0.0)
+    fill(col(AT0), -15.5)
+    keep(h("GI", 0, 128, 1, 8), h("O144", 0, 128, 1, 8), [[1, 8], [0, 16]], A.is_equal, 0, -1)
+    cp(h("wj", 0, 64, 1, 8), h("wmb", 1, 128, 2, 8))
+    cp(h("wj", 64, 128, 1, 8), h("wmb", 0, 128, 2, 8))
+    mm(h("M1", 0, 128), [(h("wj", 0, 128, 1, 8), h("GI", 0, 128, 1, 8))])
+    tt(h("wmf"), h("M1", 0, 128), h("MQ"), A.mult)
+    mm(h("M2", 0, 128), [(h("blb"), h("wmf"))])
+    act(h("N0"), h("M2", 0, 128), bias=1.0, scale=-1.0)
+    fill(h("P0"), 0.0)
 
     def constants():
-        ts(h("RS1"), m128("NQ"), 1.0, A.min)
-        ts(m128("tg"), m128("NQ"), -0.0625, A.mult, 0.9375, A.add)
-        for hh in (0, 1):
-            tt(h("Kc", *half(hh)), h("tg", 0, 64), h("KC1"), A.add)
-        tt(h("tf", 0, 64), h("VB", 0, 128, 2), h("MQ", 0, 64), A.mult)
-        tt(h("tf", 64, 128), h("VB", 1, 128, 2), h("MQ", 0, 64), A.mult)
-        ts(col(QC), h("PQ", 0, 1), 1.0, A.mult)
-        ts(h("JS"), h("JJ"), col(QC), A.add, float(SB), A.add)
-        cp(h("VB", 384, 512), h("Kc"))
-        ts(h("JS"), h("JS"), SC, A.mult)
-        scan(h("WX"), h("RS1"), m128("tf"), 0.0, A.mult, A.add)
-        fill(h("V", ZC, ZC + 8), ZC)
-        ts(h("HX"), h("WX", 15, 128, 16), -1.0, A.mult, 1.0, A.add)
-        ts(h("TB"), h("HX"), 1.0e6, A.mult, 8192.0, A.add)
-        tt(h("JN"), h("JS"), h("HX"), A.subtract)
-        fill(h("WX"), 0.0)
+        keep(h("SP"), h("O144"), [[16, 8], [1, 18]], A.is_equal, 0, -1)
+        iota(h("mk"), [[0, 8], [1, 18]], 0, 0)
+        fill(h("SP", 16, 144, 18), 0.0)
+        fill(h("SP", 17, 144, 18), 0.0)
+        act(h("SPs"), h("SP"), scale=SC)
+        act(h("RA1"), h("SP"), scale=4096.0)
+        act(h("RB1"), h("SP"), scale=4096.0)
+        act(h("RC1"), h("SP"), scale=0.0)
+        act(h("RA1", 16, 144, 18), BK8, scale=-32768.0)
+        act(h("RA1", 17, 144, 18), BK8, scale=-65536.0)
+        act(h("RB1", 16, 144, 18), BK8, scale=-32768.0)
+        act(h("RC1", 17, 144, 18), BK8, scale=-4096.0)
+        act(h("KC"), h("mk"), bias=0.9375, scale=-0.0625)
+        act(h("KC", 16, 144, 18), BK8, bias=53248.0, scale=0.0)
+        act(h("KC", 17, 144, 18), BK8, bias=65536.0, scale=0.0)
+        act(h("RSK"), h("mk"), scale=1.0e7)
+        act(h("VC"), h("mk"), bias=3200.0 * SC, scale=0.0)
+        act(h("VC", 16, 144, 18), BK8, bias=ZV * SC, scale=0.0)
+        iota(h("i16", 8, 16), [[16, 8]], LA, 0)
+        ts(h("VC", 17, 144, 18), h("i16", 8, 16), col(QC), A.add, SC, A.mult)
+        fill(h("V", ZV, ZV + 8), MARK)
+        ts(h("V", VB + 2048, VB + 3072), h("V", VB, VB + 1024), 12, A.logical_shift_right)
+        ts(h("V", VB + 3072, VB + 4096), h("V", VB + 1024, VB + 2048), 12, A.logical_shift_right)
+        iota(h("X", ZC, ZC + 16), [[0, 16]], 0, 0)
+        iota(h("RSN"), [[0, 32], [-256, 16]], 255, 0)
 
     def constants2():
-        ts(col(K37), col(QC), 37.0, A.mult)
-        ts(col(C64), col(QC), 64.0, A.mult)
-        ts(h("ti"), h("ti"), 8.0, A.add)
-        ts(col(WC), h("wb"), 1.0, A.mult)
-        cp(col(AK0), col(K37))
-        ts(h("BASE"), h("J8"), col(C64), A.add)
-        tt(h("WpH"), m128("ti"), m128("NI"), A.is_equal)
-        times(h("WB"), h("blk"), col(WC))
-        ts(h("JZ"), h("JJ"), col(QC), A.add, 64.0, A.mult)
-        tt(h("WpY"), h("WpR"), h("WpH"), A.subtract)
-        times(h("WpM"), h("WpH"), 2.0)
-        times(h("WpX"), h("WpH"), -1.0)
-        fill(h("ONE"), 1.0)
+        act(h("ID2"), h("ID"), scale=2.0)
+        act(h("IDn"), h("ID"), scale=-1.0)
+        tt(h("blx"), h("blb"), h("ID2"), A.subtract)
+        ts(col(WC), h("wb"), 2.0, A.mult)
+        ts(col(WN), h("wb"), -1.0, A.mult)
+        act(h("WB2"), h("blk"), scale=col(WC))
+        act(h("WBn"), h("blk"), scale=col(WN))
+        act(h("MQ20"), h("MQ", 0, 64), scale=2.0 ** 20)
+        act(h("RSU"), h("NQ", 0, 64), scale=1.0e7)
+        act(col(K37), col(QC), bias=15.5, scale=37.0)
+        act(col(AK0), col(QC), scale=37.0)
+        act(col(C64), col(QC), scale=64.0)
+        act(h("RH", 0, 8), BK8, scale=-TR / 16.0)
+        act(h("RH", 8, 16), BK8, scale=8.0)
+        iota(h("fi", 0, 4), [[1024, 4]], TR, 0)
+        iota(h("fi", 8, 16), [[16, 8]], 0, 0)
+        fill(h("CB", 0, 4), float(TR))
+        ts(h("CB", 4, 8), h("fi", 0, 4), col(C64), A.add)
+        ts(h("CB", 8, 16), h("fi", 8, 16), col(QC), A.add)
+        ts(h("f16", 0, 4), h("CB", 4, 8), 32.0 - TR, A.add)
+        iota(h("JR", 0, 64, 1, 1), [[1, 64]], 0, 0)
+        act(h("L3", 0, 128, 1, 1), h("NQ", 0, 128, 1, 1), scale=0.0)
+        act(h("L3", 3, 128, 16, 1), h("O144", 0, 8, 1, 1))
+        iota(h("i16", 0, 10), [[64, 5], [64, 2]], VB + 128, 0)
+        iota(h("si", 0, 10), [[1, 5], [0, 2]], 1, 0)
+        ts(h("QB", 0, 10), h("i16", 0, 10), col(M3), A.mult)
+        ts(h("so", 0, 10), h("si", 0, 10), col(M2), A.mult)
+        tt(h("QB", 0, 10), h("QB", 0, 10), h("so", 0, 10), A.add)
+        for n in range(8):
+            iota(h("X", TR + 512 * n, TR + 512 * n + 512), [[0, 512]], 0, 0)
 
-    def gathers(hh):
-        lst = h("S16", *half(hh))
-        tt(h("T%d" % hh), ind(h("X", 0, 4096), lst), h("zx", 1024 * hh, 1024 * hh + 1024), A.max)
-        act(h("C%d" % hh), ind(h("Q", 0, 4096), lst), AF.Copy)
+    def starts(t):
+        n, p = h("N%d" % (t % 2)), h("P%d" % (t % 2))
+        mm(h("RA", 0, 256), [(h("IDb"), h("ZR"))], True, False)
+        mm(h("RB", 0, 128), [(h("MQh"), h("THr")), (h("IDm"), n)], True, False)
+        mm(h("KB", 0, 144), [(h("IDb"), h("KC")), (p, h("RB1")), (n, h("RC1"))], True, False)
+        mm(h("PT", 0, 144), [(h("ID"), h("VC"))], True, False)
 
-    def sums(t, hh):
-        r = h("Ro" if hh else "Re", 0, 64)
-        part = lambda w, b: [(h(w, 15 - q, 143 - q), h("%s%d" % (b, hh), q, 1024, 16)) for q in range(16)]
-        mms(r, part("WT2", "T"), False, False)
-        mms(r, part("WQ", "C"), False, t > 0)
-        if t == 0:
-            mms(r, part("WQ0", "C"), False, True)
+    def first(t):
+        lst, zx = "S%d" % (max(t - 1, 0) % 2), "zx%d" % (max(t - 1, 0) % 2)
+        for a, b in zip(PIECES, PIECES[1:]):
+            l, lo, hi = h(lst, 8 * a, 8 * b), 128 * a, 128 * b
+            act(h("C", lo, hi), ind(h("Q", 0, 4096), l), bias=col(QBIAS))
+            chain("@c")
+            tt(h("T", lo, hi), ind(h("X", 0, 4096), l), h(zx, lo, hi), A.max)
+            chain("@t")
+        ra = [("@ra", 0, 1, 1)]
+        for a, b in zip(PIECES, PIECES[1:]):
+            mms([(h("RA", q, 128, 16), h("T", 128 * q, 128 * q + 128), h("W2")) for q in range(a, b)], False, False, (), ra)
+        for a, b in zip(PIECES, PIECES[1:]):
+            end = b == 16
+            mms([(h("RB", q, 128, 16), h("C", 128 * q, 128 * q + 128), h("WQb")) for q in range(a, b)], False, end, [("@rb", 0, 1, 1)])
+            mms([(h("RA", q, 256, 16), h("C", 128 * q, 128 * q + 128), h("WQa")) for q in range(a, b)], False, end, ra if end else (), () if end else ra)
 
-    def keys(t, hh):
-        c, f = half(hh), four(hh)
-        r = h("Ro" if hh else "Re", 0, 64)
-        vb = lambda n: h("VB", 128 * n + c[0], 128 * n + c[1])
-        ns = h("NS", c[0] + 15, c[1], 16)
-        x = lambda n: h("fs", 4 * n + 16 * hh, 4 * n + 4 + 16 * hh)
-        ts(h("MV", *c), r, 0.0, A.is_ge, 4096.0, A.mult)
-        cp(h("Ri", *c), r)
-        tt(vb(0), h("MV", *c), vb(3), A.add)
-        ts(h("vi", *c), h("Ri", *c), 4095, A.bitwise_and)
-        scan(h("NS", *c), h("RS1", 0, 64), h("MV", *c), 0.0, A.mult, A.add)
-        tt(h("ky", *c), vb(0), h("vi", *c), A.add)
-        tt(x(0), h("TB", *f), ns, A.subtract)
-        scan(vb(1), h("ky", *c), h("ky", *c), -1.0, A.max, A.max)
-        tt(x(1), h("JN", *f), ns, A.subtract)
-        tt(h("dd", *c), vb(1), h("ky", *c), A.subtract)
-        ts(x(0), x(0), ZC * SC, A.min)
-        tt(h("GG", *c), h("Sx", *c), h("dd", *c), A.subtract)
-        tt(x(2), x(0), x(1), A.max)
-        scan(h("DR", *c), h("dd", *c), h("GG", *c), 0.0, A.min, A.max)
-        tt(h("XS", *f), h("DR", c[0] + 15, c[1], 16), x(2), A.max)
-        ts(h("ov", *f), h("XS", *f), 1.0 / SC, A.mult)
-        cp(h("F%d" % t, *c), ind(h("V", 0, VW), h("ov", *f)))
+    def keys(t):
+        ts(h("MV"), h("RB", 0, 128), col(AT0 + t % 2), A.subtract, 15.5, A.is_gt)
+        act(h("RO", 0, 128), h("RA", 0, 128))
+        act(h("RO", 128, 256), h("RA", 128, 256))
+        k, p = h("KB", 0, 144), h("PT", 0, 144)
+        mm(k, [(h("MV"), h("RA1"))], False, False)
+        mm(k, [(h("RO", 0, 128), h("SP"))], False, True)
+        mm(p, [(h("RO", 128, 256), h("SPs"))], False, True)
+        scan(h("mk"), h("RSK"), k, 0.0, A.min, A.max)
+        tt(h("dd"), h("mk"), k, A.subtract)
+        tt(h("GG"), p, h("dd"), A.subtract)
+        scan(h("DR"), h("dd"), h("GG"), 0.0, A.min, A.max)
+        lo = kept(t - 1)
+        ts(h("ov"), h("DR", 17, 144, 18), 1.0 / SC, A.mult, -float(lo), A.add)
+        for hh in (1, 0):
+            c = half(hh)
+            f = h("V", kept(t) + c[0], kept(t) + c[1])
+            ts(f, ind(h("V", lo, merged(max(t - 2, -1)) + 128), h("ov", *four(hh))), MARK + 4095, A.bitwise_and)
+            ts(h("F16", *c), f, float(ZC), A.min)
 
-    def dgather(t, hh, n):
-        a = 32 * n
-        act(h("D%d" % hh, 16 * a, 16 * a + 512), ind(h("X", 0, 4112), h("F%d" % t, 64 * hh + a, 64 * hh + a + 32)), AF.Copy)
+    def books(t):
+        mv, p, n = h("MV"), h("P%d" % (t % 2)), h("N%d" % (t % 2))
+        p2, n2 = h("P%d" % ((t + 1) % 2)), h("N%d" % ((t + 1) % 2))
+        mm(h("M1", 0, 128), [(h("blx"), mv), (h("blb"), p)])
+        ts(p2, h("M1", 0, 128), -1.0, A.is_equal)
+        mm(h("M2", 0, 128), [(h("IDb"), n), (h("blb"), p2)])
+        act(n2, h("M2", 0, 128), bias=1.0, scale=-1.0)
+        mm(h("M1", 128, 144), [(h("ID"), h("CB")), (n2, h("RH"))])
+        ts(h("og"), h("M1", 136, 144), 1.0, A.mult)
+        if t == NSTEP - 1:
+            return
+        mm(h("M2", 128, 256), [(h("blb"), mv), (h("blb"), p)])
+        act(h("sg"), h("M2", 128, 256), AF.Sign, bias=-1.5, accum=col(ACC))
+        mm(h("M2", 256, 257), [(h("OF"), col(ACC))])
+        act(col(AP), h("M2", 256, 257), bias=512.0 - 15.5, scale=1.0 / 32)
+        act(col(T1), col(AP), bias=RND)
+        act(col(T2), col(T1), bias=RND + 8192.0 * (t + 1), scale=-1.0)
+        act(col(AT0 + (t + 1) % 2), col(AP), bias=col(T2))
+        act(col(AK0 + (t + 1) % 2), col(AP), bias=col(K37))
+        if t >= 1:
+            act(h("VC", 17, 144, 18), h("VC", 17, 144, 18), bias=256 * SC)
 
-    def extremes(hh):
-        for a, b in ((0, 512), (512, 1024)):
-            scan(h("mx", a, b), h("RSM", a, b), h("D%d" % hh, a, b), 0.0, A.min, A.max)
-            scan(h("mn", a, b), h("RSN", a, b), h("D%d" % hh, a, b), 255.0, A.max, A.min)
+    def dgather(q, a, b):
+        o, x = h("D", 16 * a, 16 * b), ind(h("X", 0, 4112), h("F16", a, b))
+        if q == "s":
+            act(o, x, bias=-0.125, scale=0.5)
+        else:
+            ts(o, x, 0.5, A.mult, -0.125, A.add)
+
+    def extremes(a, b):
+        n, lo = 16 * (b - a), 16 * (a % 64)
+        scan(h("mx", lo, lo + n), h("RSM", 0, n), h("D", 16 * a, 16 * b), 0.0, A.min, A.max)
+        scan(h("mn", lo, lo + n), h("RSN", 0, n), h("D", 16 * a, 16 * b), 0.0, A.max, A.min)
+
+    def u_start(t, hh):
+        mm(h("Uo" if hh else "Ue", 0, 64), [(h("IDb"), h("MQ20")), (h("WBn"), h("Z%d" % (t % 2), *half(hh)))], True, False)
 
     def y_of(t, hh):
-        c = half(hh)
-        tt(h("ym", *c), h("mx", 15, 1024, 16), h("mn", 15, 1024, 16), A.add)
-        ts(h("yi", *c), h("ym", *c), 1, A.arith_shift_right)
-        tt(h("dz", *c), h("yi", *c), h("Z%d" % (t % 2), *c), A.subtract)
-        zn = h("Z%d" % ((t + 1) % 2), *c)
-        act(zn, h("dz", *c), AF.Abs)
-        cp(h("msg", 72 * t, 72 * t + 64) if hh else h("yE%d" % (t % 2)), h("yi", *c))
-        mms(h("Uo" if hh else "Ue", 0, 64), [(h("WB"), zn)])
-
-    def place(t, hh):
         c, f = half(hh), four(hh)
-        fi = lambda n: h("fi", 4 * n, 4 * n + 4)
-        tt(h("um", *c), h("Uo" if hh else "Ue", 0, 64), h("MQ", 0, 64), A.mult)
-        scan(h("us", *c), h("RS1", 0, 64), h("um", *c), 0.0, A.mult, A.add)
-        cp(fi(2 * hh), h("us", c[0] + 15, c[1], 16))
-        ts(fi(2 * hh + 1), fi(2 * hh), 31, A.bitwise_and)
+        z, u = h("Z%d" % (t % 2), *c), h("Uo" if hh else "Ue", 0, 64)
+        y = h("msg", 72 * t, 72 * t + 64) if hh else h("yE%d" % (t % 2))
+        tt(h("yi", *c), h("mx", 15, 1024, 16), h("mn", 15, 1024, 16), A.add)
+        tt(h("ymx", *c), h("yi", *c), z, A.max)
+        cp(y, h("yi", *c))
+        mm(u, [(h("WB2"), h("ymx", *c)), (h("WBn"), y)], False, True)
+        scan(h("us", *c), h("RSU"), u, 0.0, A.min, A.max)
+        cp(h("fi", *f), h("us", c[0] + 15, c[1], 16))
+        ts(h("fi", f[0] + 8, f[1] + 8), h("fi", *f), 31, A.bitwise_and)
         if hh:
-            tt(h("msg", 72 * t + 64, 72 * t + 68), fi(3), h("HX", *f), A.add)
+            tt(h("msg", 72 * t + 64, 72 * t + 68), h("fi", 8, 12), h("M1", 128, 132), A.add)
         else:
-            tt(h("fs", 36, 40), fi(1), h("fs", 32, 36), A.add)
-            cp(h("L%d" % (t % 2), *f), h("fs", 36, 40))
+            tt(h("f16", 4, 8), h("fi", 12, 16), h("M1", 132, 136), A.add)
+            cp(h("L%d" % (t % 2), 4, 8), h("f16", 4, 8))
+        cp(h("si", *c), u)
+        zp = h("M2", 320 + c[0], 320 + c[1])
+        mm(zp, [(h("ID2"), h("ymx", *c)), (h("IDn"), y), (h("IDn"), z)])
+        act(h("Z%d" % ((t + 1) % 2), *c), zp)
 
     def write_half(t, hh, y):
         c = half(hh)
@@ -458,141 +545,77 @@ def rank_program(g, core, T, topo):
         if t == NSTEP - 1:
             cp(ind(win, lst), y)
             return
-        act(h("qx", *c), ind(win, lst), AF.Copy)
+        act(h("qx", *c), ind(win, lst))
         tt(h("qm", *c), ind(win, lst), y, A.max)
-        pq = h("PQs", *c)
-        mms(pq, [(h("WpY"), y), (h("WpX"), h("qx", *c)), (h("WpM"), h("qm", *c))])
+        pq = h("M2", 448, 512)
+        mm(pq, [(h("L3", 0, 128, 1, 1), h("JR", 0, 64, 1, 1)), (WY, y), (WX, h("qx", *c)), (WM, h("qm", *c))])
         cp(ind(win, lst), y)
-        act(h("Qn", *c), pq, AF.Identity, -255.0)
+        act(h("Qn", *c), pq, bias=h("QB", 2 * t + hh, 2 * t + hh + 1))
         cp(ind(h("Q", 0, WIN), lst), h("Qn", *c))
 
-    x8 = lambda n: h("tg", 8 * n, 8 * n + 8)
-
-    def books1(t):
-        ts(h("HX"), h("XS"), ZC * SC, A.is_equal, float(TR), A.mult)
-        if t < NSTEP - 1:
-            tt(h("BO"), h("NS", 15, 128, 16), h("TB"), A.is_ge)
-            ts(h("HAS"), h("XS"), ZC * SC, A.not_equal)
-            mms(h("P7", 0, 8), [(h("ONE"), h("BO"))])
-
-    def books2(t):
-        ak = AK1 if t % 2 == 0 else AK0
-        run("v", lambda: V.tensor_reduce(ap(col(A1)), ap(h("P7", 0, 8)), AX.X, A.add), col(A1), [h("P7", 0, 8)], 64 * CY)
-        ts(x8(0), h("TB"), 5.0e5, A.is_lt)
-        cp(h("fi", 0, 1), col(A1))
-        tt(x8(1), x8(0), h("HAS"), A.subtract)
-        ts(h("fi", 0, 1), h("fi", 0, 1), 31, A.bitwise_and)
-        cp(h("WX", 0, 128, 16), x8(1))
-        ts(col(CA), h("fi", 0, 1), -4096.0, A.mult)
-        ts(x8(2), x8(1), -4096.0, A.mult, 8192.0, A.add)
-        ts(h("THC"), h("THB"), col(CA), A.add, -4096.0 * 2041 - 2040, A.max)
-        scan(h("VB", 256, 384), h("RS1"), h("WX"), 0.0, A.mult, A.add)
-        ts(x8(3), h("HAS"), 1.0e6, A.mult)
-        tt(h("JN"), h("JS"), h("HAS"), A.subtract)
-        tt(h("VB", 0, 128), h("MV"), h("VB", 256, 384), A.mult)
-        tt(h("TB"), x8(2), x8(3), A.add)
-        tt(col(ak), col(A1), col(K37), A.add)
-        tt(h("VB", 384, 512), h("VB", 0, 128), h("Kc"), A.add)
-
     def new_lists(t):
-        ff = h("VB", 256, 384)
-        cp(h("si", 0, 64), h("Ue", 0, 64))
-        cp(h("si", 64, 128), h("Uo", 0, 64))
-        tt(h("tf", 0, 8), h("HX"), h("JZ"), A.add)
-        cp(ff, h("F%d" % t))
+        f, fp, fa = h("V", kept(t), kept(t) + 128), h("M1", 256, 384), h("M1", 384, 512)
+        m = merged(t)
+        ts(fp, f, float(ZC), A.min)
+        ts(fa, f, float(ZC), A.min, col(AK0 + t % 2), A.add)
         ts(h("si"), h("si"), 4095, A.bitwise_and)
-        ts(h("oz"), h("tf", 0, 8), 1.0 / 64, A.mult)
-        tt(h("sj"), h("si"), ff, A.mult)
+        tt(h("sj"), h("si"), fp, A.mult)
         ts(h("sj"), h("sj"), 5, A.logical_shift_right)
-        tt(h("si"), h("sj"), ff, A.add)
-        ts(h("si"), h("si"), col(AK0 if t % 2 == 0 else AK1), A.add)
-        ts(h("sj"), h("si"), 4095, A.bitwise_and)
-        cp(ind(h("V", SB, SB + 256), h("oz")), h("sj"))
+        tt(h("V", m - 128, m), h("sj"), fa, A.add)
+        ts(h("V", m, m + 128), ind(h("V", m - 256, m), h("og")), 4095, A.bitwise_and)
+        if t < NSTEP - 2:
+            cp(h("S%d" % ((t + 1) % 2)), ind(h("V", m, m + 128), h("PL")))
 
     cores = T.cores
-    start_z(1)
-    start_t(1)
+    constants()
+    starts(0)
     for t in range(NSTEP):
         last = t == NSTEP - 1
-        fresh = 1 <= t < NSTEP - 1
-        gathers(1)
-        if t == 0:
-            ts(h("V", 0, 2048), h("vwb"), 4095, A.bitwise_and)
-            ts(h("V", 2048, 4096), h("vwb"), 12, A.logical_shift_right)
-            refresh_zx("Z0", 0)
-            start_z(0)
-            start_t(0)
-        gathers(0)
-        sums(t, 1)
-        sums(t, 0)
-        if fresh:
-            refresh_zx("Z%d" % (t % 2), 1)
-        p = (t - 1) % 2
-        if t == 0:
-            constants()
-        else:
-            cp(ind(h("V", 0, WIN), h("L%d" % p, 0, 4)), h("F%d" % (t - 1), 0, 64))
-            cp(ind(h("V", 0, WIN), h("L%d" % p, 4, 8)), h("rxf", 64 * t - 64, 64 * t))
-        keys(t, 1)
-        dst = cores[(rank + 1 + t % 3) % len(cores)]
-        if not last:
-            send(h("rxf", 64 * t, 64 * t + 64), h("F%d" % t, 64, 128), "rf%d" % t, dst)
-        dgather(t, 1, 0)
-        dgather(t, 1, 1)
-        keys(t, 0)
-        dgather(t, 0, 0)
+        first(t)
         if t == 0:
             constants2()
-        extremes(1)
+        if 1 <= t < NSTEP - 1:
+            spread("Z%d" % (t % 2), "zx%d" % (t % 2), ZG)
+        u_start(t, 1)
+        u_start(t, 0)
+        keys(t)
+        books(t)
+        dgather("s", 16, 40)
+        dgather("v", 0, 16)
+        dgather("s", 40, 64)
+        for a in (64, 96):
+            dgather("s", a, a + 32)
+        extremes(0, 16)
+        extremes(16, 40)
+        extremes(40, 64)
         y_of(t, 1)
-        dgather(t, 0, 1)
-        books1(t)
-        if fresh:
-            refresh_zx("Z%d" % (t % 2), 0)
-        if not last:
-            start_z(1)
-        tt(h("fs", 32, 36), h("HX", 0, 4), h("BASE", 0, 4), A.add)
-        place(t, 1)
+        dst = cores[(rank + 1 + t % 3) % len(cores)]
         send(h("rxy", 72 * t, 72 * t + 68), h("msg", 72 * t, 72 * t + 68), "ry%d" % t, dst)
-        if fresh:
-            relocate_vector()
-            relocate_tensor()
-            cp(ind(h("Q", 0, WIN), h("L%d" % p)), h("QR"))
-        extremes(0)
+        if not last:
+            send(h("V", kept(t) + 128, kept(t) + 192), h("V", kept(t), kept(t) + 64), "rf%d" % t, dst, "ry%d" % t)
+            starts(t + 1)
+        extremes(64, 96)
+        extremes(96, 128)
         y_of(t, 0)
-        if not last:
-            books2(t)
-        place(t, 0)
-        yE = h("yE%d" % (t % 2))
-        write_half(t, 0, yE)
-        if not last:
-            start_z(0)
-            start_t(1)
-            start_t(0)
+        write_half(t, 0, h("yE%d" % (t % 2)))
         new_lists(t)
-        if fresh:
-            relocate_list()
         if last:
-            cp(h("so", 0, 128, 2), h("V", SB, SB + 64))
-            cp(h("so", 1, 128, 2), h("V", SB + 64, SB + 128))
+            m = merged(t)
+            cp(h("so", 1, 128, 2), h("V", m, m + 64))
+            cp(h("so", 0, 128, 2), h("V", m + 64, m + 128))
             dma("y", "dys", T.ys[:, :], ap(h("so")), None, h("so"))
             zf = "Z%d" % (NSTEP % 2)
-            act(h("zo", 0, 128, 2), h(zf, 0, 64), AF.Copy)
-            act(h("zo", 1, 128, 2), h(zf, 64, 128), AF.Copy)
+            act(h("zo", 1, 128, 2), h(zf, 0, 64))
+            act(h("zo", 0, 128, 2), h(zf, 64, 128))
             dma("y", "dyz", T.yz[:, :], ap(h("zo")), None, h("zo"))
         src = cores[(rank - 1 - t % 3) % len(cores)]
         landed = len(topo.engines(src, core)[:ENG])
-        if not last:
-            recv(h("rxf", 64 * t, 64 * t + 64), "rf%d" % t, landed)
         recv(h("rxy", 72 * t, 72 * t + 68), "ry%d" % t, landed)
-        rx = h("rxy", 72 * t, 72 * t + 64)
-        tt(h("fs", 40, 44), h("rxy", 72 * t + 64, 72 * t + 68), h("BASE", 4, 8), A.add)
-        cp(h("L%d" % (t % 2), 4, 8), h("fs", 40, 44))
-        write_half(t, 1, rx)
-        if t < NSTEP - 2:
-            mms(h("P7", 128, 192), [(h("WpR"), yE)])
-            mms(h("P7", 192, 256), [(h("WpR"), rx)])
-            act(h("QR"), h("P7", 128, 256), AF.Identity, -255.0)
+        if not last:
+            recv(h("V", kept(t) + 128, kept(t) + 192), "rf%d" % t, landed)
+        tt(h("f16", 8, 12), h("rxy", 72 * t + 64, 72 * t + 68), h("f16", 0, 4), A.add)
+        cp(h("L%d" % (t % 2), 0, 4), h("f16", 8, 12))
+        write_half(t, 1, h("rxy", 72 * t, 72 * t + 64))
     dma("y", "dyx", T.yx[:, :], ap(h("X", 0, 4096)), None, h("X", 0, 4096))
     schedule()
     for s in sorted(total):

@@ -4,7 +4,7 @@ BF, F32, I32, U16, F16 = "bfloat16", "float32", "int32", "uint16", "float16"
 NSTEP = 6
 ZC = 4096
 TR = 8192
-WIN = 12288
+WIN = 12304
 HW = 192
 VB = HW * NSTEP
 ZV = VB + 4096
@@ -12,27 +12,35 @@ LA = ZV + 8
 MARK = 1 << 24
 SC = 2.0 ** -17
 RND = 1.5 * 2.0 ** 28
-CY = 0.83e-3 * 1.25
-WAKE = 0.1
-ROUNDS = 2
+CY = 0.83e-3 * 1.1
+WAKE = 0.18
+ROUNDS = 10
+JITTER = 0.2
+RANKS = ["C1", "T1", "R1", "T0", "K1", "C0", "R0", "D1", "Y1", "K0", "D0", "Y0"]
 ENG = 8
-PIECES = (0, 2, 6, 10, 14, 16)
+PC = ((0, 2, 4, 6, 8), (0, 3, 6, 8))
+PT = ((0, 2, 4, 6, 8), (0, 3, 6, 8))
+CLEAN = 1
+DG = ((("s", 80, 104), ("v", 64, 80), ("s", 104, 128)), (("v", 0, 16), ("s", 16, 32), ("s", 32, 48), ("s", 48, 64)))
+XCUT = (0, 512, 1024, 2048, 3072, 4096)
 ZG = 15
 
 SCRATCH = {"X": ("sbuf", [128, WIN], BF), "Q": ("sbuf", [128, WIN], F32), "V": ("sbuf", [128, LA + 128 + 256 * NSTEP], I32)}
 for _w, _d, _names in (
-        (1, I32, "wb thb"), (8, I32, "p8"), (8, U16, "ov og PL L0 L1"), (8, BF, "W2"), (16, F16, "WQa"), (8, F16, "WQb"), (16, F32, "CB QB f16"), (16, BF, "RH"), (16, I32, "fi i16"),
-        (32, F32, "cols"), (64, F32, "RSU"), (64, BF, "yE0 yE1 MQ20 JR"), (256, BF, "ZR"), (512, BF, "WZ d0 RSM RSN"),
-        (128, I32, "scb wmb si sj yi"), (128, BF, "zb Z0 Z1 WB2 WBn IDb ID2 IDn IDm blb blx MV P0 P1 N0 N1 ymx qm qx zo wmf wj GI L3 sg"), (128, U16, "S0 S1 F16"), (128, F16, "MQh THr"),
-        (128, F32, "OF blk ID MQ NQ us so Qn tf"), (256, F32, "RO"), (144, F32, "SP SPs VC RSK mk dd GG DR O144"), (144, BF, "RA1 RB1 RC1 KC"),
-        (NSTEP * 72, BF, "msg rxy"), (2048, BF, "T zx0 zx1"), (2048, F16, "C D"), (1024, F16, "mx mn")):
+        (1, I32, "wb thb"), (8, I32, "p8"), (8, U16, "ov og PL L0 L1"), (8, BF, "W2"), (24, F16, "WQ"), (192, F16, "THr"), (16, F32, "CB QB f16"), (16, BF, "RH"), (16, I32, "fi i16"),
+        (32, F32, "cols"), (64, F32, "RSU"), (64, BF, "MQ20 JR"), (64, F16, "yE0 yE1"), (512, BF, "WZ d0 RSM RSN"),
+        (128, I32, "scb wmb si sj yi us"), (128, BF, "zb Z0 Z1 WB2 WBn IDb ID2 IDn IDm blb blh blx ymx qm qx zo wmf wj GI L3 sg"), (128, U16, "S0 S1 F16"),
+        (128, F16, "MQh WY IDh WBh"), (1280, BF, "ST"), (4, F32, "BK4"),
+        (128, F32, "OF blk ID MQ NQ so Qn tf"), (512, F32, "RO"), (72, F32, "SP SPs RSK"), (144, F32, "VC mk dd GG DR O144"), (72, BF, "RA1 RB1 RC1 KC"),
+        (NSTEP * 72, F16, "msg rxy"), (2048, BF, "T zx0 zx1"), (2048, F16, "C D mx mn")):
     for _n in _names.split():
         SCRATCH[_n] = ("sbuf", [128, _w], _d)
-PSUM = ("RA", "RB", "KB", "PT", "Uo", "Ue", "M1", "M2")
+PSUM = ("Ro", "Re", "KB", "PT", "Uo", "Ue", "M1", "M2")
 for _n in PSUM:
     SCRATCH[_n] = ("psum", [128, 512], F32)
-LOADS = ["scb", "zb", "wb", "thb", "wmb", "vw", "X0", "X1", "X2", "X3"]
+LOADS = ["scb", "zb", "wb", "thb", "wmb", "vw"] + ["X%d" % n for n in range(len(XCUT) - 1)]
 SEMAPHORES = ["sv", "ss", "sp", "sg", "ls", "dyx", "dys", "dyz"] + ["d" + n for n in LOADS] + ["ry%d" % t for t in range(NSTEP)] + ["rf%d" % t for t in range(NSTEP - 1)]
+ORDER = []
 
 
 def rank_program(g, core, T, topo):
@@ -44,11 +52,12 @@ def rank_program(g, core, T, topo):
     total = {}
     know = {q: {} for q in queues}
     ops = []
+    ranks = []
     adds = set()
     hist = {}
 
-    def h(name, lo=0, hi=None, step=1, rows=None):
-        return (name, lo, T[name].shape[1] if hi is None else hi, step, rows)
+    def h(name, lo=0, hi=None, step=1, rows=128):
+        return (name, lo, T[name].shape[1] if hi is None else hi, step, rows if isinstance(rows, tuple) else (0, rows))
 
     def ind(win, off):
         return ("ind", win, off)
@@ -57,18 +66,20 @@ def rank_program(g, core, T, topo):
         if x[0] == "ind":
             return ap(x[1]).indirect(ap(x[2]))
         t = T[x[0]]
-        if x[4]:
-            return t[0:x[4], x[1]:x[2]] if x[3] == 1 else t[0:x[4], x[1]:x[2]:x[3]]
-        return t[:, x[1]:x[2]] if x[3] == 1 else t[:, x[1]:x[2]:x[3]]
+        p, q = x[4]
+        return t[p:q, x[1]:x[2]] if x[3] == 1 else t[p:q, x[1]:x[2]:x[3]]
 
     def regions(x):
         return [x[1], x[2]] if x[0] == "ind" else [x]
 
     def apart(a, b):
-        return a[1] >= b[2] or a[2] <= b[1] or (a[3] == b[3] > 1 and (a[1] - b[1]) % a[3] != 0)
+        return a[1] >= b[2] or a[2] <= b[1] or (a[3] == b[3] > 1 and (a[1] - b[1]) % a[3] != 0) or a[4][0] >= b[4][1] or a[4][1] <= b[4][0]
 
     def covers(a, b):
-        return a[1] <= b[1] and b[2] <= a[2] and (a[3] == 1 or (a[3] == b[3] and (a[1] - b[1]) % a[3] == 0))
+        return a[1] <= b[1] and b[2] <= a[2] and (a[3] == 1 or (a[3] == b[3] and (a[1] - b[1]) % a[3] == 0)) and a[4][0] <= b[4][0] and b[4][1] <= a[4][1]
+
+    def flag(name):
+        return (name, 0, 1, 1, (0, 128))
 
     def wait(q, tok, clock):
         if know[q].get(tok[0], 0) >= tok[1]:
@@ -149,25 +160,36 @@ def rank_program(g, core, T, topo):
                 while was < st:
                     was = st
                     for r in holds[i]:
-                        for a, b, who in used.setdefault(r, []):
-                            m = 0.0 if who == q else WAKE
-                            if a - m < st + us and st < b + m and (r == q or who != q):
-                                st = b + m
+                        for slot in range(int(was - 1.0), int(was + us + 1.0) + 1):
+                            for a, b, who in used.get((r, slot), ()):
+                                m = 0.0 if who == q else WAKE
+                                if a - m < st + us and st < b + m and (r == q or who != q):
+                                    st = b + m
                 end[i] = st + us
                 for r in holds[i]:
-                    used[r].append((st, end[i], q))
+                    for slot in range(int(st), int(end[i]) + 1):
+                        used.setdefault((r, slot), []).append((st, end[i], q))
                 for j in after[i]:
                     left[j] -= 1
                     if not left[j]:
                         cand.append(j)
             return end
-        best = end = place(list(range(n)), pred, succ, False)
+        key = [1000] * n
+        for a, r in ranks:
+            key[a:] = [r] * (n - a)
+        for i in range(n - 1, -1, -1):
+            key[i] = min([key[i]] + [key[j] for j in succ[i]])
+        best = end = place(key, pred, succ, False)
+        seed = 1
         for _ in range(ROUNDS):
-            end = place([-e for e in place([-e for e in end], succ, pred, True)], pred, succ, False)
-            if max(end) < max(best):
+            key = []
+            for e in best:
+                seed = seed * 48271 % 2147483647
+                key.append(-e + JITTER * seed / 2147483647)
+            end = place([-e for e in place(key, succ, pred, True)], pred, succ, False)
+            if max(end) <= max(best):
                 best = end
-        for i in sorted(range(n), key=lambda c: (best[c] - ops[c][4], c)):
-            ops[i][1]()
+        ORDER.extend(sorted(range(n), key=lambda c: (best[c] - ops[c][4], c)))
 
     def elems(x):
         return 16 * (x[2][2] - x[2][1]) if x[0] == "ind" else -(-(x[2] - x[1]) // x[3])
@@ -229,8 +251,8 @@ def rank_program(g, core, T, topo):
         small = SCRATCH[o[0]][2] != I32
         run("g", lambda: g.iota(ap(o), pattern, base, cm, allow_small_or_imprecise_dtypes=small), o, [], 0.13 + 2 * elems(o) * CY)
 
-    def keep(o, x, pattern, op, base, cm):
-        run("g", lambda: g.affine_select(ap(o), ap(x), pattern, op, 0.0, base, cm), o, [x], 0.17 + 2 * elems(o) * CY)
+    def keep(o, x, pattern, op, base, cm, other=0.0):
+        run("g", lambda: g.affine_select(ap(o), ap(x), pattern, op, other, base, cm), o, [x], 0.17 + 2 * elems(o) * CY)
 
     def mms(items, start=True, stop=True, after=(), mark=()):
         reads = [x for p in items for x in p[1:]] + list(mark)
@@ -270,36 +292,29 @@ def rank_program(g, core, T, topo):
             need("g", [in_], [])
             g.remote_dma(ap(out), ap(in_), T.sem[remote], T.sem["ls"], pid, rid, m)
             bump("ls", len(eng))
-        ops.append(("g", emit, [in_] + ([("@" + after, 0, 1, 1)] if after else []), [("@" + remote, 0, 1, 1)], 0.8, 0.0, "g"))
+        ops.append(("g", emit, [in_] + ([flag("@" + after)] if after else []), [flag("@" + remote)], 0.8, 0.0, "g"))
 
     def recv(out, sem, n):
         def emit():
             hist.setdefault(out[0], []).append((out, True, "remote", bump(sem, n), {sem: n}))
-        ops.append(("remote" + sem, emit, [("@" + sem, 0, 1, 1)], [out], 2.5, 0.0, "remote"))
+        ops.append(("remote" + sem, emit, [flag("@" + sem)], [out], 2.7, 0.0, "remote"))
 
-    def chain(name):
-        o = ops[-1]
-        ops[-1] = o[:3] + (o[3] + [(name, 0, 1, 1)],) + o[4:]
+    def rank_as(t, name):
+        ranks.append((len(ops), len(RANKS) * t + RANKS.index(name) if name != "fill" else 1000))
 
-    def load_x(n):
-        dma("y", "dX%d" % n, ap(h("X", 1024 * n, 1024 * n + 1024)), T.reg[:, 1024 * n:1024 * n + 1024], h("X", 1024 * n, 1024 * n + 1024), lat=0.0)
-        ops[-1] = ops[-1][:4] + (0.9, 1.6) + ops[-1][6:]
-    for b, t in (("zb", T.z0), ("scb", T.scan), ("thb", T.th), ("wb", T.wt)):
-        dma("y", "d" + b, ap(h(b)), t[:, :], h(b))
-    dma("s", "dwmb", T["wmb"][0:8, :], T.warm[:, :], h("wmb"))
-    for n in range(4):
-        load_x(n)
-    dma("y", "dvw", ap(h("V", VB, VB + 2048)), T.vw[:, :], h("V", VB, VB + 2048), lat=5.0)
+    for n, (a, b) in enumerate(zip(XCUT, XCUT[1:])):
+        dma("y", "dX%d" % n, ap(h("X", a, b)), T.reg[:, a:b], h("X", a, b), lat=2.0 + 0.3 * n + b * 0.85e-3)
+    dma("y", "dvw", ap(h("V", VB, VB + 2048)), T.vw[:, :], h("V", VB, VB + 2048), lat=10.2)
+    for n, (b, t) in enumerate((("zb", T.z0), ("scb", T.scan), ("thb", T.th), ("wb", T.wt))):
+        dma("s", "d" + b, ap(h(b)), t[:, :], h(b), lat=2.4 + n)
+        if n == 1:
+            dma("s", "dwmb", T["wmb"][0:8, :], T.warm[:, :], h("wmb"), lat=4.0)
     for o in ops:
         o[1]()
-    landing = {o[3][0][:3]: 2.0 for o in ops}
-    for n in range(4):
-        landing[("X", 1024 * n, 1024 * n + 1024)] = 2.8 + 0.9 * n
-    landing[("V", VB, VB + 2048)] = 9.0
-    ops[:] = [("load%d" % n, lambda: None, [], o[3], landing[o[3][0][:3]], 0.0, o[6]) for n, o in enumerate(ops)]
+    ops[:] = [("load%d" % n, lambda: None, [], o[3], o[5], 0.0, o[6]) for n, o in enumerate(ops)]
 
     col = lambda c: h("cols", c, c + 1)
-    QC, M0, M1, M2, M3, QBIAS, D0C, THN, WC, WN, K37, AK0, AK1, AT0, AT1, AP, T1, T2, ACC, C64 = range(20)
+    QC, M0, M1, M2, M3, QBIAS, D0C, THN, WC, WN, K37, AK0, AK1, AT0, AT1, AP, T1, T2, ACC, C64, CRX, AN = range(22)
     half = lambda hh: (0, 64) if hh else (64, 128)
     four = lambda hh: (0, 4) if hh else (4, 8)
     BK8 = h("blk", 0, 128, 16)
@@ -316,11 +331,11 @@ def rank_program(g, core, T, topo):
     ts(col(M1), col(QC), 1.0, A.is_equal)
     ts(col(M2), col(QC), 2.0, A.is_equal)
     ts(col(M3), col(QC), 3.0, A.is_equal)
-    ts(h("p8", 2, 3), h("p8", 0, 1), 7, A.bitwise_and)
-    ts(h("p8", 3, 4), h("p8", 0, 1), 3, A.logical_shift_right, 1, A.bitwise_and)
+    ts(h("p8", 2, 3), h("p8", 0, 1), 3, A.bitwise_and)
+    ts(h("p8", 3, 4), h("p8", 0, 1), 2, A.logical_shift_right, 3, A.bitwise_and)
     ts(col(T1), h("p8", 2, 3), 16.0, A.mult)
     tt(col(T1), col(T1), h("p8", 3, 4), A.add)
-    iota(h("i16", 0, 8), [[2, 8]], 0, 0)
+    iota(h("i16", 0, 8), [[64, 2], [4, 4]], 0, 0)
     ts(h("PL"), h("i16", 0, 8), col(T1), A.add)
     fill(h("WZ"), 0.0)
     WS, WY, WX, WM = [h("WZ", 128 * n, 128 * n + 128) for n in range(4)]
@@ -354,78 +369,101 @@ def rank_program(g, core, T, topo):
     tt(col(QBIAS), col(QBIAS), col(T2), A.add)
     act(h("W2"), BK8, scale=2.0)
     ts(col(T2), col(M2), -256.0, A.mult, col(M3), A.add)
-    ts(h("WQa", 0, 8), BK8, col(M0), A.mult, -1.0, A.mult)
-    ts(h("WQa", 8, 16), BK8, col(T2), A.mult)
+    ts(h("WQ", 0, 8), BK8, col(M0), A.mult, -1.0, A.mult)
+    ts(h("WQ", 8, 16), BK8, col(T2), A.mult)
     ts(col(T1), col(M2), 8192.0, A.mult, col(M1), A.add)
-    ts(h("WQb"), BK8, col(T1), A.mult)
+    ts(h("WQ", 16, 24), BK8, col(T1), A.mult)
     iota(h("NQ"), [[0, 8], [1, 16]], 0, 0)
     ts(h("MQ"), h("NQ"), col(QC), A.is_equal)
     act(h("MQh"), h("MQ"))
     ts(col(THN), h("thb"), -1.0, A.mult, 2040.0, A.add)
-    act(h("THr"), h("blk"), scale=col(THN))
+    act(h("THr", 0, 128), h("blk"), scale=0.0)
+    act(h("THr", 128, 192), h("blk", 0, 128, 2), scale=col(THN))
     keep(h("ID"), h("OF"), [[1, 128]], A.is_equal, 0, -1)
     act(h("IDb"), h("ID"))
     act(h("IDm"), h("ID"), scale=-16384.0)
     act(h("blb"), h("blk"))
-    fill(h("ZR"), 0.0)
-    fill(col(AT0), -15.5)
+    fill(col(AT0), -0.5)
     keep(h("GI", 0, 128, 1, 8), h("O144", 0, 128, 1, 8), [[1, 8], [0, 16]], A.is_equal, 0, -1)
     cp(h("wj", 0, 64, 1, 8), h("wmb", 1, 128, 2, 8))
     cp(h("wj", 64, 128, 1, 8), h("wmb", 0, 128, 2, 8))
     mm(h("M1", 0, 128), [(h("wj", 0, 128, 1, 8), h("GI", 0, 128, 1, 8))])
     tt(h("wmf"), h("M1", 0, 128), h("MQ"), A.mult)
-    mm(h("M2", 0, 128), [(h("blb"), h("wmf"))])
-    act(h("N0"), h("M2", 0, 128), bias=1.0, scale=-1.0)
-    fill(h("P0"), 0.0)
+    fill(h("ST"), 0.0)
+    fill(h("RO"), 0.0)
+    MV, P0, N0 = 0, 1, 3
+
+    def state(n, hh, b=None):
+        lo = 256 * n + (0 if hh else 128)
+        return h("ST", lo, lo + 128) if b is None else h("ST", lo + b, lo + 128, 2)
+
+    def unfold(name, lo, x, f=AF.Identity, bias=0.0, scale=1.0):
+        for b in (0, 1):
+            r = (64 * b, 64 * b + 64)
+            act(h(name, lo + b, lo + 128, 2, r), h(x[0], x[1], x[2], 1, r), f, h(bias[0], bias[1], bias[2], 1, r) if isinstance(bias, tuple) else bias, scale)
+    for hh in (1, 0):
+        r, lo = half(hh), half(hh)[0]
+        for b in (0, 1):
+            mm(h("M2", lo, lo + 64, 1, (64 * b, 64 * b + 64)), [(h("blb", r[0], r[1], 1, r), h("wmf", b, 128, 2, r))])
+        unfold("ST", state(N0, hh)[1], h("M2", lo, lo + 64), bias=1.0, scale=-1.0)
 
     def constants():
-        keep(h("SP"), h("O144"), [[16, 8], [1, 18]], A.is_equal, 0, -1)
+        for b in (0, 1):
+            r = (64 * b, 64 * b + 64)
+            keep(h("SP"), h("SP" if b else "RO", 0, 72), [[16, 4], [1, 18]], A.not_equal, 64 * b, -1, 1.0)
+            act(h("BK4", 0, 4, 1, r), h("blk", r[0], r[1], 16, r))
+        BK4 = h("BK4")
         iota(h("mk"), [[0, 8], [1, 18]], 0, 0)
-        fill(h("SP", 16, 144, 18), 0.0)
-        fill(h("SP", 17, 144, 18), 0.0)
+        fill(h("SP", 16, 72, 18), 0.0)
+        fill(h("SP", 17, 72, 18), 0.0)
         act(h("SPs"), h("SP"), scale=SC)
-        act(h("RA1"), h("SP"), scale=4096.0)
+        act(h("RA1"), h("SP"), scale=2048.0)
         act(h("RB1"), h("SP"), scale=4096.0)
         act(h("RC1"), h("SP"), scale=0.0)
-        act(h("RA1", 16, 144, 18), BK8, scale=-32768.0)
-        act(h("RA1", 17, 144, 18), BK8, scale=-65536.0)
-        act(h("RB1", 16, 144, 18), BK8, scale=-32768.0)
-        act(h("RC1", 17, 144, 18), BK8, scale=-4096.0)
-        act(h("KC"), h("mk"), bias=0.9375, scale=-0.0625)
-        act(h("KC", 16, 144, 18), BK8, bias=53248.0, scale=0.0)
-        act(h("KC", 17, 144, 18), BK8, bias=65536.0, scale=0.0)
-        act(h("RSK"), h("mk"), scale=1.0e7)
+        act(h("RA1", 16, 72, 18), BK4, scale=-16384.0)
+        act(h("RA1", 17, 72, 18), BK4, scale=-32768.0)
+        act(h("RB1", 16, 72, 18), BK4, scale=-32768.0)
+        act(h("RC1", 17, 72, 18), BK4, scale=-4096.0)
+        act(h("KC"), h("mk", 0, 72), bias=0.9375, scale=-0.0625)
+        act(h("KC", 16, 72, 18), BK4, bias=53248.0 - 16 * 16384, scale=0.0)
+        act(h("KC", 17, 72, 18), BK4, bias=65536.0 - 16 * 32768, scale=0.0)
+        act(h("RSK"), h("mk", 0, 72), scale=1.0e7)
         act(h("VC"), h("mk"), bias=3200.0 * SC, scale=0.0)
         act(h("VC", 16, 144, 18), BK8, bias=ZV * SC, scale=0.0)
         iota(h("i16", 8, 16), [[16, 8]], LA, 0)
         ts(h("VC", 17, 144, 18), h("i16", 8, 16), col(QC), A.add, SC, A.mult)
         fill(h("V", ZV, ZV + 8), MARK)
-        ts(h("V", VB + 2048, VB + 3072), h("V", VB, VB + 1024), 12, A.logical_shift_right)
-        ts(h("V", VB + 3072, VB + 4096), h("V", VB + 1024, VB + 2048), 12, A.logical_shift_right)
         iota(h("X", ZC, ZC + 16), [[0, 16]], 0, 0)
         iota(h("RSN"), [[0, 32], [-256, 16]], 255, 0)
 
     def constants2():
+        for n in range(VB, VB + 2048, 256):
+            ts(h("V", n + 2048, n + 2304), h("V", n, n + 256), 12, A.logical_shift_right)
+        act(h("WY"), WY)
+        act(h("IDh"), h("ID"), scale=-1.0)
         act(h("ID2"), h("ID"), scale=2.0)
         act(h("IDn"), h("ID"), scale=-1.0)
-        tt(h("blx"), h("blb"), h("ID2"), A.subtract)
+        act(h("blh"), h("blk"), scale=0.5)
+        tt(h("blx"), h("blh"), h("IDb"), A.subtract)
         ts(col(WC), h("wb"), 2.0, A.mult)
         ts(col(WN), h("wb"), -1.0, A.mult)
         act(h("WB2"), h("blk"), scale=col(WC))
         act(h("WBn"), h("blk"), scale=col(WN))
+        act(h("WBh"), h("blk"), scale=col(WN))
         act(h("MQ20"), h("MQ", 0, 64), scale=2.0 ** 20)
         act(h("RSU"), h("NQ", 0, 64), scale=1.0e7)
         act(col(K37), col(QC), bias=15.5, scale=37.0)
         act(col(AK0), col(QC), scale=37.0)
         act(col(C64), col(QC), scale=64.0)
-        act(h("RH", 0, 8), BK8, scale=-TR / 16.0)
-        act(h("RH", 8, 16), BK8, scale=8.0)
+        act(h("RH", 0, 4), h("BK4"), scale=-TR / 16.0)
+        act(h("RH", 4, 8), h("BK4"), scale=8.0)
+        act(h("RH", 8, 12), h("BK4"), scale=-TR / 16.0)
         iota(h("fi", 0, 4), [[1024, 4]], TR, 0)
         iota(h("fi", 8, 16), [[16, 8]], 0, 0)
-        fill(h("CB", 0, 4), float(TR))
-        ts(h("CB", 4, 8), h("fi", 0, 4), col(C64), A.add)
-        ts(h("CB", 8, 16), h("fi", 8, 16), col(QC), A.add)
-        ts(h("f16", 0, 4), h("CB", 4, 8), 32.0 - TR, A.add)
+        ts(h("CB", 0, 4), h("fi", 0, 4), -2048.0, A.add)
+        ts(h("CB", 12, 16), h("fi", 0, 4), col(C64), A.add)
+        ts(h("CB", 4, 12), h("fi", 8, 16), col(QC), A.add)
+        act(col(CRX), col(QC), bias=2048.0 + 32, scale=64.0)
         iota(h("JR", 0, 64, 1, 1), [[1, 64]], 0, 0)
         act(h("L3", 0, 128, 1, 1), h("NQ", 0, 128, 1, 1), scale=0.0)
         act(h("L3", 3, 128, 16, 1), h("O144", 0, 8, 1, 1))
@@ -435,69 +473,88 @@ def rank_program(g, core, T, topo):
         ts(h("so", 0, 10), h("si", 0, 10), col(M2), A.mult)
         tt(h("QB", 0, 10), h("QB", 0, 10), h("so", 0, 10), A.add)
         for n in range(8):
-            iota(h("X", TR + 512 * n, TR + 512 * n + 512), [[0, 512]], 0, 0)
+            iota(h("X", TR + 514 * n, TR + 514 * n + 514), [[0, 514]], 0, 0)
 
-    def starts(t):
-        n, p = h("N%d" % (t % 2)), h("P%d" % (t % 2))
-        mm(h("RA", 0, 256), [(h("IDb"), h("ZR"))], True, False)
-        mm(h("RB", 0, 128), [(h("MQh"), h("THr")), (h("IDm"), n)], True, False)
-        mm(h("KB", 0, 144), [(h("IDb"), h("KC")), (p, h("RB1")), (n, h("RC1"))], True, False)
-        mm(h("PT", 0, 144), [(h("ID"), h("VC"))], True, False)
+    bank = lambda hh: "Ro" if hh else "Re"
+    seg = lambda hh: (0, 72) if hh else (72, 144)
 
-    def first(t):
+    def start_sums(t, hh):
+        mms([(h(bank(hh), 0, 192), h("MQh"), h("THr"))] + [(h(bank(hh), 128, 192), h("IDm"), state(N0 + t % 2, hh, b)) for b in (0, 1)], True, False)
+
+    def start_keys(t, hh):
+        mm(h("KB", 0, 72), [(h("IDb"), h("KC")), (state(P0 + t % 2, hh), h("RB1")), (state(N0 + t % 2, hh), h("RC1"))], True, False)
+        mm(h("PT", 0, 72), [(h("ID"), h("VC", *seg(hh)))], True, False)
+
+    def first(t, hh):
         lst, zx = "S%d" % (max(t - 1, 0) % 2), "zx%d" % (max(t - 1, 0) % 2)
-        for a, b in zip(PIECES, PIECES[1:]):
-            l, lo, hi = h(lst, 8 * a, 8 * b), 128 * a, 128 * b
-            act(h("C", lo, hi), ind(h("Q", 0, 4096), l), bias=col(QBIAS))
-            chain("@c")
-            tt(h("T", lo, hi), ind(h("X", 0, 4096), l), h(zx, lo, hi), A.max)
-            chain("@t")
-        ra = [("@ra", 0, 1, 1)]
-        for a, b in zip(PIECES, PIECES[1:]):
-            mms([(h("RA", q, 128, 16), h("T", 128 * q, 128 * q + 128), h("W2")) for q in range(a, b)], False, False, (), ra)
-        for a, b in zip(PIECES, PIECES[1:]):
-            end = b == 16
-            mms([(h("RB", q, 128, 16), h("C", 128 * q, 128 * q + 128), h("WQb")) for q in range(a, b)], False, end, [("@rb", 0, 1, 1)])
-            mms([(h("RA", q, 256, 16), h("C", 128 * q, 128 * q + 128), h("WQa")) for q in range(a, b)], False, end, ra if end else (), () if end else ra)
+        o = half(hh)[0]
+        rank_as(t, "C%d" % hh)
+        for a, b in zip(PC[hh], PC[hh][1:]):
+            act(h("C", 16 * o + 128 * a, 16 * o + 128 * b), ind(h("Q", 0, 4096), h(lst, o + 8 * a, o + 8 * b)), bias=col(QBIAS))
+        rank_as(t, "T%d" % hh)
+        for a, b in zip(PT[hh], PT[hh][1:]):
+            lo, hi = 16 * o + 128 * a, 16 * o + 128 * b
+            tt(h("T", lo, hi), ind(h("X", 0, 4096), h(lst, o + 8 * a, o + 8 * b)), h(zx, lo, hi), A.max)
+        rank_as(t, "R%d" % hh)
+        ra = [flag("@r%d" % hh)]
+        part = lambda nm, q: h(nm, 16 * o + 128 * q, 16 * o + 128 * q + 128)
+        for a, b in zip(PT[hh], PT[hh][1:]):
+            mms([(h(bank(hh), q, 64, 8), part("T", q), h("W2")) for q in range(a, b)], False, False, (), ra)
+        for a, b in zip(PC[hh], PC[hh][1:]):
+            end = b == 8
+            mms([(h(bank(hh), q, 192, 8), part("C", q), h("WQ")) for q in range(a, b)], False, end, ra if end else (), () if end else ra)
 
-    def keys(t):
-        ts(h("MV"), h("RB", 0, 128), col(AT0 + t % 2), A.subtract, 15.5, A.is_gt)
-        act(h("RO", 0, 128), h("RA", 0, 128))
-        act(h("RO", 128, 256), h("RA", 128, 256))
-        k, p = h("KB", 0, 144), h("PT", 0, 144)
-        mm(k, [(h("MV"), h("RA1"))], False, False)
-        mm(k, [(h("RO", 0, 128), h("SP"))], False, True)
-        mm(p, [(h("RO", 128, 256), h("SPs"))], False, True)
-        scan(h("mk"), h("RSK"), k, 0.0, A.min, A.max)
-        tt(h("dd"), h("mk"), k, A.subtract)
-        tt(h("GG"), p, h("dd"), A.subtract)
-        scan(h("DR"), h("dd"), h("GG"), 0.0, A.min, A.max)
+    def keys(t, hh):
+        (a, b), c, ro = seg(hh), half(hh), 0 if hh else 256
+        rank_as(t, "R%d" % hh)
+        unfold("RO", ro, h(bank(hh), 0, 64), bias=2048.0)
+        unfold("ST", state(MV, hh)[1], h(bank(hh), 128, 192), AF.Sign, col(AT0 + t % 2))
+        unfold("RO", ro + 128, h(bank(hh), 64, 128))
+        k, p = h("KB", 0, 72), h("PT", 0, 72)
+        mm(k, [(h("RO", ro, ro + 128), h("SP"))], False, False)
+        mm(k, [(state(MV, hh), h("RA1"))], False, True)
+        mm(p, [(h("RO", ro + 128, ro + 256), h("SPs"))], False, True)
+        rank_as(t, "K%d" % hh)
+        scan(h("mk", a, b), h("RSK", 0, 72), k, 0.0, A.min, A.max)
+        tt(h("dd", a, b), h("mk", a, b), k, A.subtract)
+        tt(h("GG", a, b), p, h("dd", a, b), A.subtract)
+        scan(h("DR", a, b), h("dd", a, b), h("GG", a, b), 0.0, A.min, A.max)
         lo = kept(t - 1)
-        ts(h("ov"), h("DR", 17, 144, 18), 1.0 / SC, A.mult, -float(lo), A.add)
-        for hh in (1, 0):
-            c = half(hh)
-            f = h("V", kept(t) + c[0], kept(t) + c[1])
-            ts(f, ind(h("V", lo, merged(max(t - 2, -1)) + 128), h("ov", *four(hh))), MARK + 4095, A.bitwise_and)
+        ts(h("ov", *four(hh)), h("DR", a + 17, b, 18), 1.0 / SC, A.mult, -float(lo), A.add)
+        f = h("V", kept(t) + c[0], kept(t) + c[1])
+        view = ind(h("V", lo, merged(max(t - 2, -1)) + 128), h("ov", *four(hh)))
+        if t < CLEAN:
+            ts(f, view, MARK + 4095, A.bitwise_and)
             ts(h("F16", *c), f, float(ZC), A.min)
+        else:
+            cp(h("F16", *c), view)
+            rank_as(t, "fill")
+            cp(f, view)
 
-    def books(t):
-        mv, p, n = h("MV"), h("P%d" % (t % 2)), h("N%d" % (t % 2))
-        p2, n2 = h("P%d" % ((t + 1) % 2)), h("N%d" % ((t + 1) % 2))
-        mm(h("M1", 0, 128), [(h("blx"), mv), (h("blb"), p)])
-        ts(p2, h("M1", 0, 128), -1.0, A.is_equal)
-        mm(h("M2", 0, 128), [(h("IDb"), n), (h("blb"), p2)])
-        act(n2, h("M2", 0, 128), bias=1.0, scale=-1.0)
-        mm(h("M1", 128, 144), [(h("ID"), h("CB")), (n2, h("RH"))])
-        ts(h("og"), h("M1", 136, 144), 1.0, A.mult)
-        if t == NSTEP - 1:
-            return
-        mm(h("M2", 128, 256), [(h("blb"), mv), (h("blb"), p)])
-        act(h("sg"), h("M2", 128, 256), AF.Sign, bias=-1.5, accum=col(ACC))
+    both = lambda w, n, hh: [(h(w), state(n, hh, b)) for b in (0, 1)]
+
+    def books(t, hh):
+        p, n, p2, n2 = P0 + t % 2, N0 + t % 2, P0 + (t + 1) % 2, N0 + (t + 1) % 2
+        o, lo = half(hh)[0], four(hh)[0]
+        mm(h("M2", 128 + o, 192 + o), both("blx", MV, hh) + both("blb", p, hh))
+        unfold("ST", state(p2, hh)[1], h("M2", 128 + o, 192 + o), AF.Relu, -7.0, -1.0)
+        mm(h("M2", o, o + 64), both("IDb", n, hh) + both("blb", p2, hh))
+        unfold("ST", state(n2, hh)[1], h("M2", o, o + 64), bias=1.0, scale=-1.0)
+        mm(h("M1", 128 + 2 * lo, 136 + 2 * lo), [(h("ID"), h("CB", 2 * lo, 2 * lo + 8)), (state(n2, hh), h("RH", lo, lo + 8))])
+        if not hh:
+            ts(h("og"), h("M1", 132, 140), 1.0, A.mult)
+
+    def borrowers(t):
+        for hh in (1, 0):
+            o = half(hh)[0]
+            mm(h("M2", 128 + o, 192 + o), both("blh", MV, hh) + both("blb", P0 + t % 2, hh))
+        act(h("sg"), h("M2", 128, 256), AF.Sign, bias=6.5, accum=col(ACC))
         mm(h("M2", 256, 257), [(h("OF"), col(ACC))])
         act(col(AP), h("M2", 256, 257), bias=512.0 - 15.5, scale=1.0 / 32)
+        act(col(AN), h("M2", 256, 257), bias=-512.0 - 0.5, scale=-1.0 / 32)
         act(col(T1), col(AP), bias=RND)
-        act(col(T2), col(T1), bias=RND + 8192.0 * (t + 1), scale=-1.0)
-        act(col(AT0 + (t + 1) % 2), col(AP), bias=col(T2))
+        act(col(T2), col(T1), bias=-RND - 8192.0 * (t + 1))
+        act(col(AT0 + (t + 1) % 2), col(AN), bias=col(T2))
         act(col(AK0 + (t + 1) % 2), col(AP), bias=col(K37))
         if t >= 1:
             act(h("VC", 17, 144, 18), h("VC", 17, 144, 18), bias=256 * SC)
@@ -510,7 +567,7 @@ def rank_program(g, core, T, topo):
             ts(o, x, 0.5, A.mult, -0.125, A.add)
 
     def extremes(a, b):
-        n, lo = 16 * (b - a), 16 * (a % 64)
+        n, lo = 16 * (b - a), 16 * a
         scan(h("mx", lo, lo + n), h("RSM", 0, n), h("D", 16 * a, 16 * b), 0.0, A.min, A.max)
         scan(h("mn", lo, lo + n), h("RSN", 0, n), h("D", 16 * a, 16 * b), 0.0, A.max, A.min)
 
@@ -521,21 +578,20 @@ def rank_program(g, core, T, topo):
         c, f = half(hh), four(hh)
         z, u = h("Z%d" % (t % 2), *c), h("Uo" if hh else "Ue", 0, 64)
         y = h("msg", 72 * t, 72 * t + 64) if hh else h("yE%d" % (t % 2))
-        tt(h("yi", *c), h("mx", 15, 1024, 16), h("mn", 15, 1024, 16), A.add)
+        tt(h("yi", *c), h("mx", 16 * c[0] + 15, 16 * c[1], 16), h("mn", 16 * c[0] + 15, 16 * c[1], 16), A.add)
         tt(h("ymx", *c), h("yi", *c), z, A.max)
         cp(y, h("yi", *c))
-        mm(u, [(h("WB2"), h("ymx", *c)), (h("WBn"), y)], False, True)
+        mm(u, [(h("WB2"), h("ymx", *c)), (h("WBh"), y)], False, True)
         scan(h("us", *c), h("RSU"), u, 0.0, A.min, A.max)
-        cp(h("fi", *f), h("us", c[0] + 15, c[1], 16))
-        ts(h("fi", f[0] + 8, f[1] + 8), h("fi", *f), 31, A.bitwise_and)
+        ts(h("fi", f[0] + 8, f[1] + 8), h("us", c[0] + 15, c[1], 16), 31, A.bitwise_and)
         if hh:
             tt(h("msg", 72 * t + 64, 72 * t + 68), h("fi", 8, 12), h("M1", 128, 132), A.add)
         else:
-            tt(h("f16", 4, 8), h("fi", 12, 16), h("M1", 132, 136), A.add)
+            tt(h("f16", 4, 8), h("fi", 12, 16), h("M1", 140, 144), A.add)
             cp(h("L%d" % (t % 2), 4, 8), h("f16", 4, 8))
         cp(h("si", *c), u)
         zp = h("M2", 320 + c[0], 320 + c[1])
-        mm(zp, [(h("ID2"), h("ymx", *c)), (h("IDn"), y), (h("IDn"), z)])
+        mm(zp, [(h("ID2"), h("ymx", *c)), (h("IDh"), y), (h("IDn"), z)])
         act(h("Z%d" % ((t + 1) % 2), *c), zp)
 
     def write_half(t, hh, y):
@@ -547,8 +603,10 @@ def rank_program(g, core, T, topo):
             return
         act(h("qx", *c), ind(win, lst))
         tt(h("qm", *c), ind(win, lst), y, A.max)
-        pq = h("M2", 448, 512)
-        mm(pq, [(h("L3", 0, 128, 1, 1), h("JR", 0, 64, 1, 1)), (WY, y), (WX, h("qx", *c)), (WM, h("qm", *c))])
+        pq = h("Uo" if hh else "Ue", 0, 64)
+        mm(pq, [(h("L3", 0, 128, 1, 1), h("JR", 0, 64, 1, 1))], True, False)
+        mm(pq, [(h("WY"), y)], False, False)
+        mm(pq, [(WX, h("qx", *c)), (WM, h("qm", *c))], False, True)
         cp(ind(win, lst), y)
         act(h("Qn", *c), pq, bias=h("QB", 2 * t + hh, 2 * t + hh + 1))
         cp(ind(h("Q", 0, WIN), lst), h("Qn", *c))
@@ -568,36 +626,56 @@ def rank_program(g, core, T, topo):
 
     cores = T.cores
     constants()
-    starts(0)
+    start_sums(0, 1)
+    start_sums(0, 0)
+    start_keys(0, 1)
     for t in range(NSTEP):
         last = t == NSTEP - 1
-        first(t)
+        first(t, 1)
         if t == 0:
+            rank_as(t, "fill")
             constants2()
+        first(t, 0)
+        keys(t, 1)
+        rank_as(t, "fill")
         if 1 <= t < NSTEP - 1:
             spread("Z%d" % (t % 2), "zx%d" % (t % 2), ZG)
         u_start(t, 1)
         u_start(t, 0)
-        keys(t)
-        books(t)
-        dgather("s", 16, 40)
-        dgather("v", 0, 16)
-        dgather("s", 40, 64)
-        for a in (64, 96):
-            dgather("s", a, a + 32)
-        extremes(0, 16)
-        extremes(16, 40)
-        extremes(40, 64)
+        start_keys(t, 0)
+        keys(t, 0)
+        rank_as(t, "fill")
+        if t == CLEAN - 1:
+            for n in range(VB, VB + 2048, 128):
+                ts(h("V", n, n + 128), h("V", n, n + 128), 4095, A.bitwise_and)
+            fill(h("V", ZV, ZV + 8), ZC)
+        books(t, 1)
+        rank_as(t, "D1")
+        for q, a, b in DG[1]:
+            dgather(q, a, b)
+        for q, a, b in sorted(DG[1], key=lambda d: d[1]):
+            extremes(a, b)
+        rank_as(t, "Y1")
         y_of(t, 1)
         dst = cores[(rank + 1 + t % 3) % len(cores)]
         send(h("rxy", 72 * t, 72 * t + 68), h("msg", 72 * t, 72 * t + 68), "ry%d" % t, dst)
+        rank_as(t, "fill")
+        books(t, 0)
         if not last:
             send(h("V", kept(t) + 128, kept(t) + 192), h("V", kept(t), kept(t) + 64), "rf%d" % t, dst, "ry%d" % t)
-            starts(t + 1)
-        extremes(64, 96)
-        extremes(96, 128)
+            borrowers(t)
+            start_sums(t + 1, 1)
+            start_sums(t + 1, 0)
+            start_keys(t + 1, 1)
+        rank_as(t, "D0")
+        for q, a, b in DG[0]:
+            dgather(q, a, b)
+        for q, a, b in sorted(DG[0], key=lambda d: d[1]):
+            extremes(a, b)
+        rank_as(t, "Y0")
         y_of(t, 0)
         write_half(t, 0, h("yE%d" % (t % 2)))
+        rank_as(t, "fill")
         new_lists(t)
         if last:
             m = merged(t)
@@ -608,15 +686,18 @@ def rank_program(g, core, T, topo):
             act(h("zo", 1, 128, 2), h(zf, 0, 64))
             act(h("zo", 0, 128, 2), h(zf, 64, 128))
             dma("y", "dyz", T.yz[:, :], ap(h("zo")), None, h("zo"))
+        rank_as(t, "Y0")
         src = cores[(rank - 1 - t % 3) % len(cores)]
         landed = len(topo.engines(src, core)[:ENG])
         recv(h("rxy", 72 * t, 72 * t + 68), "ry%d" % t, landed)
         if not last:
             recv(h("V", kept(t) + 128, kept(t) + 192), "rf%d" % t, landed)
-        tt(h("f16", 8, 12), h("rxy", 72 * t + 64, 72 * t + 68), h("f16", 0, 4), A.add)
-        cp(h("L%d" % (t % 2), 0, 4), h("f16", 8, 12))
+        ts(h("L%d" % (t % 2), 0, 4), h("rxy", 72 * t + 64, 72 * t + 68), col(CRX), A.add)
         write_half(t, 1, h("rxy", 72 * t, 72 * t + 64))
     dma("y", "dyx", T.yx[:, :], ap(h("X", 0, 4096)), None, h("X", 0, 4096))
-    schedule()
+    if not ORDER:
+        schedule()
+    for i in ORDER:
+        ops[i][1]()
     for s in sorted(total):
         wait("g", (s, total[s]), {s: total[s]})

@@ -10,35 +10,38 @@ VB = HW * NSTEP
 ZV = VB + 4096
 LA = ZV + 8
 MARK = 1 << 24
-SC = 2.0 ** -17
+SC = 2.0 ** 17
 RND = 1.5 * 2.0 ** 28
 CY = 0.83e-3 * 1.1
 WAKE = 0.18
-ROUNDS = 10
-JITTER = 0.2
+ROUNDS = 100
+JITTER = 0.3
 RANKS = ["C1", "T1", "R1", "T0", "K1", "C0", "R0", "D1", "Y1", "K0", "D0", "Y0"]
 ENG = 8
-PC = ((0, 2, 4, 6, 8), (0, 3, 6, 8))
-PT = ((0, 2, 4, 6, 8), (0, 3, 6, 8))
+PC = ((0, 2, 6, 8), (0, 3, 6, 8))
+PT = ((0, 4, 8), (0, 3, 6, 8))
+UP = 128
+QS = (10, 12, 14, 15)
+CV = (0, 0)
 CLEAN = 1
-DG = ((("s", 80, 104), ("v", 64, 80), ("s", 104, 128)), (("v", 0, 16), ("s", 16, 32), ("s", 32, 48), ("s", 48, 64)))
+DG = ((("s", 64, 88), ("v", 88, 104), ("s", 104, 120), ("s", 120, 128)), (("v", 0, 16), ("s", 16, 40), ("s", 40, 56), ("s", 56, 64)))
 XCUT = (0, 512, 1024, 2048, 3072, 4096)
 ZG = 15
 
 SCRATCH = {"X": ("sbuf", [128, WIN], BF), "Q": ("sbuf", [128, WIN], F32), "V": ("sbuf", [128, LA + 128 + 256 * NSTEP], I32)}
 for _w, _d, _names in (
-        (1, I32, "wb thb"), (8, I32, "p8"), (8, U16, "ov og PL L0 L1"), (8, BF, "W2"), (24, F16, "WQ"), (192, F16, "THr"), (16, F32, "CB QB f16"), (16, BF, "RH"), (16, I32, "fi i16"),
-        (32, F32, "cols"), (64, F32, "RSU"), (64, BF, "MQ20 JR"), (64, F16, "yE0 yE1"), (512, BF, "WZ d0 RSM RSN"),
+        (1, I32, "wb thb"), (8, I32, "p8"), (8, U16, "ov og PL L0 L1"), (8, BF, "W2"), (24, F16, "WQ"), (192, F16, "THr"), (16, F32, "CB QB QI f16"), (16, BF, "RH"), (16, I32, "fi i16"),
+        (32, F32, "cols"), (64, F32, "RSU"), (64, BF, "MQ20 MQ22"), (128, F16, "IDu uh"), (256, BF, "JR d0"), (64, F16, "yE0 yE1"), (512, BF, "WZ RSM RSN"),
         (128, I32, "scb wmb si sj yi us"), (128, BF, "zb Z0 Z1 WB2 WBn IDb ID2 IDn IDm blb blh blx ymx qm qx zo wmf wj GI L3 sg"), (128, U16, "S0 S1 F16"),
         (128, F16, "MQh WY IDh WBh"), (1280, BF, "ST"), (4, F32, "BK4"),
-        (128, F32, "OF blk ID MQ NQ so Qn tf"), (512, F32, "RO"), (72, F32, "SP SPs RSK"), (144, F32, "VC mk dd GG DR O144"), (72, BF, "RA1 RB1 RC1 KC"),
+        (128, F32, "OF blk ID MQ NQ so Qn tf"), (512, F32, "RO"), (72, F32, "SP SPs RSK"), (144, F32, "VC mk dd GG O144"), (144, U16, "DR"), (72, BF, "RA1 RB1 RC1 KC"),
         (NSTEP * 72, F16, "msg rxy"), (2048, BF, "T zx0 zx1"), (2048, F16, "C D mx mn")):
     for _n in _names.split():
         SCRATCH[_n] = ("sbuf", [128, _w], _d)
 PSUM = ("Ro", "Re", "KB", "PT", "Uo", "Ue", "M1", "M2")
 for _n in PSUM:
     SCRATCH[_n] = ("psum", [128, 512], F32)
-LOADS = ["scb", "zb", "wb", "thb", "wmb", "vw"] + ["X%d" % n for n in range(len(XCUT) - 1)]
+LOADS = ["scb", "zb", "wb", "thb", "wmb", "vw0", "vw1", "vw2", "vw3"] + ["X%d" % n for n in range(len(XCUT) - 1)]
 SEMAPHORES = ["sv", "ss", "sp", "sg", "ls", "dyx", "dys", "dyz"] + ["d" + n for n in LOADS] + ["ry%d" % t for t in range(NSTEP)] + ["rf%d" % t for t in range(NSTEP - 1)]
 ORDER = []
 
@@ -175,17 +178,21 @@ def rank_program(g, core, T, topo):
                         cand.append(j)
             return end
         key = [1000] * n
-        for a, r in ranks:
+        kind, met = [("", 0, i) for i in range(n)], {}
+        for a, r, t, name in ranks:
             key[a:] = [r] * (n - a)
+            met[(t, name)] = met.get((t, name), 0) + 1
+            kind[a:] = [(name, met[(t, name)], i) for i in range(n - a)]
         for i in range(n - 1, -1, -1):
             key[i] = min([key[i]] + [key[j] for j in succ[i]])
         best = end = place(key, pred, succ, False)
         seed = 1
         for _ in range(ROUNDS):
-            key = []
-            for e in best:
+            shift = {}
+            for k in sorted(set(kind)):
                 seed = seed * 48271 % 2147483647
-                key.append(-e + JITTER * seed / 2147483647)
+                shift[k] = JITTER * (seed / 2147483647) ** 3
+            key = [shift[kind[i]] - best[i] for i in range(n)]
             end = place([-e for e in place(key, succ, pred, True)], pred, succ, False)
             if max(end) <= max(best):
                 best = end
@@ -300,12 +307,15 @@ def rank_program(g, core, T, topo):
         ops.append(("remote" + sem, emit, [flag("@" + sem)], [out], 2.7, 0.0, "remote"))
 
     def rank_as(t, name):
-        ranks.append((len(ops), len(RANKS) * t + RANKS.index(name) if name != "fill" else 1000))
+        ranks.append((len(ops), len(RANKS) * t + RANKS.index(name) if name != "fill" else 1000, t, name))
 
     for n, (a, b) in enumerate(zip(XCUT, XCUT[1:])):
         dma("y", "dX%d" % n, ap(h("X", a, b)), T.reg[:, a:b], h("X", a, b), lat=2.0 + 0.3 * n + b * 0.85e-3)
-    dma("y", "dvw", ap(h("V", VB, VB + 2048)), T.vw[:, :], h("V", VB, VB + 2048), lat=10.2)
-    for n, (b, t) in enumerate((("zb", T.z0), ("scb", T.scan), ("thb", T.th), ("wb", T.wt))):
+    for n in range(4):
+        a = 512 * n
+        dma("y", "dvw%d" % n, ap(h("V", VB + a, VB + a + 512)), T.vw[:, a:a + 512], h("V", VB + a, VB + a + 512), lat=7.3 + 0.87 * n)
+    dma("y", "dwb", ap(h("wb")), T.wt[:, :], h("wb"), lat=10.4)
+    for n, (b, t) in enumerate((("zb", T.z0), ("scb", T.scan), ("thb", T.th))):
         dma("s", "d" + b, ap(h(b)), t[:, :], h(b), lat=2.4 + n)
         if n == 1:
             dma("s", "dwmb", T["wmb"][0:8, :], T.warm[:, :], h("wmb"), lat=4.0)
@@ -335,20 +345,31 @@ def rank_program(g, core, T, topo):
     ts(h("p8", 3, 4), h("p8", 0, 1), 2, A.logical_shift_right, 3, A.bitwise_and)
     ts(col(T1), h("p8", 2, 3), 16.0, A.mult)
     tt(col(T1), col(T1), h("p8", 3, 4), A.add)
-    iota(h("i16", 0, 8), [[64, 2], [4, 4]], 0, 0)
-    ts(h("PL"), h("i16", 0, 8), col(T1), A.add)
+    iota(h("us", 0, 8), [[64, 2], [4, 4]], 0, 0)
+    ts(h("PL"), h("us", 0, 8), col(T1), A.add)
     fill(h("WZ"), 0.0)
     WS, WY, WX, WM = [h("WZ", 128 * n, 128 * n + 128) for n in range(4)]
     for lo, s in ((0, 1.0), (1, 1.0), (128, 1.0), (129, -1.0), (257, -1.0), (385, 2.0)):
         act(h("WZ", lo, lo + 113, 16), BK8, scale=s)
     ts(col(D0C), col(M3), 30001.0, A.mult, -30000.0, A.add)
     iota(h("RSM"), [[0, 32], [256, 16]], -1, 0)
-    act(h("d0"), h("WZ"), bias=col(D0C), scale=0.0)
+    act(h("d0"), h("WZ", 0, 256), bias=col(D0C), scale=0.0)
     banks = ["KB", "PT", "Uo", "Ue"]
-    for n in range(8):
-        b = h(banks[n % 4])
-        mm(b, [(WS, h("X", 512 * n, 512 * n + 512))])
-        scan(h("Q", 512 * n, 512 * n + 512), h("d0"), b, float(VB + 512 * n - 1), A.add, A.max)
+    iota(h("JR", 0, 256, 1, 1), [[1, 256]], 0, 0)
+    act(h("L3", 0, 128, 1, 1), h("O144", 0, 128, 1, 1), scale=0.0)
+    act(h("L3", 3, 128, 16, 1), h("O144", 0, 8, 1, 1))
+    iota(h("i16"), [[256, 16]], VB, 0)
+    ts(h("QI"), h("i16"), col(M3), A.mult)
+    for m in range(16):
+        if m in QS:
+            b = h(("Ue", "Re", "M2", "Ro")[QS.index(m) % 4], 0, 256)
+            mm(b, [(h("L3", 0, 128, 1, 1), h("JR", 0, 256, 1, 1))], True, False)
+            mm(b, [(WS, h("X", 256 * m, 256 * m + 256))], False, True)
+            act(h("Q", 256 * m, 256 * m + 256), b, bias=h("QI", m, m + 1))
+        else:
+            b = h(banks[m % 3], 0, 256)
+            mm(b, [(WS, h("X", 256 * m, 256 * m + 256))])
+            scan(h("Q", 256 * m, 256 * m + 256), h("d0"), b, float(VB + 256 * m - 1), A.add, A.max)
     act(h("Z0", 0, 64), h("zb", 1, 128, 2))
     act(h("Z0", 64, 128), h("zb", 0, 128, 2))
     cp(h("V", LA, LA + 64), h("scb", 1, 128, 2))
@@ -389,8 +410,10 @@ def rank_program(g, core, T, topo):
     cp(h("wj", 64, 128, 1, 8), h("wmb", 0, 128, 2, 8))
     mm(h("M1", 0, 128), [(h("wj", 0, 128, 1, 8), h("GI", 0, 128, 1, 8))])
     tt(h("wmf"), h("M1", 0, 128), h("MQ"), A.mult)
-    fill(h("ST"), 0.0)
-    fill(h("RO"), 0.0)
+    for n in range(0, 1280, 256):
+        fill(h("ST", n, n + 256), 0.0)
+    for n in range(0, 512, 128):
+        fill(h("RO", n, n + 128), 0.0)
     MV, P0, N0 = 0, 1, 3
 
     def state(n, hh, b=None):
@@ -404,7 +427,7 @@ def rank_program(g, core, T, topo):
     for hh in (1, 0):
         r, lo = half(hh), half(hh)[0]
         for b in (0, 1):
-            mm(h("M2", lo, lo + 64, 1, (64 * b, 64 * b + 64)), [(h("blb", r[0], r[1], 1, r), h("wmf", b, 128, 2, r))])
+            mm(h("M2", lo, lo + 64, 1, (64 * b, 64 * b + 64)), [(h("blb", r[0], r[1]), h("wmf", b, 128, 2))])
         unfold("ST", state(N0, hh)[1], h("M2", lo, lo + 64), bias=1.0, scale=-1.0)
 
     def constants():
@@ -416,29 +439,35 @@ def rank_program(g, core, T, topo):
         iota(h("mk"), [[0, 8], [1, 18]], 0, 0)
         fill(h("SP", 16, 72, 18), 0.0)
         fill(h("SP", 17, 72, 18), 0.0)
-        act(h("SPs"), h("SP"), scale=SC)
-        act(h("RA1"), h("SP"), scale=2048.0)
-        act(h("RB1"), h("SP"), scale=4096.0)
+        act(h("dd", 0, 1), h("SP", 0, 1), scale=-1.0)
+        tt(h("dd", 1, 72), h("SP", 0, 71), h("SP", 1, 72), A.subtract)
+        act(h("SPs"), h("dd", 0, 72), scale=SC)
+        act(h("RA1"), h("dd", 0, 72), scale=2048.0 * SC)
+        act(h("RB1"), h("dd", 0, 72), scale=4096.0 * SC)
         act(h("RC1"), h("SP"), scale=0.0)
-        act(h("RA1", 16, 72, 18), BK4, scale=-16384.0)
-        act(h("RA1", 17, 72, 18), BK4, scale=-32768.0)
-        act(h("RB1", 16, 72, 18), BK4, scale=-32768.0)
-        act(h("RC1", 17, 72, 18), BK4, scale=-4096.0)
-        act(h("KC"), h("mk", 0, 72), bias=0.9375, scale=-0.0625)
-        act(h("KC", 16, 72, 18), BK4, bias=53248.0 - 16 * 16384, scale=0.0)
-        act(h("KC", 17, 72, 18), BK4, bias=65536.0 - 16 * 32768, scale=0.0)
-        act(h("RSK"), h("mk", 0, 72), scale=1.0e7)
-        act(h("VC"), h("mk"), bias=3200.0 * SC, scale=0.0)
-        act(h("VC", 16, 144, 18), BK8, bias=ZV * SC, scale=0.0)
-        iota(h("i16", 8, 16), [[16, 8]], LA, 0)
-        ts(h("VC", 17, 144, 18), h("i16", 8, 16), col(QC), A.add, SC, A.mult)
+        ts(h("GG", 0, 4), h("SP", 15, 72, 18), 0.125, A.mult)
+        tt(h("GG", 0, 4), h("GG", 0, 4), BK4, A.add)
+        act(h("RA1", 16, 72, 18), h("GG", 0, 4), scale=16384.0 * SC)
+        act(h("RA1", 17, 72, 18), BK4, scale=16384.0 * SC)
+        act(h("RB1", 16, 72, 18), h("GG", 0, 4), scale=32768.0 * SC)
+        act(h("RB1", 17, 72, 18), BK4, scale=-32768.0 * SC)
+        act(h("RC1", 17, 72, 18), BK4, scale=4096.0 * SC)
+        act(h("KC"), h("SP"), bias=0.0625 * SC, scale=0.0)
+        act(h("KC", 0, 72, 18), BK4, bias=-2.0 ** 22 * SC, scale=0.0)
+        act(h("KC", 16, 72, 18), BK4, bias=(16 * 16384 - 53248.0) * SC, scale=0.0)
+        act(h("KC", 17, 72, 18), BK4, bias=(53248.0 - 16 * 16384 - 65536.0 + 16 * 32768) * SC, scale=0.0)
+        act(h("RSK"), h("SP"), scale=0.0)
+        act(h("VC"), h("mk"), bias=3200.0 - VB, scale=0.0)
+        act(h("VC", 16, 144, 18), BK8, bias=float(ZV - VB), scale=0.0)
+        iota(h("yi", 0, 8), [[16, 8]], LA, 0)
+        ts(h("VC", 17, 144, 18), h("yi", 0, 8), col(QC), A.add, -float(VB), A.add)
         fill(h("V", ZV, ZV + 8), MARK)
         iota(h("X", ZC, ZC + 16), [[0, 16]], 0, 0)
         iota(h("RSN"), [[0, 32], [-256, 16]], 255, 0)
 
     def constants2():
-        for n in range(VB, VB + 2048, 256):
-            ts(h("V", n + 2048, n + 2304), h("V", n, n + 256), 12, A.logical_shift_right)
+        for n in range(VB, VB + 2048, UP):
+            ts(h("V", n + 2048, n + 2048 + UP), h("V", n, n + UP), 12, A.logical_shift_right)
         act(h("WY"), WY)
         act(h("IDh"), h("ID"), scale=-1.0)
         act(h("ID2"), h("ID"), scale=2.0)
@@ -451,6 +480,8 @@ def rank_program(g, core, T, topo):
         act(h("WBn"), h("blk"), scale=col(WN))
         act(h("WBh"), h("blk"), scale=col(WN))
         act(h("MQ20"), h("MQ", 0, 64), scale=2.0 ** 20)
+        act(h("MQ22"), h("MQ", 0, 64), bias=1280.0 * 4096, scale=2.0 ** 20)
+        act(h("IDu"), h("ID"), scale=-4096.0)
         act(h("RSU"), h("NQ", 0, 64), scale=1.0e7)
         act(col(K37), col(QC), bias=15.5, scale=37.0)
         act(col(AK0), col(QC), scale=37.0)
@@ -464,12 +495,9 @@ def rank_program(g, core, T, topo):
         ts(h("CB", 12, 16), h("fi", 0, 4), col(C64), A.add)
         ts(h("CB", 4, 12), h("fi", 8, 16), col(QC), A.add)
         act(col(CRX), col(QC), bias=2048.0 + 32, scale=64.0)
-        iota(h("JR", 0, 64, 1, 1), [[1, 64]], 0, 0)
-        act(h("L3", 0, 128, 1, 1), h("NQ", 0, 128, 1, 1), scale=0.0)
-        act(h("L3", 3, 128, 16, 1), h("O144", 0, 8, 1, 1))
-        iota(h("i16", 0, 10), [[64, 5], [64, 2]], VB + 128, 0)
+        iota(h("sj", 0, 10), [[64, 5], [64, 2]], VB + 128, 0)
         iota(h("si", 0, 10), [[1, 5], [0, 2]], 1, 0)
-        ts(h("QB", 0, 10), h("i16", 0, 10), col(M3), A.mult)
+        ts(h("QB", 0, 10), h("sj", 0, 10), col(M3), A.mult)
         ts(h("so", 0, 10), h("si", 0, 10), col(M2), A.mult)
         tt(h("QB", 0, 10), h("QB", 0, 10), h("so", 0, 10), A.add)
         for n in range(8):
@@ -489,12 +517,17 @@ def rank_program(g, core, T, topo):
         lst, zx = "S%d" % (max(t - 1, 0) % 2), "zx%d" % (max(t - 1, 0) % 2)
         o = half(hh)[0]
         rank_as(t, "C%d" % hh)
+        from_q = lambda a, b: (h("C", 16 * o + 128 * a, 16 * o + 128 * b), ind(h("Q", 0, 4096), h(lst, o + 8 * a, o + 8 * b)))
         for a, b in zip(PC[hh], PC[hh][1:]):
-            act(h("C", 16 * o + 128 * a, 16 * o + 128 * b), ind(h("Q", 0, 4096), h(lst, o + 8 * a, o + 8 * b)), bias=col(QBIAS))
+            if b <= 8 - CV[hh]:
+                act(*from_q(a, b), bias=col(QBIAS))
         rank_as(t, "T%d" % hh)
         for a, b in zip(PT[hh], PT[hh][1:]):
             lo, hi = 16 * o + 128 * a, 16 * o + 128 * b
             tt(h("T", lo, hi), ind(h("X", 0, 4096), h(lst, o + 8 * a, o + 8 * b)), h(zx, lo, hi), A.max)
+        rank_as(t, "C%d" % hh)
+        for a in range(8 - CV[hh], 8):
+            ts(*from_q(a, a + 1), col(QBIAS), A.add)
         rank_as(t, "R%d" % hh)
         ra = [flag("@r%d" % hh)]
         part = lambda nm, q: h(nm, 16 * o + 128 * q, 16 * o + 128 * q + 128)
@@ -511,25 +544,24 @@ def rank_program(g, core, T, topo):
         unfold("ST", state(MV, hh)[1], h(bank(hh), 128, 192), AF.Sign, col(AT0 + t % 2))
         unfold("RO", ro + 128, h(bank(hh), 64, 128))
         k, p = h("KB", 0, 72), h("PT", 0, 72)
-        mm(k, [(h("RO", ro, ro + 128), h("SP"))], False, False)
+        mm(k, [(h("RO", ro, ro + 128), h("SPs"))], False, False)
         mm(k, [(state(MV, hh), h("RA1"))], False, True)
-        mm(p, [(h("RO", ro + 128, ro + 256), h("SPs"))], False, True)
+        mm(p, [(h("RO", ro + 128, ro + 256), h("SP"))], False, True)
         rank_as(t, "K%d" % hh)
-        scan(h("mk", a, b), h("RSK", 0, 72), k, 0.0, A.min, A.max)
-        tt(h("dd", a, b), h("mk", a, b), k, A.subtract)
+        scan(h("dd", a, b), k, h("RSK"), 0.0, A.add, A.max)
         tt(h("GG", a, b), p, h("dd", a, b), A.subtract)
-        scan(h("DR", a, b), h("dd", a, b), h("GG", a, b), 0.0, A.min, A.max)
+        for n in range(4):
+            scan(h("DR", a + n, b, 4), h("dd", a + 18 * n, a + 18 * n + 18), h("GG", a + 18 * n, a + 18 * n + 18), 0.0, A.min, A.max)
         lo = kept(t - 1)
-        ts(h("ov", *four(hh)), h("DR", a + 17, b, 18), 1.0 / SC, A.mult, -float(lo), A.add)
         f = h("V", kept(t) + c[0], kept(t) + c[1])
-        view = ind(h("V", lo, merged(max(t - 2, -1)) + 128), h("ov", *four(hh)))
+        view = ind(h("V", lo, merged(max(t - 2, -1)) + 128), h("DR", b - 4, b))
         if t < CLEAN:
-            ts(f, view, MARK + 4095, A.bitwise_and)
-            ts(h("F16", *c), f, float(ZC), A.min)
+            ts(h("si", *c), view, MARK + 4095, A.bitwise_and)
+            ts(h("F16", *c), h("si", *c), float(ZC), A.min)
         else:
             cp(h("F16", *c), view)
-            rank_as(t, "fill")
-            cp(f, view)
+        rank_as(t, "fill")
+        cp(f, h("F16", *c))
 
     both = lambda w, n, hh: [(h(w), state(n, hh, b)) for b in (0, 1)]
 
@@ -556,8 +588,9 @@ def rank_program(g, core, T, topo):
         act(col(T2), col(T1), bias=-RND - 8192.0 * (t + 1))
         act(col(AT0 + (t + 1) % 2), col(AN), bias=col(T2))
         act(col(AK0 + (t + 1) % 2), col(AP), bias=col(K37))
+        act(h("VC"), h("VC"), bias=float(HW))
         if t >= 1:
-            act(h("VC", 17, 144, 18), h("VC", 17, 144, 18), bias=256 * SC)
+            act(h("VC", 17, 144, 18), h("VC", 17, 144, 18), bias=256.0)
 
     def dgather(q, a, b):
         o, x = h("D", 16 * a, 16 * b), ind(h("X", 0, 4112), h("F16", a, b))
@@ -579,17 +612,20 @@ def rank_program(g, core, T, topo):
         z, u = h("Z%d" % (t % 2), *c), h("Uo" if hh else "Ue", 0, 64)
         y = h("msg", 72 * t, 72 * t + 64) if hh else h("yE%d" % (t % 2))
         tt(h("yi", *c), h("mx", 16 * c[0] + 15, 16 * c[1], 16), h("mn", 16 * c[0] + 15, 16 * c[1], 16), A.add)
-        tt(h("ymx", *c), h("yi", *c), z, A.max)
         cp(y, h("yi", *c))
-        mm(u, [(h("WB2"), h("ymx", *c)), (h("WBh"), y)], False, True)
+        tt(h("ymx", *c), h("yi", *c), z, A.max)
+        mm(u, [(h("WBh"), y)], False, False)
+        mm(u, [(h("WB2"), h("ymx", *c))], False, True)
         scan(h("us", *c), h("RSU"), u, 0.0, A.min, A.max)
         ts(h("fi", f[0] + 8, f[1] + 8), h("us", c[0] + 15, c[1], 16), 31, A.bitwise_and)
         if hh:
             tt(h("msg", 72 * t + 64, 72 * t + 68), h("fi", 8, 12), h("M1", 128, 132), A.add)
         else:
-            tt(h("f16", 4, 8), h("fi", 12, 16), h("M1", 140, 144), A.add)
-            cp(h("L%d" % (t % 2), 4, 8), h("f16", 4, 8))
-        cp(h("si", *c), u)
+            for n in range(4):
+                ts(h("L%d" % (t % 2), 4 + n, 5 + n), h("fi", 12 + n, 13 + n), h("M1", 140 + n, 141 + n), A.add)
+        rank_as(t, "fill" if t < NSTEP - 1 else "Y0")
+        act(h("uh", *c), u, bias=1280.0 - 2047.5 / 4096, scale=1.0 / 4096)
+        mm(h("M1", 256 + c[0], 256 + c[1]), [(h("IDb"), h("MQ22")), (h("WBn"), z), (h("WBh"), y), (h("WB2"), h("ymx", *c)), (h("IDu"), h("uh", *c))])
         zp = h("M2", 320 + c[0], 320 + c[1])
         mm(zp, [(h("ID2"), h("ymx", *c)), (h("IDh"), y), (h("IDn"), z)])
         act(h("Z%d" % ((t + 1) % 2), *c), zp)
@@ -614,10 +650,8 @@ def rank_program(g, core, T, topo):
     def new_lists(t):
         f, fp, fa = h("V", kept(t), kept(t) + 128), h("M1", 256, 384), h("M1", 384, 512)
         m = merged(t)
-        ts(fp, f, float(ZC), A.min)
-        ts(fa, f, float(ZC), A.min, col(AK0 + t % 2), A.add)
-        ts(h("si"), h("si"), 4095, A.bitwise_and)
-        tt(h("sj"), h("si"), fp, A.mult)
+        ts(fa, f, col(AK0 + t % 2), A.add)
+        tt(h("sj"), f, fp, A.mult)
         ts(h("sj"), h("sj"), 5, A.logical_shift_right)
         tt(h("V", m - 128, m), h("sj"), fa, A.add)
         ts(h("V", m, m + 128), ind(h("V", m - 256, m), h("og")), 4095, A.bitwise_and)
@@ -657,12 +691,16 @@ def rank_program(g, core, T, topo):
             extremes(a, b)
         rank_as(t, "Y1")
         y_of(t, 1)
+        rank_as(t, "Y1")
         dst = cores[(rank + 1 + t % 3) % len(cores)]
+        if t == 0:
+            send(h("V", kept(t) + 128, kept(t) + 192), h("V", kept(t), kept(t) + 64), "rf%d" % t, dst)
         send(h("rxy", 72 * t, 72 * t + 68), h("msg", 72 * t, 72 * t + 68), "ry%d" % t, dst)
         rank_as(t, "fill")
         books(t, 0)
         if not last:
-            send(h("V", kept(t) + 128, kept(t) + 192), h("V", kept(t), kept(t) + 64), "rf%d" % t, dst, "ry%d" % t)
+            if t:
+                send(h("V", kept(t) + 128, kept(t) + 192), h("V", kept(t), kept(t) + 64), "rf%d" % t, dst, "ry%d" % t)
             borrowers(t)
             start_sums(t + 1, 1)
             start_sums(t + 1, 0)
@@ -674,6 +712,7 @@ def rank_program(g, core, T, topo):
             extremes(a, b)
         rank_as(t, "Y0")
         y_of(t, 0)
+        rank_as(t, "Y0")
         write_half(t, 0, h("yE%d" % (t % 2)))
         rank_as(t, "fill")
         new_lists(t)
@@ -681,7 +720,7 @@ def rank_program(g, core, T, topo):
             m = merged(t)
             cp(h("so", 1, 128, 2), h("V", m, m + 64))
             cp(h("so", 0, 128, 2), h("V", m + 64, m + 128))
-            dma("y", "dys", T.ys[:, :], ap(h("so")), None, h("so"))
+            dma("s", "dys", T.ys[:, :], ap(h("so")), None, h("so"), 4.5)
             zf = "Z%d" % (NSTEP % 2)
             act(h("zo", 1, 128, 2), h(zf, 0, 64))
             act(h("zo", 0, 128, 2), h(zf, 64, 128))
@@ -694,7 +733,7 @@ def rank_program(g, core, T, topo):
             recv(h("V", kept(t) + 128, kept(t) + 192), "rf%d" % t, landed)
         ts(h("L%d" % (t % 2), 0, 4), h("rxy", 72 * t + 64, 72 * t + 68), col(CRX), A.add)
         write_half(t, 1, h("rxy", 72 * t, 72 * t + 64))
-    dma("y", "dyx", T.yx[:, :], ap(h("X", 0, 4096)), None, h("X", 0, 4096))
+    dma("y", "dyx", T.yx[:, :], ap(h("X", 0, 4096)), None, h("X", 0, 4096), 5.0)
     if not ORDER:
         schedule()
     for i in ORDER:

@@ -12,37 +12,55 @@ LA = ZV + 8
 MARK = 1 << 24
 SC = 2.0 ** 17
 RND = 1.5 * 2.0 ** 28
-CY = 0.83e-3 * 1.1
-WAKE = 0.18
-ROUNDS = 100
+CY = 0.83e-3 * 1.2
+WAKE = 0.2
+ROUNDS = 20
 JITTER = 0.3
-RANKS = ["C1", "T1", "R1", "T0", "K1", "C0", "R0", "D1", "Y1", "K0", "D0", "Y0"]
+FIX = 0
+QK = 9
+QM = 14
+ZS = 256
+QL = 9
+PT0 = (0, 4, 8)
+FIRST = {"p": "Ro6 -Uo3 KB1 KB2 PT1 -Ue3",
+         "v": "F161 D1 V1 mx1 mn1 mx2 mn2 dd2 mx3 mn3 GG2 mx4 mn4 "
+              "DR5 DR6 DR7 DR8 yi1 si2 msg1 ymx1 F162 us1 D2 fi1 Ls1 mx5 mn5 mx6 mn6 mx7 mn7 mx8 mn8 V2 yi2 yE1 ymx2 us2 og1 fi2 L1 L2 qm1 X1",
+         "s": "RO1 RO2 ST1 ST2 RO3 RO4 C5 C6 C7 -Q1 -Q2 RO5 RO6 ST3 ST4 RO7 RO8 D1 D2 D3 ST5 ST6 -Q3 ST7 ST8 D4 D5 D6 uh1 Z1 uh2 Z2 qx1 Qn1"}
+T00 = "T0"
+MOVES = 2200
+EARLY = 100
+LOOSE = ("sj1",)
+TURNS = {"p": "",
+         "v": "-Q1 -qm2 -X2 -Q2 T1 T2 T3 T4 T5 C1 dd1 -sj2 GG1 -V3 DR1 DR2 DR3 DR4 F161 D1 V1 dd2 mx1 mn1 GG2 mx2 mn2 mx3 mn3 mx4 mn4 DR5 DR6 DR7 DR8 yi1 F162 msg1 ymx1 "
+              "D2 us1 mx6 fi1 mn6 Ls1 mx5 mn5 mx7 mn7 mx8 mn8 V2 yi2 yE1 ymx2 -V4 M1 us2 og1 fi2 L1 L2 -S1 qm1 X1 sj1",
+         "s": "zx1 -qx2 -Qn2 C1 C2 C3 C4 RO1 RO2 ST1 ST2 RO3 RO4 C5 C6 RO5 RO6 ST3 ST4 RO7 RO8 D1 D2 D3 ST5 ST6 VC1 ST7 ST8 ST9 ST10 D4 D5 D6 uh1 Z1 uh2 Z2 qx1 Qn1"}
+RANKS = ["C1", "T1", "R1", "T0", "K1", "C0", "R0", "K0", "D1", "Y1", "D0", "Y0"]
 ENG = 8
-PC = ((0, 2, 6, 8), (0, 3, 6, 8))
-PT = ((0, 4, 8), (0, 3, 6, 8))
+PC = ((0, 2, 6, 7, 8), (0, 3, 6, 8))
+PT = ((0, 4, 8), (0, 4, 8))
 UP = 128
-QS = (10, 12, 14, 15)
-CV = (0, 0)
+QS = (9, 10, 11, 12, 13, 14, 15)
+CV = (1, 0)
 CLEAN = 1
 DG = ((("s", 64, 88), ("v", 88, 104), ("s", 104, 120), ("s", 120, 128)), (("v", 0, 16), ("s", 16, 40), ("s", 40, 56), ("s", 56, 64)))
-XCUT = (0, 512, 1024, 2048, 3072, 4096)
+XCUT = (0, 512, 1536, 2560, 3584, 4096)
 ZG = 15
 
 SCRATCH = {"X": ("sbuf", [128, WIN], BF), "Q": ("sbuf", [128, WIN], F32), "V": ("sbuf", [128, LA + 128 + 256 * NSTEP], I32)}
 for _w, _d, _names in (
-        (1, I32, "wb thb"), (8, I32, "p8"), (8, U16, "ov og PL L0 L1"), (8, BF, "W2"), (24, F16, "WQ"), (192, F16, "THr"), (16, F32, "CB QB QI f16"), (16, BF, "RH"), (16, I32, "fi i16"),
+        (1, I32, "wb"), (128, I32, "thr"), (8, I32, "p8"), (8, U16, "ov og PL L0 L1"), (8, BF, "W2"), (24, F16, "WQ W0"), (192, F16, "THr"), (16, F32, "CB QB QI f16"), (16, BF, "RH"), (16, I32, "fi i16"),
         (32, F32, "cols"), (64, F32, "RSU"), (64, BF, "MQ20 MQ22"), (128, F16, "IDu uh"), (256, BF, "JR d0"), (64, F16, "yE0 yE1"), (512, BF, "WZ RSM RSN"),
         (128, I32, "scb wmb si sj yi us"), (128, BF, "zb Z0 Z1 WB2 WBn IDb ID2 IDn IDm blb blh blx ymx qm qx zo wmf wj GI L3 sg"), (128, U16, "S0 S1 F16"),
         (128, F16, "MQh WY IDh WBh"), (1280, BF, "ST"), (4, F32, "BK4"),
         (128, F32, "OF blk ID MQ NQ so Qn tf"), (512, F32, "RO"), (72, F32, "SP SPs RSK"), (144, F32, "VC mk dd GG O144"), (144, U16, "DR"), (72, BF, "RA1 RB1 RC1 KC"),
-        (NSTEP * 72, F16, "msg rxy"), (2048, BF, "T zx0 zx1"), (2048, F16, "C D mx mn")):
+        (NSTEP * 72, F16, "msg rxy"), (NSTEP * 8, U16, "Ls Lr"), (2048, BF, "T zx0 zx1"), (2048, F16, "C D mx mn")):
     for _n in _names.split():
         SCRATCH[_n] = ("sbuf", [128, _w], _d)
 PSUM = ("Ro", "Re", "KB", "PT", "Uo", "Ue", "M1", "M2")
 for _n in PSUM:
     SCRATCH[_n] = ("psum", [128, 512], F32)
 LOADS = ["scb", "zb", "wb", "thb", "wmb", "vw0", "vw1", "vw2", "vw3"] + ["X%d" % n for n in range(len(XCUT) - 1)]
-SEMAPHORES = ["sv", "ss", "sp", "sg", "ls", "dyx", "dys", "dyz"] + ["d" + n for n in LOADS] + ["ry%d" % t for t in range(NSTEP)] + ["rf%d" % t for t in range(NSTEP - 1)]
+SEMAPHORES = ["sv", "ss", "sp", "sg", "ls", "dyx", "dys", "dyz"] + ["d" + n for n in LOADS] + ["ry%d" % t for t in range(NSTEP)] + ["rl%d" % t for t in range(NSTEP)] + ["rf%d" % t for t in range(NSTEP - 1)]
 ORDER = []
 
 
@@ -55,6 +73,7 @@ def rank_program(g, core, T, topo):
     total = {}
     know = {q: {} for q in queues}
     ops = []
+    order = []
     ranks = []
     adds = set()
     hist = {}
@@ -142,6 +161,25 @@ def rank_program(g, core, T, topo):
                     if wr and i not in adds:
                         lst[:] = [e for e in lst if not covers(x, e[0])]
                     lst.append((x, wr, tag, i))
+        step, met, named = [-1] * n, {}, {}
+        for a, _r, t, _name in ranks:
+            step[a:] = [t] * (n - a)
+        for i, o in enumerate(ops):
+            k = (step[i], o[0], o[3][0][0].rstrip("01") if o[3] else "")
+            met[k] = met.get(k, 0) + 1
+            named[k[:2] + (k[2] + str(met[k]),)] = i
+        for q in TURNS:
+            for t in range(NSTEP):
+                for at, name in enumerate((TURNS if t else FIRST)[q].split()):
+                    k = (t - 1, q, name[1:]) if name[0] == "-" else (t, q, name)
+                    if k in named and (t < NSTEP - 1 or name not in LOOSE):
+                        order.append((q, 100 * t + at, named[k]))
+        free, last = set(), {}
+        for name, _at, i in sorted(order):
+            if name in last and last[name] not in pred[i]:
+                pred[i].append(last[name])
+                free.add((last[name], i))
+            last[name] = i
         succ = [[] for _ in ops]
         for i in range(n):
             pred[i] = sorted(set(pred[i]))
@@ -150,7 +188,7 @@ def rank_program(g, core, T, topo):
         holds = [[o[0]] + sorted(set([x[0] for x in o[2] + o[3] if x[0] in PSUM])) for o in ops]
 
         def lag(i, j):
-            return ops[i][5] + (0.0 if ops[i][0] == ops[j][0] == "p" else WAKE)
+            return ops[i][5] + (0.0 if ops[i][0] == ops[j][0] == "p" or (i, j) in free else WAKE)
 
         def place(key, before, after, back):
             end, used, left = [0.0] * n, {}, [len(b) for b in before]
@@ -196,6 +234,51 @@ def rank_program(g, core, T, topo):
             end = place([-e for e in place(key, succ, pred, True)], pred, succ, False)
             if max(end) <= max(best):
                 best = end
+        for _ in range(EARLY):
+            key = [best[i] - ops[i][4] for i in range(n)]
+            for i in range(n):
+                if step[i] < 1:
+                    seed = seed * 48271 % 2147483647
+                    if seed % 8 == 0:
+                        key[i] -= (seed % 1000) * (0.003 if step[i] < 0 else 0.0005)
+            end = place(key, pred, succ, False)
+            if max(end) <= max(best):
+                best = end
+        twins = {}
+        for i in range(n):
+            twins.setdefault(kind[i], []).append(i)
+        now = best
+        for move in range(MOVES):
+            start = [now[i] - ops[i][4] for i in range(n)]
+            ending = {}
+            for i in range(n):
+                for r in holds[i]:
+                    ending[(r, round(now[i], 6))] = i
+            i, held = now.index(max(now)), []
+            while start[i] > 1e-6:
+                by = [j for j in pred[i] if abs(now[j] + lag(j, i) - start[i]) < 1e-6]
+                other = [ending.get((r, round(start[i] - m, 6))) for r in holds[i] for m in (0.0, WAKE)]
+                other = [j for j in other if j is not None and j != i and j not in pred[i]]
+                held += [(j, i) for j in other[:1]]
+                if not by + other:
+                    break
+                seed = seed * 48271 % 2147483647
+                i = (by + other)[seed % len(by + other)]
+            if not held:
+                break
+            seed = seed * 48271 % 2147483647
+            j, i = held[seed % len(held)]
+            pairs = [(j, i)]
+            if seed % 3 and len(twins[kind[i]]) == len(twins[kind[j]]):
+                pairs = list(zip(twins[kind[j]], twins[kind[i]]))
+            for j, i in pairs:
+                if abs(start[i] - start[j]) < 2.0:
+                    start[j] = start[i] + 1e-3 + (seed % 5) * 0.1
+            end = place(start, pred, succ, False)
+            if max(end) <= max(now):
+                now = end
+                if max(now) < max(best):
+                    best = now
         ORDER.extend(sorted(range(n), key=lambda c: (best[c] - ops[c][4], c)))
 
     def elems(x):
@@ -306,19 +389,23 @@ def rank_program(g, core, T, topo):
             hist.setdefault(out[0], []).append((out, True, "remote", bump(sem, n), {sem: n}))
         ops.append(("remote" + sem, emit, [flag("@" + sem)], [out], 2.7, 0.0, "remote"))
 
+    def chain(name, at=0):
+        order.append((name, at, len(ops) - 1))
+
     def rank_as(t, name):
         ranks.append((len(ops), len(RANKS) * t + RANKS.index(name) if name != "fill" else 1000, t, name))
 
     for n, (a, b) in enumerate(zip(XCUT, XCUT[1:])):
-        dma("y", "dX%d" % n, ap(h("X", a, b)), T.reg[:, a:b], h("X", a, b), lat=2.0 + 0.3 * n + b * 0.85e-3)
+        dma("y", "dX%d" % n, ap(h("X", a, b)), T.reg[:, a:b], h("X", a, b), lat=(2.4 if n else 1.6) + b * 0.855e-3)
+        if n == 0:
+            for m, (nm, t) in enumerate((("zb", T.z0), ("scb", T.scan))):
+                dma("y", "d" + nm, ap(h(nm)), t[:, :], h(nm), lat=2.4 + 0.32 * m)
+            dma("y", "dwmb", T["wmb"][0:8, :], T.warm[:, :], h("wmb"), lat=2.8)
+            dma("y", "dthb", T["thr"][0:1, :], T.th[:, :], h("thr"), lat=2.9)
     for n in range(4):
         a = 512 * n
-        dma("y", "dvw%d" % n, ap(h("V", VB + a, VB + a + 512)), T.vw[:, a:a + 512], h("V", VB + a, VB + a + 512), lat=7.3 + 0.87 * n)
-    dma("y", "dwb", ap(h("wb")), T.wt[:, :], h("wb"), lat=10.4)
-    for n, (b, t) in enumerate((("zb", T.z0), ("scb", T.scan), ("thb", T.th))):
-        dma("s", "d" + b, ap(h(b)), t[:, :], h(b), lat=2.4 + n)
-        if n == 1:
-            dma("s", "dwmb", T["wmb"][0:8, :], T.warm[:, :], h("wmb"), lat=4.0)
+        dma("y", "dvw%d" % n, ap(h("V", VB + a, VB + a + 512)), T.vw[:, a:a + 512], h("V", VB + a, VB + a + 512), lat=6.8 + 0.87 * n)
+    dma("y", "dwb", ap(h("wb")), T.wt[:, :], h("wb"), lat=9.8)
     for o in ops:
         o[1]()
     ops[:] = [("load%d" % n, lambda: None, [], o[3], o[5], 0.0, o[6]) for n, o in enumerate(ops)]
@@ -360,21 +447,26 @@ def rank_program(g, core, T, topo):
     act(h("L3", 3, 128, 16, 1), h("O144", 0, 8, 1, 1))
     iota(h("i16"), [[256, 16]], VB, 0)
     ts(h("QI"), h("i16"), col(M3), A.mult)
-    for m in range(16):
-        if m in QS:
-            b = h(("Ue", "Re", "M2", "Ro")[QS.index(m) % 4], 0, 256)
-            mm(b, [(h("L3", 0, 128, 1, 1), h("JR", 0, 256, 1, 1))], True, False)
-            mm(b, [(WS, h("X", 256 * m, 256 * m + 256))], False, True)
-            act(h("Q", 256 * m, 256 * m + 256), b, bias=h("QI", m, m + 1))
-        else:
-            b = h(banks[m % 3], 0, 256)
-            mm(b, [(WS, h("X", 256 * m, 256 * m + 256))])
-            scan(h("Q", 256 * m, 256 * m + 256), h("d0"), b, float(VB + 256 * m - 1), A.add, A.max)
+
+    def fill_q():
+        for m in list(range(QL)) + list(QS) + list(range(QL, QK)):
+            b = h("M1", 256, 512) if m >= QM or QL <= m < QK else h(("KB", "PT", "Uo", "Ue")[m % 4] if m < QK else "Uo" if m == QK else "Ue", 0, 256)
+            if m in QS:
+                mm(b, [(h("L3", 0, 128, 1, 1), h("JR", 0, 256, 1, 1)), (WS, h("X", 256 * m, 256 * m + 256))])
+                act(h("Q", 256 * m, 256 * m + 256), b, bias=h("QI", m, m + 1))
+            else:
+                rank_as(-1, RANKS[0] if m < QL else "fill")
+                mm(b, [(WS, h("X", 256 * m, 256 * m + 256))])
+                scan(h("Q", 256 * m, 256 * m + 256), h("d0"), b, float(VB + 256 * m - 1), A.add, A.max)
+                if m < QL:
+                    chain("@0", 0.5 if m > 1 else -1)
+                rank_as(-1, "fill")
     act(h("Z0", 0, 64), h("zb", 1, 128, 2))
     act(h("Z0", 64, 128), h("zb", 0, 128, 2))
     cp(h("V", LA, LA + 64), h("scb", 1, 128, 2))
     cp(h("V", LA + 64, LA + 128), h("scb", 0, 128, 2))
     cp(h("S0"), ind(h("V", LA, LA + 128), h("PL")))
+    chain("@0", 0.2)
 
     def spread(z, zx, ng):
         act(h(zx, 0, 2048, 16), ind(h(z), h("PL")))
@@ -397,23 +489,34 @@ def rank_program(g, core, T, topo):
     iota(h("NQ"), [[0, 8], [1, 16]], 0, 0)
     ts(h("MQ"), h("NQ"), col(QC), A.is_equal)
     act(h("MQh"), h("MQ"))
-    ts(col(THN), h("thb"), -1.0, A.mult, 2040.0, A.add)
+    ts(h("so", 0, 128, 1, 1), h("thr", 0, 128, 1, 1), -1.0, A.mult, 2040.0, A.add)
+    mm(h("M2", 256, 257), [(h("so", 0, 128, 1, 1), h("OF", 0, 1, 1, 1))])
+    cp(col(THN), h("M2", 256, 257))
     act(h("THr", 0, 128), h("blk"), scale=0.0)
     act(h("THr", 128, 192), h("blk", 0, 128, 2), scale=col(THN))
     keep(h("ID"), h("OF"), [[1, 128]], A.is_equal, 0, -1)
     act(h("IDb"), h("ID"))
     act(h("IDm"), h("ID"), scale=-16384.0)
     act(h("blb"), h("blk"))
-    fill(col(AT0), -0.5)
+    fill(col(AT0), -2040.5)
+    act(h("W0", 0, 8), BK8, scale=-1.0)
+    act(h("W0", 8, 16), BK8, scale=0.0)
+    act(h("W0", 16, 24), BK8)
+    ts(h("uh"), ind(h("V", LA, LA + 128), h("PL")), -2048.0, A.add)
+    for k in range(16):
+        ts(h("D", k, 2048, 16), h("uh"), h("MQ", k, k + 1), A.mult)
+        chain("@0")
     keep(h("GI", 0, 128, 1, 8), h("O144", 0, 128, 1, 8), [[1, 8], [0, 16]], A.is_equal, 0, -1)
     cp(h("wj", 0, 64, 1, 8), h("wmb", 1, 128, 2, 8))
     cp(h("wj", 64, 128, 1, 8), h("wmb", 0, 128, 2, 8))
     mm(h("M1", 0, 128), [(h("wj", 0, 128, 1, 8), h("GI", 0, 128, 1, 8))])
     tt(h("wmf"), h("M1", 0, 128), h("MQ"), A.mult)
-    for n in range(0, 1280, 256):
+    for n in range(0, ZS, 128):
+        act(h("ST", n, n + 128), h("OF"), scale=0.0)
+    for n in range(ZS, 1280, 256):
         fill(h("ST", n, n + 256), 0.0)
     for n in range(0, 512, 128):
-        fill(h("RO", n, n + 128), 0.0)
+        act(h("RO", n, n + 128), h("OF"), scale=0.0)
     MV, P0, N0 = 0, 1, 3
 
     def state(n, hh, b=None):
@@ -424,11 +527,14 @@ def rank_program(g, core, T, topo):
         for b in (0, 1):
             r = (64 * b, 64 * b + 64)
             act(h(name, lo + b, lo + 128, 2, r), h(x[0], x[1], x[2], 1, r), f, h(bias[0], bias[1], bias[2], 1, r) if isinstance(bias, tuple) else bias, scale)
+            if x[0] != "M2":
+                chain("@" + x[0])
     for hh in (1, 0):
         r, lo = half(hh), half(hh)[0]
         for b in (0, 1):
             mm(h("M2", lo, lo + 64, 1, (64 * b, 64 * b + 64)), [(h("blb", r[0], r[1]), h("wmf", b, 128, 2))])
         unfold("ST", state(N0, hh)[1], h("M2", lo, lo + 64), bias=1.0, scale=-1.0)
+    fill_q()
 
     def constants():
         for b in (0, 1):
@@ -441,12 +547,14 @@ def rank_program(g, core, T, topo):
         fill(h("SP", 17, 72, 18), 0.0)
         act(h("dd", 0, 1), h("SP", 0, 1), scale=-1.0)
         tt(h("dd", 1, 72), h("SP", 0, 71), h("SP", 1, 72), A.subtract)
+        chain("@0")
         act(h("SPs"), h("dd", 0, 72), scale=SC)
         act(h("RA1"), h("dd", 0, 72), scale=2048.0 * SC)
         act(h("RB1"), h("dd", 0, 72), scale=4096.0 * SC)
         act(h("RC1"), h("SP"), scale=0.0)
         ts(h("GG", 0, 4), h("SP", 15, 72, 18), 0.125, A.mult)
         tt(h("GG", 0, 4), h("GG", 0, 4), BK4, A.add)
+        chain("@0")
         act(h("RA1", 16, 72, 18), h("GG", 0, 4), scale=16384.0 * SC)
         act(h("RA1", 17, 72, 18), BK4, scale=16384.0 * SC)
         act(h("RB1", 16, 72, 18), h("GG", 0, 4), scale=32768.0 * SC)
@@ -491,10 +599,9 @@ def rank_program(g, core, T, topo):
         act(h("RH", 8, 12), h("BK4"), scale=-TR / 16.0)
         iota(h("fi", 0, 4), [[1024, 4]], TR, 0)
         iota(h("fi", 8, 16), [[16, 8]], 0, 0)
-        ts(h("CB", 0, 4), h("fi", 0, 4), -2048.0, A.add)
+        ts(h("CB", 0, 4), h("fi", 0, 4), col(C64), A.add, 32.0, A.add)
         ts(h("CB", 12, 16), h("fi", 0, 4), col(C64), A.add)
         ts(h("CB", 4, 12), h("fi", 8, 16), col(QC), A.add)
-        act(col(CRX), col(QC), bias=2048.0 + 32, scale=64.0)
         iota(h("sj", 0, 10), [[64, 5], [64, 2]], VB + 128, 0)
         iota(h("si", 0, 10), [[1, 5], [0, 2]], 1, 0)
         ts(h("QB", 0, 10), h("sj", 0, 10), col(M3), A.mult)
@@ -519,23 +626,31 @@ def rank_program(g, core, T, topo):
         rank_as(t, "C%d" % hh)
         from_q = lambda a, b: (h("C", 16 * o + 128 * a, 16 * o + 128 * b), ind(h("Q", 0, 4096), h(lst, o + 8 * a, o + 8 * b)))
         for a, b in zip(PC[hh], PC[hh][1:]):
-            if b <= 8 - CV[hh]:
+            if t == 0:
+                act(from_q(a, b)[0], ind(h("X", 0, 4096), h(lst, o + 8 * a, o + 8 * b)))
+            elif b <= 8 - CV[hh]:
                 act(*from_q(a, b), bias=col(QBIAS))
-        rank_as(t, "T%d" % hh)
-        for a, b in zip(PT[hh], PT[hh][1:]):
+        rank_as(t, "T%d" % hh if t or hh else T00)
+        cuts = PT[hh] if t or hh else PT0
+        for a, b in zip(cuts, cuts[1:]):
             lo, hi = 16 * o + 128 * a, 16 * o + 128 * b
             tt(h("T", lo, hi), ind(h("X", 0, 4096), h(lst, o + 8 * a, o + 8 * b)), h(zx, lo, hi), A.max)
-        rank_as(t, "C%d" % hh)
-        for a in range(8 - CV[hh], 8):
-            ts(*from_q(a, a + 1), col(QBIAS), A.add)
+            if t == 0:
+                chain("@0", 1)
+        if CV[hh] and t:
+            ts(*from_q(8 - CV[hh], 8), col(QBIAS), A.add)
+            if t and FIX:
+                chain("@v%d" % t, 3)
         rank_as(t, "R%d" % hh)
         ra = [flag("@r%d" % hh)]
         part = lambda nm, q: h(nm, 16 * o + 128 * q, 16 * o + 128 * q + 128)
-        for a, b in zip(PT[hh], PT[hh][1:]):
+        for a, b in zip(cuts, cuts[1:]):
             mms([(h(bank(hh), q, 64, 8), part("T", q), h("W2")) for q in range(a, b)], False, False, (), ra)
+        if t == 0:
+            mms([(h(bank(hh), 64 + q, 128, 8), part("D", q), h("W0", 16, 24)) for q in range(8)], False, False, (), ra)
         for a, b in zip(PC[hh], PC[hh][1:]):
             end = b == 8
-            mms([(h(bank(hh), q, 192, 8), part("C", q), h("WQ")) for q in range(a, b)], False, end, ra if end else (), () if end else ra)
+            mms([(h(bank(hh), q, 192, 8), part("C", q), h("WQ" if t else "W0")) for q in range(a, b)], False, end, ra if end else (), () if end else ra)
 
     def keys(t, hh):
         (a, b), c, ro = seg(hh), half(hh), 0 if hh else 256
@@ -549,7 +664,11 @@ def rank_program(g, core, T, topo):
         mm(p, [(h("RO", ro + 128, ro + 256), h("SP"))], False, True)
         rank_as(t, "K%d" % hh)
         scan(h("dd", a, b), k, h("RSK"), 0.0, A.add, A.max)
+        if t and hh and FIX:
+            chain("@v%d" % t, 5)
         tt(h("GG", a, b), p, h("dd", a, b), A.subtract)
+        if t and hh and FIX:
+            chain("@v%d" % t, 7)
         for n in range(4):
             scan(h("DR", a + n, b, 4), h("dd", a + 18 * n, a + 18 * n + 18), h("GG", a + 18 * n, a + 18 * n + 18), 0.0, A.min, A.max)
         lo = kept(t - 1)
@@ -619,10 +738,10 @@ def rank_program(g, core, T, topo):
         scan(h("us", *c), h("RSU"), u, 0.0, A.min, A.max)
         ts(h("fi", f[0] + 8, f[1] + 8), h("us", c[0] + 15, c[1], 16), 31, A.bitwise_and)
         if hh:
-            tt(h("msg", 72 * t + 64, 72 * t + 68), h("fi", 8, 12), h("M1", 128, 132), A.add)
+            scan(h("Ls", 8 * t, 8 * t + 4), h("fi", 8, 12), h("M1", 128, 132), 32.0, A.min, A.add)
         else:
-            for n in range(4):
-                ts(h("L%d" % (t % 2), 4 + n, 5 + n), h("fi", 12 + n, 13 + n), h("M1", 140 + n, 141 + n), A.add)
+            for a, b in ((0, 1), (1, 4)):
+                scan(h("L%d" % (t % 2), 4 + a, 4 + b), h("fi", 12 + a, 12 + b), h("M1", 140 + a, 140 + b), 32.0, A.min, A.add)
         rank_as(t, "fill" if t < NSTEP - 1 else "Y0")
         act(h("uh", *c), u, bias=1280.0 - 2047.5 / 4096, scale=1.0 / 4096)
         mm(h("M1", 256 + c[0], 256 + c[1]), [(h("IDb"), h("MQ22")), (h("WBn"), z), (h("WBh"), y), (h("WB2"), h("ymx", *c)), (h("IDu"), h("uh", *c))])
@@ -632,7 +751,7 @@ def rank_program(g, core, T, topo):
 
     def write_half(t, hh, y):
         c = half(hh)
-        lst = h("L%d" % (t % 2), *four(hh))
+        lst = h("Lr", 8 * t, 8 * t + 4) if hh else h("L%d" % (t % 2), 4, 8)
         win = h("X", 0, WIN)
         if t == NSTEP - 1:
             cp(ind(win, lst), y)
@@ -642,10 +761,13 @@ def rank_program(g, core, T, topo):
         pq = h("Uo" if hh else "Ue", 0, 64)
         mm(pq, [(h("L3", 0, 128, 1, 1), h("JR", 0, 64, 1, 1))], True, False)
         mm(pq, [(h("WY"), y)], False, False)
-        mm(pq, [(WX, h("qx", *c)), (WM, h("qm", *c))], False, True)
+        mm(pq, [(WM, h("qm", *c))], False, False)
+        mm(pq, [(WX, h("qx", *c))], False, True)
         cp(ind(win, lst), y)
         act(h("Qn", *c), pq, bias=h("QB", 2 * t + hh, 2 * t + hh + 1))
         cp(ind(h("Q", 0, WIN), lst), h("Qn", *c))
+        if hh and FIX:
+            chain("@v%d" % (t + 1), 1)
 
     def new_lists(t):
         f, fp, fa = h("V", kept(t), kept(t) + 128), h("M1", 256, 384), h("M1", 384, 512)
@@ -667,7 +789,7 @@ def rank_program(g, core, T, topo):
         last = t == NSTEP - 1
         first(t, 1)
         if t == 0:
-            rank_as(t, "fill")
+            rank_as(-1, "fill")
             constants2()
         first(t, 0)
         keys(t, 1)
@@ -680,9 +802,11 @@ def rank_program(g, core, T, topo):
         keys(t, 0)
         rank_as(t, "fill")
         if t == CLEAN - 1:
+            rank_as(-1, "fill")
             for n in range(VB, VB + 2048, 128):
                 ts(h("V", n, n + 128), h("V", n, n + 128), 4095, A.bitwise_and)
             fill(h("V", ZV, ZV + 8), ZC)
+            rank_as(t, "fill")
         books(t, 1)
         rank_as(t, "D1")
         for q, a, b in DG[1]:
@@ -695,12 +819,13 @@ def rank_program(g, core, T, topo):
         dst = cores[(rank + 1 + t % 3) % len(cores)]
         if t == 0:
             send(h("V", kept(t) + 128, kept(t) + 192), h("V", kept(t), kept(t) + 64), "rf%d" % t, dst)
-        send(h("rxy", 72 * t, 72 * t + 68), h("msg", 72 * t, 72 * t + 68), "ry%d" % t, dst)
+        send(h("rxy", 72 * t, 72 * t + 64), h("msg", 72 * t, 72 * t + 64), "ry%d" % t, dst, None if t else "rf0")
+        send(h("Lr", 8 * t, 8 * t + 4), h("Ls", 8 * t, 8 * t + 4), "rl%d" % t, dst, "ry%d" % t)
         rank_as(t, "fill")
         books(t, 0)
         if not last:
             if t:
-                send(h("V", kept(t) + 128, kept(t) + 192), h("V", kept(t), kept(t) + 64), "rf%d" % t, dst, "ry%d" % t)
+                send(h("V", kept(t) + 128, kept(t) + 192), h("V", kept(t), kept(t) + 64), "rf%d" % t, dst, "rl%d" % t)
             borrowers(t)
             start_sums(t + 1, 1)
             start_sums(t + 1, 0)
@@ -728,10 +853,10 @@ def rank_program(g, core, T, topo):
         rank_as(t, "Y0")
         src = cores[(rank - 1 - t % 3) % len(cores)]
         landed = len(topo.engines(src, core)[:ENG])
-        recv(h("rxy", 72 * t, 72 * t + 68), "ry%d" % t, landed)
+        recv(h("rxy", 72 * t, 72 * t + 64), "ry%d" % t, landed)
+        recv(h("Lr", 8 * t, 8 * t + 4), "rl%d" % t, landed)
         if not last:
             recv(h("V", kept(t) + 128, kept(t) + 192), "rf%d" % t, landed)
-        ts(h("L%d" % (t % 2), 0, 4), h("rxy", 72 * t + 64, 72 * t + 68), col(CRX), A.add)
         write_half(t, 1, h("rxy", 72 * t, 72 * t + 64))
     dma("y", "dyx", T.yx[:, :], ap(h("X", 0, 4096)), None, h("X", 0, 4096), 5.0)
     if not ORDER:

from concourse.mybir import AluOpType as A, ActivationFunctionType as AF

BF, F32, I32, U16, F16 = "bfloat16", "float32", "int32", "uint16", "float16"
NSTEP = 6
ZC = 4096
TR = 8192
WIN = 12304
HW = 192
VB = HW * NSTEP
ZV = VB + 4096
LA = ZV + 8
MARK = 1 << 24
SC = 2.0 ** 17
RND = 1.5 * 2.0 ** 28
CY = 0.83e-3 * 1.2
WAKE = 0.2
ROUNDS = 20
JITTER = 0.3
FIX = 0
QK = 9
QM = 14
ZS = 256
QL = 9
PT0 = (0, 4, 8)
FIRST = {"p": "Ro6 -Uo3 KB1 KB2 PT1 -Ue3",
         "v": "F161 D1 V1 mx1 mn1 mx2 mn2 dd2 mx3 mn3 GG2 mx4 mn4 "
              "DR5 DR6 DR7 DR8 yi1 si2 msg1 ymx1 F162 us1 D2 fi1 Ls1 mx5 mn5 mx6 mn6 mx7 mn7 mx8 mn8 V2 yi2 yE1 ymx2 us2 og1 fi2 L1 L2 qm1 X1",
         "s": "RO1 RO2 ST1 ST2 RO3 RO4 C5 C6 C7 -Q1 -Q2 RO5 RO6 ST3 ST4 RO7 RO8 D1 D2 D3 ST5 ST6 -Q3 ST7 ST8 D4 D5 D6 uh1 Z1 uh2 Z2 qx1 Qn1"}
T00 = "T0"
MOVES = 2200
EARLY = 100
LOOSE = ("sj1",)
TURNS = {"p": "",
         "v": "-Q1 -qm2 -X2 -Q2 T1 T2 T3 T4 T5 C1 dd1 -sj2 GG1 -V3 DR1 DR2 DR3 DR4 F161 D1 V1 dd2 mx1 mn1 GG2 mx2 mn2 mx3 mn3 mx4 mn4 DR5 DR6 DR7 DR8 yi1 F162 msg1 ymx1 "
              "D2 us1 mx6 fi1 mn6 Ls1 mx5 mn5 mx7 mn7 mx8 mn8 V2 yi2 yE1 ymx2 -V4 M1 us2 og1 fi2 L1 L2 -S1 qm1 X1 sj1",
         "s": "zx1 -qx2 -Qn2 C1 C2 C3 C4 RO1 RO2 ST1 ST2 RO3 RO4 C5 C6 RO5 RO6 ST3 ST4 RO7 RO8 D1 D2 D3 ST5 ST6 VC1 ST7 ST8 ST9 ST10 D4 D5 D6 uh1 Z1 uh2 Z2 qx1 Qn1"}
RANKS = ["C1", "T1", "R1", "T0", "K1", "C0", "R0", "K0", "D1", "Y1", "D0", "Y0"]
ENG = 8
PC = ((0, 2, 6, 7, 8), (0, 3, 6, 8))
PT = ((0, 4, 8), (0, 4, 8))
UP = 128
QS = (9, 10, 11, 12, 13, 14, 15)
CV = (1, 0)
CLEAN = 1
DG = ((("s", 64, 88), ("v", 88, 104), ("s", 104, 120), ("s", 120, 128)), (("v", 0, 16), ("s", 16, 40), ("s", 40, 56), ("s", 56, 64)))
XCUT = (0, 512, 1536, 2560, 3584, 4096)
ZG = 15

SCRATCH = {"X": ("sbuf", [128, WIN], BF), "Q": ("sbuf", [128, WIN], F32), "V": ("sbuf", [128, LA + 128 + 256 * NSTEP], I32)}
for _w, _d, _names in (
        (1, I32, "wb"), (128, I32, "thr"), (8, I32, "p8"), (8, U16, "ov og PL L0 L1"), (8, BF, "W2"), (24, F16, "WQ W0"), (192, F16, "THr"), (16, F32, "CB QB QI f16"), (16, BF, "RH"), (16, I32, "fi i16"),
        (32, F32, "cols"), (64, F32, "RSU"), (64, BF, "MQ20 MQ22"), (128, F16, "IDu uh"), (256, BF, "JR d0"), (64, F16, "yE0 yE1"), (512, BF, "WZ RSM RSN"),
        (128, I32, "scb wmb si sj yi us"), (128, BF, "zb Z0 Z1 WB2 WBn IDb ID2 IDn IDm blb blh blx ymx qm qx zo wmf wj GI L3 sg"), (128, U16, "S0 S1 F16"),
        (128, F16, "MQh WY IDh WBh"), (1280, BF, "ST"), (4, F32, "BK4"),
        (128, F32, "OF blk ID MQ NQ so Qn tf"), (512, F32, "RO"), (72, F32, "SP SPs RSK"), (144, F32, "VC mk dd GG O144"), (144, U16, "DR"), (72, BF, "RA1 RB1 RC1 KC"),
        (NSTEP * 72, F16, "msg rxy"), (NSTEP * 8, U16, "Ls Lr"), (2048, BF, "T zx0 zx1"), (2048, F16, "C D mx mn")):
    for _n in _names.split():
        SCRATCH[_n] = ("sbuf", [128, _w], _d)
PSUM = ("Ro", "Re", "KB", "PT", "Uo", "Ue", "M1", "M2")
for _n in PSUM:
    SCRATCH[_n] = ("psum", [128, 512], F32)
LOADS = ["scb", "zb", "wb", "thb", "wmb", "vw0", "vw1", "vw2", "vw3"] + ["X%d" % n for n in range(len(XCUT) - 1)]
SEMAPHORES = ["sv", "ss", "sp", "sg", "ls", "dyx", "dys", "dyz"] + ["d" + n for n in LOADS] + ["ry%d" % t for t in range(NSTEP)] + ["rl%d" % t for t in range(NSTEP)] + ["rf%d" % t for t in range(NSTEP - 1)]
ORDER = []


def rank_program(g, core, T, topo):
    rank = T.rank_of(core)
    if rank is None:
        return
    queues = {"v": g.vector, "s": g.scalar, "p": g.tensor, "g": g, "y": g.sync}
    own = {"v": "sv", "s": "ss", "p": "sp", "g": "sg"}
    total = {}
    know = {q: {} for q in queues}
    ops = []
    order = []
    ranks = []
    adds = set()
    hist = {}

    def h(name, lo=0, hi=None, step=1, rows=128):
        return (name, lo, T[name].shape[1] if hi is None else hi, step, rows if isinstance(rows, tuple) else (0, rows))

    def ind(win, off):
        return ("ind", win, off)

    def ap(x):
        if x[0] == "ind":
            return ap(x[1]).indirect(ap(x[2]))
        t = T[x[0]]
        p, q = x[4]
        return t[p:q, x[1]:x[2]] if x[3] == 1 else t[p:q, x[1]:x[2]:x[3]]

    def regions(x):
        return [x[1], x[2]] if x[0] == "ind" else [x]

    def apart(a, b):
        return a[1] >= b[2] or a[2] <= b[1] or (a[3] == b[3] > 1 and (a[1] - b[1]) % a[3] != 0) or a[4][0] >= b[4][1] or a[4][1] <= b[4][0]

    def covers(a, b):
        return a[1] <= b[1] and b[2] <= a[2] and (a[3] == 1 or (a[3] == b[3] and (a[1] - b[1]) % a[3] == 0)) and a[4][0] <= b[4][0] and b[4][1] <= a[4][1]

    def flag(name):
        return (name, 0, 1, 1, (0, 128))

    def wait(q, tok, clock):
        if know[q].get(tok[0], 0) >= tok[1]:
            return
        queues[q].wait_ge(T.sem[tok[0]], tok[1])
        for s, v in clock.items():
            if know[q].get(s, 0) < v:
                know[q][s] = v

    def need(q, reads, writes):
        todo = []
        for wr, group in ((False, reads), (True, writes)):
            for x in group:
                for e in hist.get(x[0], []):
                    if e[2] == q and q == "p":
                        continue
                    ps = x[0] in PSUM and e[2] != q
                    if not ps and apart(e[0], x):
                        continue
                    if (e[1] or wr or ps) and (e[3], e[4]) not in todo:
                        todo.append((e[3], e[4]))
        todo.sort(key=lambda c: -len(c[1]))
        for tok, clock in todo:
            wait(q, tok, clock)

    def note(q, tok, reads, writes, tag=None):
        clock = dict(know[q])
        clock[tok[0]] = tok[1]
        tag = tag or q
        for wr, group in ((True, writes), (False, reads)):
            for x in group:
                lst = hist.setdefault(x[0], [])
                if wr:
                    lst[:] = [e for e in lst if not covers(x, e[0])]
                else:
                    lst[:] = [e for e in lst if not (not e[1] and e[2] == tag and covers(x, e[0]) and tag in own)]
                lst.append((x, wr, tag, tok, clock))

    def bump(sem, n):
        total[sem] = total.get(sem, 0) + n
        return (sem, total[sem])

    def schedule():
        n = len(ops)
        pred, seen = [[] for _ in ops], {}
        for i, (q, _e, reads, writes, us, lat, tag) in enumerate(ops):
            for wr, group in ((False, reads), (True, writes)):
                for x in group:
                    for e in seen.get(x[0], []):
                        if apart(e[0], x) or (x[0] in PSUM and i in adds and e[3] in adds):
                            continue
                        if e[1] or wr:
                            pred[i].append(e[3])
            for wr, group in ((True, writes), (False, reads)):
                for x in group:
                    lst = seen.setdefault(x[0], [])
                    if wr and i not in adds:
                        lst[:] = [e for e in lst if not covers(x, e[0])]
                    lst.append((x, wr, tag, i))
        step, met, named = [-1] * n, {}, {}
        for a, _r, t, _name in ranks:
            step[a:] = [t] * (n - a)
        for i, o in enumerate(ops):
            k = (step[i], o[0], o[3][0][0].rstrip("01") if o[3] else "")
            met[k] = met.get(k, 0) + 1
            named[k[:2] + (k[2] + str(met[k]),)] = i
        for q in TURNS:
            for t in range(NSTEP):
                for at, name in enumerate((TURNS if t else FIRST)[q].split()):
                    k = (t - 1, q, name[1:]) if name[0] == "-" else (t, q, name)
                    if k in named and (t < NSTEP - 1 or name not in LOOSE):
                        order.append((q, 100 * t + at, named[k]))
        free, last = set(), {}
        for name, _at, i in sorted(order):
            if name in last and last[name] not in pred[i]:
                pred[i].append(last[name])
                free.add((last[name], i))
            last[name] = i
        succ = [[] for _ in ops]
        for i in range(n):
            pred[i] = sorted(set(pred[i]))
            for j in pred[i]:
                succ[j].append(i)
        holds = [[o[0]] + sorted(set([x[0] for x in o[2] + o[3] if x[0] in PSUM])) for o in ops]

        def lag(i, j):
            return ops[i][5] + (0.0 if ops[i][0] == ops[j][0] == "p" or (i, j) in free else WAKE)

        def place(key, before, after, back):
            end, used, left = [0.0] * n, {}, [len(b) for b in before]
            cand = [i for i in range(n) if not left[i]]
            while cand:
                i = min(cand, key=lambda c: (key[c], c))
                cand.remove(i)
                st = max([end[j] + (lag(i, j) if back else lag(j, i)) for j in before[i]] + [0.0])
                q, us, was = ops[i][0], ops[i][4], -1.0
                while was < st:
                    was = st
                    for r in holds[i]:
                        for slot in range(int(was - 1.0), int(was + us + 1.0) + 1):
                            for a, b, who in used.get((r, slot), ()):
                                m = 0.0 if who == q else WAKE
                                if a - m < st + us and st < b + m and (r == q or who != q):
                                    st = b + m
                end[i] = st + us
                for r in holds[i]:
                    for slot in range(int(st), int(end[i]) + 1):
                        used.setdefault((r, slot), []).append((st, end[i], q))
                for j in after[i]:
                    left[j] -= 1
                    if not left[j]:
                        cand.append(j)
            return end
        key = [1000] * n
        kind, met = [("", 0, i) for i in range(n)], {}
        for a, r, t, name in ranks:
            key[a:] = [r] * (n - a)
            met[(t, name)] = met.get((t, name), 0) + 1
            kind[a:] = [(name, met[(t, name)], i) for i in range(n - a)]
        for i in range(n - 1, -1, -1):
            key[i] = min([key[i]] + [key[j] for j in succ[i]])
        best = end = place(key, pred, succ, False)
        seed = 1
        for _ in range(ROUNDS):
            shift = {}
            for k in sorted(set(kind)):
                seed = seed * 48271 % 2147483647
                shift[k] = JITTER * (seed / 2147483647) ** 3
            key = [shift[kind[i]] - best[i] for i in range(n)]
            end = place([-e for e in place(key, succ, pred, True)], pred, succ, False)
            if max(end) <= max(best):
                best = end
        for _ in range(EARLY):
            key = [best[i] - ops[i][4] for i in range(n)]
            for i in range(n):
                if step[i] < 1:
                    seed = seed * 48271 % 2147483647
                    if seed % 8 == 0:
                        key[i] -= (seed % 1000) * (0.003 if step[i] < 0 else 0.0005)
            end = place(key, pred, succ, False)
            if max(end) <= max(best):
                best = end
        twins = {}
        for i in range(n):
            twins.setdefault(kind[i], []).append(i)
        now = best
        for move in range(MOVES):
            start = [now[i] - ops[i][4] for i in range(n)]
            ending = {}
            for i in range(n):
                for r in holds[i]:
                    ending[(r, round(now[i], 6))] = i
            i, held = now.index(max(now)), []
            while start[i] > 1e-6:
                by = [j for j in pred[i] if abs(now[j] + lag(j, i) - start[i]) < 1e-6]
                other = [ending.get((r, round(start[i] - m, 6))) for r in holds[i] for m in (0.0, WAKE)]
                other = [j for j in other if j is not None and j != i and j not in pred[i]]
                held += [(j, i) for j in other[:1]]
                if not by + other:
                    break
                seed = seed * 48271 % 2147483647
                i = (by + other)[seed % len(by + other)]
            if not held:
                break
            seed = seed * 48271 % 2147483647
            j, i = held[seed % len(held)]
            pairs = [(j, i)]
            if seed % 3 and len(twins[kind[i]]) == len(twins[kind[j]]):
                pairs = list(zip(twins[kind[j]], twins[kind[i]]))
            for j, i in pairs:
                if abs(start[i] - start[j]) < 2.0:
                    start[j] = start[i] + 1e-3 + (seed % 5) * 0.1
            end = place(start, pred, succ, False)
            if max(end) <= max(now):
                now = end
                if max(now) < max(best):
                    best = now
        ORDER.extend(sorted(range(n), key=lambda c: (best[c] - ops[c][4], c)))

    def elems(x):
        return 16 * (x[2][2] - x[2][1]) if x[0] == "ind" else -(-(x[2] - x[1]) // x[3])

    def vtime(o, ins, cyc):
        n = elems(o)
        if o[0] == "ind":
            return 0.05 + 3.8 * n * CY
        if [x for x in ins if x[0] == "ind"]:
            return 0.05 + 1.56 * n * CY
        return max(64.0, cyc * n) * CY

    def rate(*xs):
        return 1.0 if [x for x in xs if SCRATCH[x[1][0] if x[0] == "ind" else x[0]][2] in (F32, I32)] else 0.5

    def run(q, call, out, ins, us, more=()):
        reads = [r for x in ins for r in regions(x)] + regions(out)[1:]
        writes = regions(out)[:1] + list(more)

        def emit():
            need(q, reads, writes)
            call().then_inc(T.sem[own[q]], 1)
            note(q, bump(own[q], 1), reads, writes)
        ops.append((q, emit, reads, writes, us, 0.0, q))

    V, S = g.vector, g.scalar

    def val(s):
        return ap(s) if isinstance(s, tuple) else s

    def tt(o, x, y, op):
        run("v", lambda: V.tensor_tensor(ap(o), ap(x), ap(y), op), o, [x, y], vtime(o, [x, y], 1.0 if x[0] in PSUM or y[0] in PSUM else 2.0))

    def ts(o, x, s1, op0, s2=None, op1=None):
        ins = [x] + [s for s in (s1, s2) if isinstance(s, tuple)]
        if op1 is None:
            run("v", lambda: V.tensor_scalar(ap(o), ap(x), val(s1), None, op0), o, ins, vtime(o, [x], rate(o, x)))
        else:
            run("v", lambda: V.tensor_scalar(ap(o), ap(x), val(s1), val(s2), op0, op1), o, ins, vtime(o, [x], rate(o, x)))

    def cp(o, x):
        run("v", lambda: V.tensor_copy(ap(o), ap(x)), o, [x], vtime(o, [x], rate(o, x)))

    def fill(o, c):
        run("v", lambda: V.memset(ap(o), c), o, [], vtime(o, [], rate(o)))

    def scan(o, d0, d1, init, op0, op1):
        run("v", lambda: V.tensor_tensor_scan(ap(o), ap(d0), ap(d1), init, op0, op1), o, [d0, d1], vtime(o, [], rate(o, d0, d1)))

    def act(o, x, f=AF.Identity, bias=0.0, scale=1.0, accum=None):
        us = 0.065 + 1.56 * elems(o) * CY if x[0] == "ind" else max(64, elems(o)) * CY
        ins = [x] + [s for s in (bias, scale) if isinstance(s, tuple)]
        if accum:
            run("s", lambda: S.activation(ap(o), ap(x), f, bias=val(bias), scale=val(scale), accum_out=ap(accum)), o, ins, us + 0.02, [accum])
        else:
            run("s", lambda: S.activation(ap(o), ap(x), f, bias=val(bias), scale=val(scale)), o, ins, us)

    def iota(o, pattern, base, cm):
        small = SCRATCH[o[0]][2] != I32
        run("g", lambda: g.iota(ap(o), pattern, base, cm, allow_small_or_imprecise_dtypes=small), o, [], 0.13 + 2 * elems(o) * CY)

    def keep(o, x, pattern, op, base, cm, other=0.0):
        run("g", lambda: g.affine_select(ap(o), ap(x), pattern, op, other, base, cm), o, [x], 0.17 + 2 * elems(o) * CY)

    def mms(items, start=True, stop=True, after=(), mark=()):
        reads = [x for p in items for x in p[1:]] + list(mark)
        writes = [p[0] for p in items] + list(after)
        us = sum([max(min(64, elems(l)), elems(o)) * CY * (4 if SCRATCH[l[0]][2] == F32 else 1) for o, l, r in items])

        def emit():
            need("p", reads, writes)
            for n, (o, l, r) in enumerate(items):
                i = g.tensor.matmul(ap(o), ap(l), ap(r), start and n == 0, stop and n == len(items) - 1)
            i.then_inc(T.sem["sp"], 1)
            note("p", bump("sp", 1), reads, writes)
        if not start and not stop:
            adds.add(len(ops))
        ops.append(("p", emit, reads, writes, us, 0.0, "p"))

    def mm(out, pairs, start=True, stop=True):
        mms([(out, l, r) for l, r in pairs], start, stop)

    def dma(q, sem, out, in_, ohandle=None, ihandle=None, lat=2.0):
        reads, writes = ([ihandle] if ihandle else []), ([ohandle] if ohandle else [])

        def emit():
            need(q, reads, writes)
            queues[q].dma_start(out, in_).then_inc(T.sem[sem], 16)
            note(q, bump(sem, 16), reads, writes, q + "dma")
        ops.append((q, emit, reads, writes, 0.06, lat, q + "dma"))

    def send(out, in_, remote, dst, after=None):
        rid, pid, _se = topo.addr(dst)
        eng = topo.engines(core, dst)[:ENG]
        m = 0
        for e in eng:
            m |= 1 << e

        def emit():
            need("g", [in_], [])
            g.remote_dma(ap(out), ap(in_), T.sem[remote], T.sem["ls"], pid, rid, m)
            bump("ls", len(eng))
        ops.append(("g", emit, [in_] + ([flag("@" + after)] if after else []), [flag("@" + remote)], 0.8, 0.0, "g"))

    def recv(out, sem, n):
        def emit():
            hist.setdefault(out[0], []).append((out, True, "remote", bump(sem, n), {sem: n}))
        ops.append(("remote" + sem, emit, [flag("@" + sem)], [out], 2.7, 0.0, "remote"))

    def chain(name, at=0):
        order.append((name, at, len(ops) - 1))

    def rank_as(t, name):
        ranks.append((len(ops), len(RANKS) * t + RANKS.index(name) if name != "fill" else 1000, t, name))

    for n, (a, b) in enumerate(zip(XCUT, XCUT[1:])):
        dma("y", "dX%d" % n, ap(h("X", a, b)), T.reg[:, a:b], h("X", a, b), lat=(2.4 if n else 1.6) + b * 0.855e-3)
        if n == 0:
            for m, (nm, t) in enumerate((("zb", T.z0), ("scb", T.scan))):
                dma("y", "d" + nm, ap(h(nm)), t[:, :], h(nm), lat=2.4 + 0.32 * m)
            dma("y", "dwmb", T["wmb"][0:8, :], T.warm[:, :], h("wmb"), lat=2.8)
            dma("y", "dthb", T["thr"][0:1, :], T.th[:, :], h("thr"), lat=2.9)
    for n in range(4):
        a = 512 * n
        dma("y", "dvw%d" % n, ap(h("V", VB + a, VB + a + 512)), T.vw[:, a:a + 512], h("V", VB + a, VB + a + 512), lat=6.8 + 0.87 * n)
    dma("y", "dwb", ap(h("wb")), T.wt[:, :], h("wb"), lat=9.8)
    for o in ops:
        o[1]()
    ops[:] = [("load%d" % n, lambda: None, [], o[3], o[5], 0.0, o[6]) for n, o in enumerate(ops)]

    col = lambda c: h("cols", c, c + 1)
    QC, M0, M1, M2, M3, QBIAS, D0C, THN, WC, WN, K37, AK0, AK1, AT0, AT1, AP, T1, T2, ACC, C64, CRX, AN = range(22)
    half = lambda hh: (0, 64) if hh else (64, 128)
    four = lambda hh: (0, 4) if hh else (4, 8)
    BK8 = h("blk", 0, 128, 16)
    merged = lambda t: LA + 256 * (t + 1)
    kept = lambda t: VB - HW * (t + 1)
    iota(h("p8", 0, 1), [[0, 1]], 0, 1)
    fill(h("O144"), 1.0)
    fill(h("OF"), 1.0)
    keep(h("tf"), h("OF"), [[-16, 8], [0, 16]], A.is_ge, 0, 1)
    keep(h("blk"), h("tf"), [[16, 8], [0, 16]], A.is_ge, 15, -1)
    ts(h("p8", 1, 2), h("p8", 0, 1), 15, A.bitwise_and)
    cp(col(QC), h("p8", 1, 2))
    ts(col(M0), col(QC), 0.0, A.is_equal)
    ts(col(M1), col(QC), 1.0, A.is_equal)
    ts(col(M2), col(QC), 2.0, A.is_equal)
    ts(col(M3), col(QC), 3.0, A.is_equal)
    ts(h("p8", 2, 3), h("p8", 0, 1), 3, A.bitwise_and)
    ts(h("p8", 3, 4), h("p8", 0, 1), 2, A.logical_shift_right, 3, A.bitwise_and)
    ts(col(T1), h("p8", 2, 3), 16.0, A.mult)
    tt(col(T1), col(T1), h("p8", 3, 4), A.add)
    iota(h("us", 0, 8), [[64, 2], [4, 4]], 0, 0)
    ts(h("PL"), h("us", 0, 8), col(T1), A.add)
    fill(h("WZ"), 0.0)
    WS, WY, WX, WM = [h("WZ", 128 * n, 128 * n + 128) for n in range(4)]
    for lo, s in ((0, 1.0), (1, 1.0), (128, 1.0), (129, -1.0), (257, -1.0), (385, 2.0)):
        act(h("WZ", lo, lo + 113, 16), BK8, scale=s)
    ts(col(D0C), col(M3), 30001.0, A.mult, -30000.0, A.add)
    iota(h("RSM"), [[0, 32], [256, 16]], -1, 0)
    act(h("d0"), h("WZ", 0, 256), bias=col(D0C), scale=0.0)
    banks = ["KB", "PT", "Uo", "Ue"]
    iota(h("JR", 0, 256, 1, 1), [[1, 256]], 0, 0)
    act(h("L3", 0, 128, 1, 1), h("O144", 0, 128, 1, 1), scale=0.0)
    act(h("L3", 3, 128, 16, 1), h("O144", 0, 8, 1, 1))
    iota(h("i16"), [[256, 16]], VB, 0)
    ts(h("QI"), h("i16"), col(M3), A.mult)

    def fill_q():
        for m in list(range(QL)) + list(QS) + list(range(QL, QK)):
            b = h("M1", 256, 512) if m >= QM or QL <= m < QK else h(("KB", "PT", "Uo", "Ue")[m % 4] if m < QK else "Uo" if m == QK else "Ue", 0, 256)
            if m in QS:
                mm(b, [(h("L3", 0, 128, 1, 1), h("JR", 0, 256, 1, 1)), (WS, h("X", 256 * m, 256 * m + 256))])
                act(h("Q", 256 * m, 256 * m + 256), b, bias=h("QI", m, m + 1))
            else:
                rank_as(-1, RANKS[0] if m < QL else "fill")
                mm(b, [(WS, h("X", 256 * m, 256 * m + 256))])
                scan(h("Q", 256 * m, 256 * m + 256), h("d0"), b, float(VB + 256 * m - 1), A.add, A.max)
                if m < QL:
                    chain("@0", 0.5 if m > 1 else -1)
                rank_as(-1, "fill")
    act(h("Z0", 0, 64), h("zb", 1, 128, 2))
    act(h("Z0", 64, 128), h("zb", 0, 128, 2))
    cp(h("V", LA, LA + 64), h("scb", 1, 128, 2))
    cp(h("V", LA + 64, LA + 128), h("scb", 0, 128, 2))
    cp(h("S0"), ind(h("V", LA, LA + 128), h("PL")))
    chain("@0", 0.2)

    def spread(z, zx, ng):
        act(h(zx, 0, 2048, 16), ind(h(z), h("PL")))
        for k in range(1, 16):
            if k <= ng:
                keep(h(zx, k, 2048, 16), h(zx, 0, 2048, 16), [[0, 128]], A.is_ge, 0, 0)
            else:
                act(h(zx, k, 2048, 16), h(zx, 0, 2048, 16))
    spread("Z0", "zx0", 0)
    tt(col(T2), col(M0), col(M1), A.add)
    ts(col(QBIAS), col(M3), -3200.0, A.mult)
    ts(col(T2), col(T2), -2040.0, A.mult)
    tt(col(QBIAS), col(QBIAS), col(T2), A.add)
    act(h("W2"), BK8, scale=2.0)
    ts(col(T2), col(M2), -256.0, A.mult, col(M3), A.add)
    ts(h("WQ", 0, 8), BK8, col(M0), A.mult, -1.0, A.mult)
    ts(h("WQ", 8, 16), BK8, col(T2), A.mult)
    ts(col(T1), col(M2), 8192.0, A.mult, col(M1), A.add)
    ts(h("WQ", 16, 24), BK8, col(T1), A.mult)
    iota(h("NQ"), [[0, 8], [1, 16]], 0, 0)
    ts(h("MQ"), h("NQ"), col(QC), A.is_equal)
    act(h("MQh"), h("MQ"))
    ts(h("so", 0, 128, 1, 1), h("thr", 0, 128, 1, 1), -1.0, A.mult, 2040.0, A.add)
    mm(h("M2", 256, 257), [(h("so", 0, 128, 1, 1), h("OF", 0, 1, 1, 1))])
    cp(col(THN), h("M2", 256, 257))
    act(h("THr", 0, 128), h("blk"), scale=0.0)
    act(h("THr", 128, 192), h("blk", 0, 128, 2), scale=col(THN))
    keep(h("ID"), h("OF"), [[1, 128]], A.is_equal, 0, -1)
    act(h("IDb"), h("ID"))
    act(h("IDm"), h("ID"), scale=-16384.0)
    act(h("blb"), h("blk"))
    fill(col(AT0), -2040.5)
    act(h("W0", 0, 8), BK8, scale=-1.0)
    act(h("W0", 8, 16), BK8, scale=0.0)
    act(h("W0", 16, 24), BK8)
    ts(h("uh"), ind(h("V", LA, LA + 128), h("PL")), -2048.0, A.add)
    for k in range(16):
        ts(h("D", k, 2048, 16), h("uh"), h("MQ", k, k + 1), A.mult)
        chain("@0")
    keep(h("GI", 0, 128, 1, 8), h("O144", 0, 128, 1, 8), [[1, 8], [0, 16]], A.is_equal, 0, -1)
    cp(h("wj", 0, 64, 1, 8), h("wmb", 1, 128, 2, 8))
    cp(h("wj", 64, 128, 1, 8), h("wmb", 0, 128, 2, 8))
    mm(h("M1", 0, 128), [(h("wj", 0, 128, 1, 8), h("GI", 0, 128, 1, 8))])
    tt(h("wmf"), h("M1", 0, 128), h("MQ"), A.mult)
    for n in range(0, ZS, 128):
        act(h("ST", n, n + 128), h("OF"), scale=0.0)
    for n in range(ZS, 1280, 256):
        fill(h("ST", n, n + 256), 0.0)
    for n in range(0, 512, 128):
        act(h("RO", n, n + 128), h("OF"), scale=0.0)
    MV, P0, N0 = 0, 1, 3

    def state(n, hh, b=None):
        lo = 256 * n + (0 if hh else 128)
        return h("ST", lo, lo + 128) if b is None else h("ST", lo + b, lo + 128, 2)

    def unfold(name, lo, x, f=AF.Identity, bias=0.0, scale=1.0):
        for b in (0, 1):
            r = (64 * b, 64 * b + 64)
            act(h(name, lo + b, lo + 128, 2, r), h(x[0], x[1], x[2], 1, r), f, h(bias[0], bias[1], bias[2], 1, r) if isinstance(bias, tuple) else bias, scale)
            if x[0] != "M2":
                chain("@" + x[0])
    for hh in (1, 0):
        r, lo = half(hh), half(hh)[0]
        for b in (0, 1):
            mm(h("M2", lo, lo + 64, 1, (64 * b, 64 * b + 64)), [(h("blb", r[0], r[1]), h("wmf", b, 128, 2))])
        unfold("ST", state(N0, hh)[1], h("M2", lo, lo + 64), bias=1.0, scale=-1.0)
    fill_q()

    def constants():
        for b in (0, 1):
            r = (64 * b, 64 * b + 64)
            keep(h("SP"), h("SP" if b else "RO", 0, 72), [[16, 4], [1, 18]], A.not_equal, 64 * b, -1, 1.0)
            act(h("BK4", 0, 4, 1, r), h("blk", r[0], r[1], 16, r))
        BK4 = h("BK4")
        iota(h("mk"), [[0, 8], [1, 18]], 0, 0)
        fill(h("SP", 16, 72, 18), 0.0)
        fill(h("SP", 17, 72, 18), 0.0)
        act(h("dd", 0, 1), h("SP", 0, 1), scale=-1.0)
        tt(h("dd", 1, 72), h("SP", 0, 71), h("SP", 1, 72), A.subtract)
        chain("@0")
        act(h("SPs"), h("dd", 0, 72), scale=SC)
        act(h("RA1"), h("dd", 0, 72), scale=2048.0 * SC)
        act(h("RB1"), h("dd", 0, 72), scale=4096.0 * SC)
        act(h("RC1"), h("SP"), scale=0.0)
        ts(h("GG", 0, 4), h("SP", 15, 72, 18), 0.125, A.mult)
        tt(h("GG", 0, 4), h("GG", 0, 4), BK4, A.add)
        chain("@0")
        act(h("RA1", 16, 72, 18), h("GG", 0, 4), scale=16384.0 * SC)
        act(h("RA1", 17, 72, 18), BK4, scale=16384.0 * SC)
        act(h("RB1", 16, 72, 18), h("GG", 0, 4), scale=32768.0 * SC)
        act(h("RB1", 17, 72, 18), BK4, scale=-32768.0 * SC)
        act(h("RC1", 17, 72, 18), BK4, scale=4096.0 * SC)
        act(h("KC"), h("SP"), bias=0.0625 * SC, scale=0.0)
        act(h("KC", 0, 72, 18), BK4, bias=-2.0 ** 22 * SC, scale=0.0)
        act(h("KC", 16, 72, 18), BK4, bias=(16 * 16384 - 53248.0) * SC, scale=0.0)
        act(h("KC", 17, 72, 18), BK4, bias=(53248.0 - 16 * 16384 - 65536.0 + 16 * 32768) * SC, scale=0.0)
        act(h("RSK"), h("SP"), scale=0.0)
        act(h("VC"), h("mk"), bias=3200.0 - VB, scale=0.0)
        act(h("VC", 16, 144, 18), BK8, bias=float(ZV - VB), scale=0.0)
        iota(h("yi", 0, 8), [[16, 8]], LA, 0)
        ts(h("VC", 17, 144, 18), h("yi", 0, 8), col(QC), A.add, -float(VB), A.add)
        fill(h("V", ZV, ZV + 8), MARK)
        iota(h("X", ZC, ZC + 16), [[0, 16]], 0, 0)
        iota(h("RSN"), [[0, 32], [-256, 16]], 255, 0)

    def constants2():
        for n in range(VB, VB + 2048, UP):
            ts(h("V", n + 2048, n + 2048 + UP), h("V", n, n + UP), 12, A.logical_shift_right)
        act(h("WY"), WY)
        act(h("IDh"), h("ID"), scale=-1.0)
        act(h("ID2"), h("ID"), scale=2.0)
        act(h("IDn"), h("ID"), scale=-1.0)
        act(h("blh"), h("blk"), scale=0.5)
        tt(h("blx"), h("blh"), h("IDb"), A.subtract)
        ts(col(WC), h("wb"), 2.0, A.mult)
        ts(col(WN), h("wb"), -1.0, A.mult)
        act(h("WB2"), h("blk"), scale=col(WC))
        act(h("WBn"), h("blk"), scale=col(WN))
        act(h("WBh"), h("blk"), scale=col(WN))
        act(h("MQ20"), h("MQ", 0, 64), scale=2.0 ** 20)
        act(h("MQ22"), h("MQ", 0, 64), bias=1280.0 * 4096, scale=2.0 ** 20)
        act(h("IDu"), h("ID"), scale=-4096.0)
        act(h("RSU"), h("NQ", 0, 64), scale=1.0e7)
        act(col(K37), col(QC), bias=15.5, scale=37.0)
        act(col(AK0), col(QC), scale=37.0)
        act(col(C64), col(QC), scale=64.0)
        act(h("RH", 0, 4), h("BK4"), scale=-TR / 16.0)
        act(h("RH", 4, 8), h("BK4"), scale=8.0)
        act(h("RH", 8, 12), h("BK4"), scale=-TR / 16.0)
        iota(h("fi", 0, 4), [[1024, 4]], TR, 0)
        iota(h("fi", 8, 16), [[16, 8]], 0, 0)
        ts(h("CB", 0, 4), h("fi", 0, 4), col(C64), A.add, 32.0, A.add)
        ts(h("CB", 12, 16), h("fi", 0, 4), col(C64), A.add)
        ts(h("CB", 4, 12), h("fi", 8, 16), col(QC), A.add)
        iota(h("sj", 0, 10), [[64, 5], [64, 2]], VB + 128, 0)
        iota(h("si", 0, 10), [[1, 5], [0, 2]], 1, 0)
        ts(h("QB", 0, 10), h("sj", 0, 10), col(M3), A.mult)
        ts(h("so", 0, 10), h("si", 0, 10), col(M2), A.mult)
        tt(h("QB", 0, 10), h("QB", 0, 10), h("so", 0, 10), A.add)
        for n in range(8):
            iota(h("X", TR + 514 * n, TR + 514 * n + 514), [[0, 514]], 0, 0)

    bank = lambda hh: "Ro" if hh else "Re"
    seg = lambda hh: (0, 72) if hh else (72, 144)

    def start_sums(t, hh):
        mms([(h(bank(hh), 0, 192), h("MQh"), h("THr"))] + [(h(bank(hh), 128, 192), h("IDm"), state(N0 + t % 2, hh, b)) for b in (0, 1)], True, False)

    def start_keys(t, hh):
        mm(h("KB", 0, 72), [(h("IDb"), h("KC")), (state(P0 + t % 2, hh), h("RB1")), (state(N0 + t % 2, hh), h("RC1"))], True, False)
        mm(h("PT", 0, 72), [(h("ID"), h("VC", *seg(hh)))], True, False)

    def first(t, hh):
        lst, zx = "S%d" % (max(t - 1, 0) % 2), "zx%d" % (max(t - 1, 0) % 2)
        o = half(hh)[0]
        rank_as(t, "C%d" % hh)
        from_q = lambda a, b: (h("C", 16 * o + 128 * a, 16 * o + 128 * b), ind(h("Q", 0, 4096), h(lst, o + 8 * a, o + 8 * b)))
        for a, b in zip(PC[hh], PC[hh][1:]):
            if t == 0:
                act(from_q(a, b)[0], ind(h("X", 0, 4096), h(lst, o + 8 * a, o + 8 * b)))
            elif b <= 8 - CV[hh]:
                act(*from_q(a, b), bias=col(QBIAS))
        rank_as(t, "T%d" % hh if t or hh else T00)
        cuts = PT[hh] if t or hh else PT0
        for a, b in zip(cuts, cuts[1:]):
            lo, hi = 16 * o + 128 * a, 16 * o + 128 * b
            tt(h("T", lo, hi), ind(h("X", 0, 4096), h(lst, o + 8 * a, o + 8 * b)), h(zx, lo, hi), A.max)
            if t == 0:
                chain("@0", 1)
        if CV[hh] and t:
            ts(*from_q(8 - CV[hh], 8), col(QBIAS), A.add)
            if t and FIX:
                chain("@v%d" % t, 3)
        rank_as(t, "R%d" % hh)
        ra = [flag("@r%d" % hh)]
        part = lambda nm, q: h(nm, 16 * o + 128 * q, 16 * o + 128 * q + 128)
        for a, b in zip(cuts, cuts[1:]):
            mms([(h(bank(hh), q, 64, 8), part("T", q), h("W2")) for q in range(a, b)], False, False, (), ra)
        if t == 0:
            mms([(h(bank(hh), 64 + q, 128, 8), part("D", q), h("W0", 16, 24)) for q in range(8)], False, False, (), ra)
        for a, b in zip(PC[hh], PC[hh][1:]):
            end = b == 8
            mms([(h(bank(hh), q, 192, 8), part("C", q), h("WQ" if t else "W0")) for q in range(a, b)], False, end, ra if end else (), () if end else ra)

    def keys(t, hh):
        (a, b), c, ro = seg(hh), half(hh), 0 if hh else 256
        rank_as(t, "R%d" % hh)
        unfold("RO", ro, h(bank(hh), 0, 64), bias=2048.0)
        unfold("ST", state(MV, hh)[1], h(bank(hh), 128, 192), AF.Sign, col(AT0 + t % 2))
        unfold("RO", ro + 128, h(bank(hh), 64, 128))
        k, p = h("KB", 0, 72), h("PT", 0, 72)
        mm(k, [(h("RO", ro, ro + 128), h("SPs"))], False, False)
        mm(k, [(state(MV, hh), h("RA1"))], False, True)
        mm(p, [(h("RO", ro + 128, ro + 256), h("SP"))], False, True)
        rank_as(t, "K%d" % hh)
        scan(h("dd", a, b), k, h("RSK"), 0.0, A.add, A.max)
        if t and hh and FIX:
            chain("@v%d" % t, 5)
        tt(h("GG", a, b), p, h("dd", a, b), A.subtract)
        if t and hh and FIX:
            chain("@v%d" % t, 7)
        for n in range(4):
            scan(h("DR", a + n, b, 4), h("dd", a + 18 * n, a + 18 * n + 18), h("GG", a + 18 * n, a + 18 * n + 18), 0.0, A.min, A.max)
        lo = kept(t - 1)
        f = h("V", kept(t) + c[0], kept(t) + c[1])
        view = ind(h("V", lo, merged(max(t - 2, -1)) + 128), h("DR", b - 4, b))
        if t < CLEAN:
            ts(h("si", *c), view, MARK + 4095, A.bitwise_and)
            ts(h("F16", *c), h("si", *c), float(ZC), A.min)
        else:
            cp(h("F16", *c), view)
        rank_as(t, "fill")
        cp(f, h("F16", *c))

    both = lambda w, n, hh: [(h(w), state(n, hh, b)) for b in (0, 1)]

    def books(t, hh):
        p, n, p2, n2 = P0 + t % 2, N0 + t % 2, P0 + (t + 1) % 2, N0 + (t + 1) % 2
        o, lo = half(hh)[0], four(hh)[0]
        mm(h("M2", 128 + o, 192 + o), both("blx", MV, hh) + both("blb", p, hh))
        unfold("ST", state(p2, hh)[1], h("M2", 128 + o, 192 + o), AF.Relu, -7.0, -1.0)
        mm(h("M2", o, o + 64), both("IDb", n, hh) + both("blb", p2, hh))
        unfold("ST", state(n2, hh)[1], h("M2", o, o + 64), bias=1.0, scale=-1.0)
        mm(h("M1", 128 + 2 * lo, 136 + 2 * lo), [(h("ID"), h("CB", 2 * lo, 2 * lo + 8)), (state(n2, hh), h("RH", lo, lo + 8))])
        if not hh:
            ts(h("og"), h("M1", 132, 140), 1.0, A.mult)

    def borrowers(t):
        for hh in (1, 0):
            o = half(hh)[0]
            mm(h("M2", 128 + o, 192 + o), both("blh", MV, hh) + both("blb", P0 + t % 2, hh))
        act(h("sg"), h("M2", 128, 256), AF.Sign, bias=6.5, accum=col(ACC))
        mm(h("M2", 256, 257), [(h("OF"), col(ACC))])
        act(col(AP), h("M2", 256, 257), bias=512.0 - 15.5, scale=1.0 / 32)
        act(col(AN), h("M2", 256, 257), bias=-512.0 - 0.5, scale=-1.0 / 32)
        act(col(T1), col(AP), bias=RND)
        act(col(T2), col(T1), bias=-RND - 8192.0 * (t + 1))
        act(col(AT0 + (t + 1) % 2), col(AN), bias=col(T2))
        act(col(AK0 + (t + 1) % 2), col(AP), bias=col(K37))
        act(h("VC"), h("VC"), bias=float(HW))
        if t >= 1:
            act(h("VC", 17, 144, 18), h("VC", 17, 144, 18), bias=256.0)

    def dgather(q, a, b):
        o, x = h("D", 16 * a, 16 * b), ind(h("X", 0, 4112), h("F16", a, b))
        if q == "s":
            act(o, x, bias=-0.125, scale=0.5)
        else:
            ts(o, x, 0.5, A.mult, -0.125, A.add)

    def extremes(a, b):
        n, lo = 16 * (b - a), 16 * a
        scan(h("mx", lo, lo + n), h("RSM", 0, n), h("D", 16 * a, 16 * b), 0.0, A.min, A.max)
        scan(h("mn", lo, lo + n), h("RSN", 0, n), h("D", 16 * a, 16 * b), 0.0, A.max, A.min)

    def u_start(t, hh):
        mm(h("Uo" if hh else "Ue", 0, 64), [(h("IDb"), h("MQ20")), (h("WBn"), h("Z%d" % (t % 2), *half(hh)))], True, False)

    def y_of(t, hh):
        c, f = half(hh), four(hh)
        z, u = h("Z%d" % (t % 2), *c), h("Uo" if hh else "Ue", 0, 64)
        y = h("msg", 72 * t, 72 * t + 64) if hh else h("yE%d" % (t % 2))
        tt(h("yi", *c), h("mx", 16 * c[0] + 15, 16 * c[1], 16), h("mn", 16 * c[0] + 15, 16 * c[1], 16), A.add)
        cp(y, h("yi", *c))
        tt(h("ymx", *c), h("yi", *c), z, A.max)
        mm(u, [(h("WBh"), y)], False, False)
        mm(u, [(h("WB2"), h("ymx", *c))], False, True)
        scan(h("us", *c), h("RSU"), u, 0.0, A.min, A.max)
        ts(h("fi", f[0] + 8, f[1] + 8), h("us", c[0] + 15, c[1], 16), 31, A.bitwise_and)
        if hh:
            scan(h("Ls", 8 * t, 8 * t + 4), h("fi", 8, 12), h("M1", 128, 132), 32.0, A.min, A.add)
        else:
            for a, b in ((0, 1), (1, 4)):
                scan(h("L%d" % (t % 2), 4 + a, 4 + b), h("fi", 12 + a, 12 + b), h("M1", 140 + a, 140 + b), 32.0, A.min, A.add)
        rank_as(t, "fill" if t < NSTEP - 1 else "Y0")
        act(h("uh", *c), u, bias=1280.0 - 2047.5 / 4096, scale=1.0 / 4096)
        mm(h("M1", 256 + c[0], 256 + c[1]), [(h("IDb"), h("MQ22")), (h("WBn"), z), (h("WBh"), y), (h("WB2"), h("ymx", *c)), (h("IDu"), h("uh", *c))])
        zp = h("M2", 320 + c[0], 320 + c[1])
        mm(zp, [(h("ID2"), h("ymx", *c)), (h("IDh"), y), (h("IDn"), z)])
        act(h("Z%d" % ((t + 1) % 2), *c), zp)

    def write_half(t, hh, y):
        c = half(hh)
        lst = h("Lr", 8 * t, 8 * t + 4) if hh else h("L%d" % (t % 2), 4, 8)
        win = h("X", 0, WIN)
        if t == NSTEP - 1:
            cp(ind(win, lst), y)
            return
        act(h("qx", *c), ind(win, lst))
        tt(h("qm", *c), ind(win, lst), y, A.max)
        pq = h("Uo" if hh else "Ue", 0, 64)
        mm(pq, [(h("L3", 0, 128, 1, 1), h("JR", 0, 64, 1, 1))], True, False)
        mm(pq, [(h("WY"), y)], False, False)
        mm(pq, [(WM, h("qm", *c))], False, False)
        mm(pq, [(WX, h("qx", *c))], False, True)
        cp(ind(win, lst), y)
        act(h("Qn", *c), pq, bias=h("QB", 2 * t + hh, 2 * t + hh + 1))
        cp(ind(h("Q", 0, WIN), lst), h("Qn", *c))
        if hh and FIX:
            chain("@v%d" % (t + 1), 1)

    def new_lists(t):
        f, fp, fa = h("V", kept(t), kept(t) + 128), h("M1", 256, 384), h("M1", 384, 512)
        m = merged(t)
        ts(fa, f, col(AK0 + t % 2), A.add)
        tt(h("sj"), f, fp, A.mult)
        ts(h("sj"), h("sj"), 5, A.logical_shift_right)
        tt(h("V", m - 128, m), h("sj"), fa, A.add)
        ts(h("V", m, m + 128), ind(h("V", m - 256, m), h("og")), 4095, A.bitwise_and)
        if t < NSTEP - 2:
            cp(h("S%d" % ((t + 1) % 2)), ind(h("V", m, m + 128), h("PL")))

    cores = T.cores
    constants()
    start_sums(0, 1)
    start_sums(0, 0)
    start_keys(0, 1)
    for t in range(NSTEP):
        last = t == NSTEP - 1
        first(t, 1)
        if t == 0:
            rank_as(-1, "fill")
            constants2()
        first(t, 0)
        keys(t, 1)
        rank_as(t, "fill")
        if 1 <= t < NSTEP - 1:
            spread("Z%d" % (t % 2), "zx%d" % (t % 2), ZG)
        u_start(t, 1)
        u_start(t, 0)
        start_keys(t, 0)
        keys(t, 0)
        rank_as(t, "fill")
        if t == CLEAN - 1:
            rank_as(-1, "fill")
            for n in range(VB, VB + 2048, 128):
                ts(h("V", n, n + 128), h("V", n, n + 128), 4095, A.bitwise_and)
            fill(h("V", ZV, ZV + 8), ZC)
            rank_as(t, "fill")
        books(t, 1)
        rank_as(t, "D1")
        for q, a, b in DG[1]:
            dgather(q, a, b)
        for q, a, b in sorted(DG[1], key=lambda d: d[1]):
            extremes(a, b)
        rank_as(t, "Y1")
        y_of(t, 1)
        rank_as(t, "Y1")
        dst = cores[(rank + 1 + t % 3) % len(cores)]
        if t == 0:
            send(h("V", kept(t) + 128, kept(t) + 192), h("V", kept(t), kept(t) + 64), "rf%d" % t, dst)
        send(h("rxy", 72 * t, 72 * t + 64), h("msg", 72 * t, 72 * t + 64), "ry%d" % t, dst, None if t else "rf0")
        send(h("Lr", 8 * t, 8 * t + 4), h("Ls", 8 * t, 8 * t + 4), "rl%d" % t, dst, "ry%d" % t)
        rank_as(t, "fill")
        books(t, 0)
        if not last:
            if t:
                send(h("V", kept(t) + 128, kept(t) + 192), h("V", kept(t), kept(t) + 64), "rf%d" % t, dst, "rl%d" % t)
            borrowers(t)
            start_sums(t + 1, 1)
            start_sums(t + 1, 0)
            start_keys(t + 1, 1)
        rank_as(t, "D0")
        for q, a, b in DG[0]:
            dgather(q, a, b)
        for q, a, b in sorted(DG[0], key=lambda d: d[1]):
            extremes(a, b)
        rank_as(t, "Y0")
        y_of(t, 0)
        rank_as(t, "Y0")
        write_half(t, 0, h("yE%d" % (t % 2)))
        rank_as(t, "fill")
        new_lists(t)
        if last:
            m = merged(t)
            cp(h("so", 1, 128, 2), h("V", m, m + 64))
            cp(h("so", 0, 128, 2), h("V", m + 64, m + 128))
            dma("s", "dys", T.ys[:, :], ap(h("so")), None, h("so"), 4.5)
            zf = "Z%d" % (NSTEP % 2)
            act(h("zo", 1, 128, 2), h(zf, 0, 64))
            act(h("zo", 0, 128, 2), h(zf, 64, 128))
            dma("y", "dyz", T.yz[:, :], ap(h("zo")), None, h("zo"))
        rank_as(t, "Y0")
        src = cores[(rank - 1 - t % 3) % len(cores)]
        landed = len(topo.engines(src, core)[:ENG])
        recv(h("rxy", 72 * t, 72 * t + 64), "ry%d" % t, landed)
        recv(h("Lr", 8 * t, 8 * t + 4), "rl%d" % t, landed)
        if not last:
            recv(h("V", kept(t) + 128, kept(t) + 192), "rf%d" % t, landed)
        write_half(t, 1, h("rxy", 72 * t, 72 * t + 64))
    dma("y", "dyx", T.yx[:, :], ap(h("X", 0, 4096)), None, h("X", 0, 4096), 5.0)
    if not ORDER:
        schedule()
    for i in ORDER:
        ops[i][1]()
    for s in sorted(total):
        wait("g", (s, total[s]), {s: total[s]})
